import numpy as np
import ml_dtypes


def mxq(x, axis, fmt="e4m3"):
    dtype, down = {"e4m3": (ml_dtypes.float8_e4m3fn, 7), "e5m2": (ml_dtypes.float8_e5m2, 14)}[fmt]
    v = np.moveaxis(np.asarray(x, np.float32).astype(ml_dtypes.bfloat16).astype(np.float64), axis, -1)
    blocks = v.reshape(v.shape[:-1] + (-1, 32))
    amax = np.abs(blocks).max(-1, keepdims=True)
    byte = np.maximum(np.where(amax > 0, np.frexp(amax)[1] - 1 + 127, 0) - down, 1)
    scale = np.exp2(byte - 127.0)
    codes = (blocks / scale).astype(np.float32).astype(dtype).astype(np.float64)
    return np.moveaxis((codes * scale).reshape(v.shape), -1, axis)


WIDE = False


def mx_kscale(k):
    if not WIDE:
        return np.ones(k)
    levels = np.array([10, -10, 5, -5, 0])
    if k % 512:
        return np.exp2(np.random.permutation(np.resize(levels, k // 32))).repeat(32)
    a = np.empty((k // 512, 16))
    for p in range(k // 512):
        a[p, :8] = np.random.permutation(np.resize(levels, 8))
        for g in range(8):
            far = levels[np.abs(levels - a[p, g]) >= 10]
            a[p, g + 8] = far[np.random.randint(len(far))]
    return np.exp2(a.ravel()).repeat(32)


def f64(x):
    return np.asarray(x).astype(np.float64)


def striped(idx):
    return np.tile(np.asarray(idx).reshape(-1, 16).T, (8, 1)).astype(np.uint16)


def unstriped(offs):
    return offs[:16].T.reshape(-1).astype(np.int64)


def striped8(idx):
    return np.asarray(idx).reshape(8, -1, 16).transpose(0, 2, 1).reshape(128, -1).astype(np.uint16)


def unstriped8(offs):
    return offs.reshape(8, 16, -1).transpose(0, 2, 1).reshape(8, -1).astype(np.int64)


def pick8(x, idx, run):
    r = np.arange(len(x))
    return x[r[:, None], idx[r % (8 * run) // run]]


E2M1 = np.array([0.0, 0.5, 1.0, 1.5, 2.0, 3.0, 4.0, 6.0, -0.0, -0.5, -1.0, -1.5, -2.0, -3.0, -4.0, -6.0])


def pack_weight(w, fmt):
    k, n = w.shape
    w = f64(np.asarray(w, np.float32).astype(ml_dtypes.bfloat16)).reshape(k // 32, 32, n)
    amax = np.abs(w).max(1)
    if fmt == "e4m3":
        byte = np.frexp(amax)[1] - 1 + 127 - 7
    else:
        mant, ex = np.frexp(amax / 6.0)
        byte = np.where(mant > 0.5, ex, ex - 1) + 127
    byte = np.clip(np.where(amax > 0, byte, 1), 1, 254)
    scaled = (w * np.exp2(127.0 - byte)[:, None, :]).reshape(k, n).astype(np.float32)
    by_word = np.ascontiguousarray(scaled.reshape(k // 512, 128, 4, n).transpose(0, 1, 3, 2))
    if fmt == "e4m3":
        words = by_word.astype(ml_dtypes.float8_e4m3fn).view(np.uint8)
    else:
        c = by_word.astype(ml_dtypes.float4_e2m1fn).view(np.uint8) & 0xF
        words = (c[..., 0::2] | (c[..., 1::2] << 4)).reshape(k // 512, 128, 2 * n)
    return np.ascontiguousarray(words), np.ascontiguousarray(byte.astype(np.uint8).reshape(k // 512, 16, n))


def unpack_weight(words, scales, fmt):
    g, _, n = scales.shape
    words = np.ascontiguousarray(words).reshape(g, 128, n, -1)
    if fmt == "e4m3":
        vals = words.view(ml_dtypes.float8_e4m3fn).astype(np.float64)
    else:
        nib = np.empty((g, 128, n, 4), np.uint8)
        nib[..., 0::2] = words & 0xF
        nib[..., 1::2] = words >> 4
        vals = E2M1[nib]
    vals = vals * np.repeat(np.exp2(scales.astype(np.float64) - 127.0), 8, axis=1)[..., None]
    return vals.transpose(0, 1, 3, 2).reshape(g * 512, n)


def bf(x):
    return np.asarray(x, np.float32).astype(ml_dtypes.bfloat16)


def planes(Y):
    r, m = Y.shape
    b = f64(bf(Y)).reshape(r // 32, 32, m)
    amax = np.abs(b).max(1)
    byte = np.clip(np.where(amax > 0, np.frexp(amax)[1] - 1 + 127 - 7, 1), 1, 254)
    codes = (b * np.exp2(127.0 - byte)[:, None, :]).reshape(r, m).astype(np.float32).astype(ml_dtypes.float8_e4m3fn).view(np.uint8)
    words = codes.reshape(r // 512, 128, 4, m).transpose(0, 1, 3, 2)
    return np.ascontiguousarray(words), np.ascontiguousarray(byte.astype(np.uint8).reshape(r // 512, 16, m))


D, C, T, I, Q, E = 512, 1024, 2048, 512, 256, 512


def setup_inputs():
    n = np.random.standard_normal
    idx = np.stack([np.random.randint(0, C, I) for _ in range(8)])
    idx2 = np.random.permutation(T)[:I]
    fd = mx_kscale(D)
    fi = mx_kscale(I)
    bookp = pack_weight(n((D, C)) / fd[:, None], "e4m3")
    finep = pack_weight(n((D, T)) * 0.5 / fd[:, None], "e2m1")
    return {
        "query": (n((D, Q)) * 0.25 / np.sqrt(D) * fd[:, None]).astype(np.float32),
        "book_words": bookp[0],
        "book_scales": bookp[1],
        "fine_words": finep[0],
        "fine_scales": finep[1],
        "size": (np.random.uniform(0.5, 2.0, (1, I)) * fi).astype(np.float32),
        "vals": (n((I, E)) / fi[:, None]).astype(np.float32),
        "offs": striped8(idx),
        "offs2": striped(idx2),
    }


def reference(query, book_words, book_scales, fine_words, fine_scales, size, vals, offs, offs2):
    idx = unstriped8(offs)
    idx2 = unstriped(offs2)
    booku = unpack_weight(book_words, book_scales, "e4m3")
    fineu = unpack_weight(fine_words, fine_scales, "e2m1")
    queryq = mxq(f64(query), 0, "e4m3")
    bookidxg = pick8(booku, idx, 64)
    fineidx2g = fineu[:, idx2]
    a = queryq.T @ bookidxg + queryq.T @ fineidx2g
    p = np.exp(a - np.max(a, axis=1, keepdims=True))
    w = p * f64(size) / np.sum(p, axis=1, keepdims=True)
    wt = w.T
    valsq = mxq(f64(vals), 0, "e4m3")
    wtq = mxq(wt, 0, "e4m3")
    o = valsq.T @ wtq
    words, scales = planes(o)
    return o, words, scales

@@ -1,0 +1,206 @@
+from contextlib import ExitStack
+
+import concourse.mybir as mybir
+from concourse.masks import make_identity
+
+D, C, T, SLOTS, Q, E = 512, 1024, 2048, 512, 256, 512
+FLOPS = 2 * D * Q * SLOTS * 2 + 2 * SLOTS * E * Q
+
+F32 = mybir.dt.float32
+BF16 = mybir.dt.bfloat16
+I32 = mybir.dt.int32
+U32 = mybir.dt.uint32
+U16 = mybir.dt.uint16
+U8 = mybir.dt.uint8
+FP8X4 = mybir.dt.float8_e4m3fn_x4
+FP4X4 = mybir.dt.float4_e2m1fn_x4
+ACT = mybir.ActivationFunctionType
+ALU = mybir.AluOpType
+
+P = 128
+PACK = 4
+QB = 128
+BLOCKS = Q // QB
+
+
+def interleave(copy, grouped, planes):
+    copy(
+        out=grouped.rearrange("p (c i) t -> p c t i", i=4),
+        in_=planes.rearrange("p t (c i) -> p c t i", i=4),
+    )
+
+
+def tile_attend_pqresid_pl_kernel(
+    tc, query, book_words, book_scales, fine_words, fine_scales, size, vals, offs, offs2, out_0, out_1, out_2
+):
+    nc = tc.nc
+    with ExitStack() as ctx:
+        sb = ctx.enter_context(tc.tile_pool(name="sb", bufs=1))
+        ps = ctx.enter_context(tc.psum_pool(name="ps", bufs=1))
+
+        book_list = sb.tile([P, SLOTS // 16], U16, name="book_list")
+        nc.sync.dma_start(book_list[:], offs)
+        book_sc = sb.tile([P, C], U8, name="book_sc")
+        nc.sync.dma_start(
+            out=book_sc[:].bitcast(I32),
+            in_=book_scales[0].bitcast(I32).unsqueeze(1).to_broadcast([16, 8, C // 4]),
+        )
+        fine_sc = sb.tile([P, T], U8, name="fine_sc")
+        for x in range(4):
+            nc.sync.dma_start(
+                out=fine_sc[32 * x : 32 * x + 32, :].bitcast(I32),
+                in_=fine_scales[0, 4 * x : 4 * x + 4, :].bitcast(I32).unsqueeze(0).to_broadcast([8, 4, T // 4]),
+            )
+        fine_list = sb.tile([P, SLOTS // 16], U16, name="fine_list")
+        nc.sync.dma_start(fine_list[:], offs2)
+        book_w = sb.tile([P, C], I32, name="book_w")
+        nc.sync.dma_start(out=book_w[:], in_=book_words[0].rearrange("p n t -> p (n t)").bitcast(I32))
+        q_raw = sb.tile([P, PACK, Q], F32, name="q_raw")
+        nc.sync.dma_start(out=q_raw[:], in_=query.rearrange("(p j) q -> p j q", j=PACK))
+        fine_w = sb.tile([P, T], U16, name="fine_w")
+        nc.sync.dma_start(out=fine_w[:].bitcast(I32), in_=fine_words[0].bitcast(I32))
+        vals_rows = vals.rearrange("(p j) e -> p j e", j=PACK)
+        v_raw = []
+        for h in range(2):
+            half = sb.tile([P, PACK, E // 2], F32, name=f"v_raw{h}")
+            nc.sync.dma_start(out=half[:], in_=vals_rows[:, :, h * (E // 2) : (h + 1) * (E // 2)])
+            v_raw.append(half)
+        size_col = sb.tile([P, PACK], F32, name="size_col")
+        nc.gpsimd.dma_start(out=size_col[:], in_=size.rearrange("o (p t) -> p (o t)", t=PACK))
+
+        ident = sb.tile([P, P], F32, name="ident")
+        make_identity(nc, ident[:])
+
+        book_plane = sb.tile([P, SLOTS], U8, name="book_plane", align_bytes=64)
+        nc.vector.memset(book_plane[:].bitcast(I32), 0)
+        warm = sb.tile([P, 2], F32, name="warm")
+        nc.vector.memset(warm[:, 0:1], 0.0)
+        nc.scalar.activation(out=warm[:, 1:2], in_=warm[:, 0:1], func=ACT.Exp)
+
+        book_sc_g = sb.tile([P, SLOTS], U8, name="book_sc_g", align_bytes=64)
+        nc.vector.tensor_copy(book_sc_g[:], book_sc[:].indirect(book_list[:]))
+        for x in range(4):
+            nc.scalar.dma_start(
+                out=book_plane[32 * x : 32 * x + 4, :].bitcast(I32),
+                in_=book_sc_g[32 * x : 32 * x + 32 : 8, :].bitcast(I32),
+            )
+        book_keys = sb.tile([P, SLOTS], U32, name="book_keys", align_bytes=64)
+        nc.vector.tensor_copy(book_keys[:], book_w[:].bitcast(U32).indirect(book_list[:]))
+        fine_plane = sb.tile([P, SLOTS], U8, name="fine_plane", align_bytes=64)
+        nc.vector.tensor_copy(fine_plane[:], fine_sc[:].indirect(fine_list[:]))
+
+        q_codes, q_plane = [], []
+        for b in range(BLOCKS):
+            grouped = sb.tile([P, QB, PACK], BF16, name=f"q_grouped{b}", align_bytes=64)
+            interleave(nc.scalar.copy, grouped[:], q_raw[:, :, b * QB : (b + 1) * QB])
+            codes = sb.tile([P, QB], U32, name=f"q_codes{b}", align_bytes=64)
+            plane = sb.tile([P, QB], U8, name=f"q_plane{b}", align_bytes=64)
+            nc.vector.quantize_mx(
+                out=codes[:].bitcast(FP8X4), scales=plane[:], in_=grouped[:].rearrange("p c t -> p (c t)")
+            )
+            q_codes.append(codes)
+            q_plane.append(plane)
+
+        fine_keys = sb.tile([P, SLOTS], U16, name="fine_keys", align_bytes=64)
+        nc.vector.tensor_copy(fine_keys[:], fine_w[:].indirect(fine_list[:]))
+
+        size_ps = ps.tile([P, PACK, P], F32, name="size_ps")
+        for t in range(PACK):
+            nc.tensor.transpose(size_ps[:, t, :], size_col[:, t : t + 1].to_broadcast([P, P]), ident[:])
+
+        scores = [ps.tile([P, SLOTS], F32, name=f"scores{b}") for b in range(BLOCKS)]
+        for b in range(BLOCKS):
+            nc.tensor.matmul_mx(
+                out=scores[b][:], lhsT=q_codes[b][:].bitcast(FP8X4), lhsT_scale=q_plane[b][:],
+                rhs=book_keys[:].bitcast(FP8X4), rhs_scale=book_plane[:], start=True, stop=False,
+            )
+        for b in range(BLOCKS):
+            nc.tensor.matmul_mx(
+                out=scores[b][:], lhsT=q_codes[b][:].bitcast(FP8X4), lhsT_scale=q_plane[b][:],
+                rhs=fine_keys[:].bitcast(FP4X4), rhs_scale=fine_plane[:], start=False, stop=True,
+            )
+
+        v_grouped = sb.tile([P, PACK, P, PACK], BF16, name="v_grouped", align_bytes=64)
+        for h in range(2):
+            nc.scalar.copy(
+                out=v_grouped[:, :, 64 * h : 64 * h + 64, :].rearrange("p t m j -> p m j t"),
+                in_=v_raw[h][:].rearrange("p j (m t) -> p m j t", t=PACK),
+            )
+        v_codes = sb.tile([P, E], U32, name="v_codes", align_bytes=64)
+        v_plane = sb.tile([P, E], U8, name="v_plane", align_bytes=64)
+        for g in range(2):
+            nc.vector.quantize_mx(
+                out=v_codes[:, 256 * g : 256 * g + 256].bitcast(FP8X4),
+                scales=v_plane[:, 256 * g : 256 * g + 256],
+                in_=v_grouped[:, 2 * g : 2 * g + 2, :, :].rearrange("p t m j -> p (t m j)"),
+            )
+
+        neg_max, probs, row_sum = [], [], []
+        for b in range(BLOCKS):
+            nm = sb.tile([P, 1], F32, name=f"neg_max{b}")
+            nc.vector.tensor_reduce(out=nm[:], in_=scores[b][:], axis=mybir.AxisListType.X, op=ALU.max, negate=True)
+            neg_max.append(nm)
+        for b in range(BLOCKS):
+            pr = sb.tile([P, 2, P, 2], F32, name=f"probs{b}")
+            rs = sb.tile([P, 1], F32, name=f"row_sum{b}")
+            nc.scalar.activation(
+                out=pr[:], in_=scores[b][:].rearrange("q (p u e) -> q u p e", u=2, e=2),
+                func=ACT.Exp, bias=neg_max[b][:], scale=1.0, accum_out=rs[:],
+            )
+            probs.append(pr)
+            row_sum.append(rs)
+
+        w_codes, w_plane = [], []
+        for b in range(BLOCKS):
+            inv = sb.tile([P, 1], F32, name=f"inv_sum{b}")
+            nc.vector.reciprocal(out=inv[:], in_=row_sum[b][:])
+            turned = ps.tile([P, 2, QB], F32, name=f"turned{b}")
+            for u in range(2):
+                w = sb.tile([P, P, 2], BF16, name=f"w{b}_{u}")
+                nc.vector.scalar_tensor_tensor(
+                    out=w[:], in0=probs[b][:, u, :, :], scalar=inv[:],
+                    in1=size_ps[:, 2 * u : 2 * u + 2, :].rearrange("q e p -> q p e"),
+                    op0=ALU.mult, op1=ALU.mult,
+                )
+                nc.tensor.transpose(turned[:, u, :], w[:].rearrange("q p e -> q (p e)").bitcast(F32), ident[:])
+            grouped = sb.tile([P, QB * PACK], BF16, name=f"w_grouped{b}", align_bytes=64)
+            nc.scalar.copy(
+                out=grouped[:].bitcast(F32).rearrange("p (q u) -> p q u", u=2),
+                in_=turned[:].rearrange("p u q -> p q u"),
+            )
+            codes = sb.tile([P, QB], U32, name=f"w_codes{b}", align_bytes=64)
+            plane = sb.tile([P, QB], U8, name=f"w_plane{b}", align_bytes=64)
+            nc.vector.quantize_mx(out=codes[:].bitcast(FP8X4), scales=plane[:], in_=grouped[:])
+            w_codes.append(codes)
+            w_plane.append(plane)
+
+        o_codes = sb.tile([P, Q], I32, name="o_codes", align_bytes=64)
+        o_plane = sb.tile([P, Q], U8, name="o_plane", align_bytes=64)
+        out_rows = out_0.rearrange("(m t) q -> m t q", t=PACK)
+        acc_tags = [["acc_a", "acc_b"], ["acc_c", "scores0"]]
+        for b in range(BLOCKS):
+            y = sb.tile([P, PACK, QB], F32, name=f"y{b}")
+            for g in range(2):
+                acc = ps.tile([P, 2, QB], F32, name=f"acc{b}_{g}", tag=acc_tags[b][g])
+                for s in range(2):
+                    t = 2 * g + s
+                    nc.tensor.matmul_mx(
+                        out=acc[:, s, :], lhsT=v_codes[:, P * t : P * (t + 1)].bitcast(FP8X4),
+                        lhsT_scale=v_plane[:, P * t : P * (t + 1)],
+                        rhs=w_codes[b][:].bitcast(FP8X4), rhs_scale=w_plane[b][:], start=True, stop=True,
+                    )
+                nc.scalar.copy(out=y[:, 2 * g : 2 * g + 2, :], in_=acc[:])
+            nc.sync.dma_start(out=out_rows[:, :, b * QB : (b + 1) * QB], in_=y[:])
+            grouped = sb.tile([P, QB, PACK], BF16, name=f"o_grouped{b}", align_bytes=64)
+            interleave(nc.vector.tensor_copy, grouped[:], y[:])
+            nc.vector.quantize_mx(
+                out=o_codes[:, b * QB : (b + 1) * QB].bitcast(FP8X4),
+                scales=o_plane[:, b * QB : (b + 1) * QB],
+                in_=grouped[:].rearrange("p c t -> p (c t)"),
+            )
+        nc.sync.dma_start(out=out_1[0].rearrange("p c t -> p (c t)").bitcast(I32), in_=o_codes[:])
+        for x in range(4):
+            queue = nc.scalar if x % 2 == 0 else nc.sync
+            queue.dma_start(
+                out=out_2[0, 4 * x : 4 * x + 4, :].bitcast(I32), in_=o_plane[32 * x : 32 * x + 4, :].bitcast(I32)
+            )

@@ -21,6 +21,7 @@ P = 128
 PACK = 4
 QB = 128
 BLOCKS = Q // QB
+V_CUTS = (0, 192, 384, 512)
 
 
 def interleave(copy, grouped, planes):
@@ -38,6 +39,9 @@ def tile_attend_pqresid_pl_kernel(
         sb = ctx.enter_context(tc.tile_pool(name="sb", bufs=1))
         ps = ctx.enter_context(tc.psum_pool(name="ps", bufs=1))
 
+        ident = sb.tile([P, P], F32, name="ident")
+        make_identity(nc, ident[:])
+
         book_list = sb.tile([P, SLOTS // 16], U16, name="book_list")
         nc.sync.dma_start(book_list[:], offs)
         book_sc = sb.tile([P, C], U8, name="book_sc")
@@ -45,53 +49,52 @@ def tile_attend_pqresid_pl_kernel(
             out=book_sc[:].bitcast(I32),
             in_=book_scales[0].bitcast(I32).unsqueeze(1).to_broadcast([16, 8, C // 4]),
         )
-        fine_sc = sb.tile([P, T], U8, name="fine_sc")
-        for x in range(4):
-            nc.sync.dma_start(
-                out=fine_sc[32 * x : 32 * x + 32, :].bitcast(I32),
-                in_=fine_scales[0, 4 * x : 4 * x + 4, :].bitcast(I32).unsqueeze(0).to_broadcast([8, 4, T // 4]),
-            )
+        fine_sc = sb.tile([P, T], U8, name="fine_sc", tag="late")
+        warm_in = sb.tile([P, 1], F32, name="warm_in")
+        warm_out = sb.tile([P, 1], F32, name="warm_out")
+        nc.vector.memset(warm_in[:], 0.0)
+        nc.scalar.activation(out=warm_out[:], in_=warm_in[:], func=ACT.Exp)
         fine_list = sb.tile([P, SLOTS // 16], U16, name="fine_list")
         nc.sync.dma_start(fine_list[:], offs2)
-        book_w = sb.tile([P, C], I32, name="book_w")
-        nc.sync.dma_start(out=book_w[:], in_=book_words[0].rearrange("p n t -> p (n t)").bitcast(I32))
+        nc.sync.dma_start(
+            out=fine_sc[:].bitcast(I32),
+            in_=fine_scales[0].bitcast(I32).unsqueeze(1).to_broadcast([16, 8, T // 4]),
+        )
+        size_col = sb.tile([P, PACK], F32, name="size_col")
+        nc.sync.dma_start(out=size_col[:], in_=size.rearrange("o (p t) -> p (o t)", t=PACK))
         q_raw = sb.tile([P, PACK, Q], F32, name="q_raw")
         nc.sync.dma_start(out=q_raw[:], in_=query.rearrange("(p j) q -> p j q", j=PACK))
+        book_w = sb.tile([P, C], I32, name="book_w")
+        nc.sync.dma_start(out=book_w[:], in_=book_words[0].rearrange("p n t -> p (n t)").bitcast(I32))
         fine_w = sb.tile([P, T], U16, name="fine_w")
         nc.sync.dma_start(out=fine_w[:].bitcast(I32), in_=fine_words[0].bitcast(I32))
         vals_rows = vals.rearrange("(p j) e -> p j e", j=PACK)
-        v_raw = []
-        for h in range(2):
-            half = sb.tile([P, PACK, E // 2], F32, name=f"v_raw{h}")
-            nc.sync.dma_start(out=half[:], in_=vals_rows[:, :, h * (E // 2) : (h + 1) * (E // 2)])
-            v_raw.append(half)
-        size_col = sb.tile([P, PACK], F32, name="size_col")
-        nc.gpsimd.dma_start(out=size_col[:], in_=size.rearrange("o (p t) -> p (o t)", t=PACK))
+        v_first = sb.tile([P, PACK, V_CUTS[1]], F32, name="v_first")
+        nc.sync.dma_start(out=v_first[:], in_=vals_rows[:, :, 0 : V_CUTS[1]])
 
-        ident = sb.tile([P, P], F32, name="ident")
-        make_identity(nc, ident[:])
+        key_planes = sb.tile([P, 2 * SLOTS], U8, name="key_planes", align_bytes=64)
+        nc.vector.memset(key_planes[:].bitcast(I32), 0)
+        book_plane = key_planes[:, 0:SLOTS]
+        fine_plane = key_planes[:, SLOTS : 2 * SLOTS]
 
-        book_plane = sb.tile([P, SLOTS], U8, name="book_plane", align_bytes=64)
-        nc.vector.memset(book_plane[:].bitcast(I32), 0)
-        warm = sb.tile([P, 2], F32, name="warm")
-        nc.vector.memset(warm[:, 0:1], 0.0)
-        nc.scalar.activation(out=warm[:, 1:2], in_=warm[:, 0:1], func=ACT.Exp)
-
-        book_sc_g = sb.tile([P, SLOTS], U8, name="book_sc_g", align_bytes=64)
-        nc.vector.tensor_copy(book_sc_g[:], book_sc[:].indirect(book_list[:]))
+        picked = sb.tile([P, 2 * SLOTS], U8, name="picked", align_bytes=64)
+        nc.vector.tensor_copy(picked[:, 0:SLOTS], book_sc[:].indirect(book_list[:]))
+        nc.vector.tensor_copy(picked[:, SLOTS : 2 * SLOTS], fine_sc[:].indirect(fine_list[:]))
         for x in range(4):
-            nc.scalar.dma_start(
-                out=book_plane[32 * x : 32 * x + 4, :].bitcast(I32),
-                in_=book_sc_g[32 * x : 32 * x + 32 : 8, :].bitcast(I32),
+            nc.sync.dma_start(
+                out=key_planes[32 * x : 32 * x + 4, :].bitcast(I32),
+                in_=picked[32 * x : 32 * x + 32 : 8, :].bitcast(I32),
             )
-        book_keys = sb.tile([P, SLOTS], U32, name="book_keys", align_bytes=64)
-        nc.vector.tensor_copy(book_keys[:], book_w[:].bitcast(U32).indirect(book_list[:]))
-        fine_plane = sb.tile([P, SLOTS], U8, name="fine_plane", align_bytes=64)
-        nc.vector.tensor_copy(fine_plane[:], fine_sc[:].indirect(fine_list[:]))
-
+        v_rest = sb.tile([P, PACK * (E - V_CUTS[1])], F32, name="v_rest", tag="late")
+        v_raw = [v_first[:]]
+        for lo, hi in zip(V_CUTS[1:-1], V_CUTS[2:]):
+            at = PACK * (lo - V_CUTS[1])
+            piece = v_rest[:, at : at + PACK * (hi - lo)].rearrange("p (j e) -> p j e", j=PACK)
+            nc.sync.dma_start(out=piece, in_=vals_rows[:, :, lo:hi])
+            v_raw.append(piece)
         q_codes, q_plane = [], []
         for b in range(BLOCKS):
-            grouped = sb.tile([P, QB, PACK], BF16, name=f"q_grouped{b}", align_bytes=64)
+            grouped = sb.tile([P, QB, PACK], BF16, name=f"q_grouped{b}", tag=f"keys{b}", align_bytes=64)
             interleave(nc.scalar.copy, grouped[:], q_raw[:, :, b * QB : (b + 1) * QB])
             codes = sb.tile([P, QB], U32, name=f"q_codes{b}", align_bytes=64)
             plane = sb.tile([P, QB], U8, name=f"q_plane{b}", align_bytes=64)
@@ -101,7 +104,10 @@ def tile_attend_pqresid_pl_kernel(
             q_codes.append(codes)
             q_plane.append(plane)
 
-        fine_keys = sb.tile([P, SLOTS], U16, name="fine_keys", align_bytes=64)
+        book_keys = sb.tile([P, SLOTS], U32, name="book_keys", tag="keys0", align_bytes=64)
+        nc.vector.tensor_copy(book_keys[:], book_w[:].bitcast(U32).indirect(book_list[:]))
+
+        fine_keys = sb.tile([P, SLOTS], U16, name="fine_keys", tag="keys1", align_bytes=64)
         nc.vector.tensor_copy(fine_keys[:], fine_w[:].indirect(fine_list[:]))
 
         size_ps = ps.tile([P, PACK, P], F32, name="size_ps")
@@ -112,19 +118,18 @@ def tile_attend_pqresid_pl_kernel(
         for b in range(BLOCKS):
             nc.tensor.matmul_mx(
                 out=scores[b][:], lhsT=q_codes[b][:].bitcast(FP8X4), lhsT_scale=q_plane[b][:],
-                rhs=book_keys[:].bitcast(FP8X4), rhs_scale=book_plane[:], start=True, stop=False,
+                rhs=book_keys[:].bitcast(FP8X4), rhs_scale=book_plane, start=True, stop=False,
             )
-        for b in range(BLOCKS):
             nc.tensor.matmul_mx(
                 out=scores[b][:], lhsT=q_codes[b][:].bitcast(FP8X4), lhsT_scale=q_plane[b][:],
-                rhs=fine_keys[:].bitcast(FP4X4), rhs_scale=fine_plane[:], start=False, stop=True,
+                rhs=fine_keys[:].bitcast(FP4X4), rhs_scale=fine_plane, start=False, stop=True,
             )
 
         v_grouped = sb.tile([P, PACK, P, PACK], BF16, name="v_grouped", align_bytes=64)
-        for h in range(2):
-            nc.scalar.copy(
-                out=v_grouped[:, :, 64 * h : 64 * h + 64, :].rearrange("p t m j -> p m j t"),
-                in_=v_raw[h][:].rearrange("p j (m t) -> p m j t", t=PACK),
+        for piece, lo, hi, copy in zip(v_raw, V_CUTS, V_CUTS[1:], [nc.vector.tensor_copy, nc.scalar.copy, nc.scalar.copy]):
+            copy(
+                out=v_grouped[:, :, lo // PACK : hi // PACK, :].rearrange("p t m j -> p m j t"),
+                in_=piece.rearrange("p j (m t) -> p m j t", t=PACK),
             )
         v_codes = sb.tile([P, E], U32, name="v_codes", align_bytes=64)
         v_plane = sb.tile([P, E], U8, name="v_plane", align_bytes=64)
@@ -163,7 +168,7 @@ def tile_attend_pqresid_pl_kernel(
                     op0=ALU.mult, op1=ALU.mult,
                 )
                 nc.tensor.transpose(turned[:, u, :], w[:].rearrange("q p e -> q (p e)").bitcast(F32), ident[:])
-            grouped = sb.tile([P, QB * PACK], BF16, name=f"w_grouped{b}", align_bytes=64)
+            grouped = sb.tile([P, QB * PACK], BF16, name=f"w_grouped{b}", tag=f"grouped{b}", align_bytes=64)
             nc.scalar.copy(
                 out=grouped[:].bitcast(F32).rearrange("p (q u) -> p q u", u=2),
                 in_=turned[:].rearrange("p u q -> p q u"),
@@ -178,6 +183,7 @@ def tile_attend_pqresid_pl_kernel(
         o_plane = sb.tile([P, Q], U8, name="o_plane", align_bytes=64)
         out_rows = out_0.rearrange("(m t) q -> m t q", t=PACK)
         acc_tags = [["acc_a", "acc_b"], ["acc_c", "scores0"]]
+        o_grouped = sb.tile([P, Q, PACK], BF16, name="o_grouped", tag=f"grouped{BLOCKS - 1}", align_bytes=64)
         for b in range(BLOCKS):
             y = sb.tile([P, PACK, QB], F32, name=f"y{b}")
             for g in range(2):
@@ -189,15 +195,19 @@ def tile_attend_pqresid_pl_kernel(
                         lhsT_scale=v_plane[:, P * t : P * (t + 1)],
                         rhs=w_codes[b][:].bitcast(FP8X4), rhs_scale=w_plane[b][:], start=True, stop=True,
                     )
+                nc.vector.tensor_copy(
+                    out=o_grouped[:, b * QB : (b + 1) * QB, 2 * g : 2 * g + 2], in_=acc[:].rearrange("p s q -> p q s")
+                )
                 nc.scalar.copy(out=y[:, 2 * g : 2 * g + 2, :], in_=acc[:])
-            nc.sync.dma_start(out=out_rows[:, :, b * QB : (b + 1) * QB], in_=y[:])
-            grouped = sb.tile([P, QB, PACK], BF16, name=f"o_grouped{b}", align_bytes=64)
-            interleave(nc.vector.tensor_copy, grouped[:], y[:])
-            nc.vector.quantize_mx(
-                out=o_codes[:, b * QB : (b + 1) * QB].bitcast(FP8X4),
-                scales=o_plane[:, b * QB : (b + 1) * QB],
-                in_=grouped[:].rearrange("p c t -> p (c t)"),
-            )
+                if b == BLOCKS - 1:
+                    nc.sync.dma_start(
+                        out=out_rows[:, 2 * g : 2 * g + 2, b * QB : (b + 1) * QB], in_=y[:, 2 * g : 2 * g + 2, :]
+                    )
+            if b < BLOCKS - 1:
+                nc.sync.dma_start(out=out_rows[:, :, b * QB : (b + 1) * QB], in_=y[:])
+        nc.vector.quantize_mx(
+            out=o_codes[:].bitcast(FP8X4), scales=o_plane[:], in_=o_grouped[:].rearrange("p c t -> p (c t)")
+        )
         nc.sync.dma_start(out=out_1[0].rearrange("p c t -> p (c t)").bitcast(I32), in_=o_codes[:])
         for x in range(4):
             queue = nc.scalar if x % 2 == 0 else nc.sync

@@ -39,8 +39,15 @@ def tile_attend_pqresid_pl_kernel(
         sb = ctx.enter_context(tc.tile_pool(name="sb", bufs=1))
         ps = ctx.enter_context(tc.psum_pool(name="ps", bufs=1))
 
+        size_col = sb.tile([P, PACK], F32, name="size_col")
+        nc.gpsimd.dma_start(out=size_col[:], in_=size.rearrange("o (p t) -> p (o t)", t=PACK))
         ident = sb.tile([P, P], F32, name="ident")
         make_identity(nc, ident[:])
+
+        warm_in = sb.tile([P, 1], F32, name="warm_in")
+        nc.vector.memset(warm_in[:], 0.0)
+        warm_out = sb.tile([P, 1], F32, name="warm_out")
+        nc.scalar.activation(out=warm_out[:], in_=warm_in[:], func=ACT.Exp)
 
         book_list = sb.tile([P, SLOTS // 16], U16, name="book_list")
         nc.sync.dma_start(book_list[:], offs)
@@ -49,25 +56,21 @@ def tile_attend_pqresid_pl_kernel(
             out=book_sc[:].bitcast(I32),
             in_=book_scales[0].bitcast(I32).unsqueeze(1).to_broadcast([16, 8, C // 4]),
         )
-        fine_sc = sb.tile([P, T], U8, name="fine_sc", tag="late")
-        warm_in = sb.tile([P, 1], F32, name="warm_in")
-        warm_out = sb.tile([P, 1], F32, name="warm_out")
-        nc.vector.memset(warm_in[:], 0.0)
-        nc.scalar.activation(out=warm_out[:], in_=warm_in[:], func=ACT.Exp)
         fine_list = sb.tile([P, SLOTS // 16], U16, name="fine_list")
         nc.sync.dma_start(fine_list[:], offs2)
+        fine_sc = sb.tile([P, T], U8, name="fine_sc", tag="then_later_vals")
         nc.sync.dma_start(
             out=fine_sc[:].bitcast(I32),
             in_=fine_scales[0].bitcast(I32).unsqueeze(1).to_broadcast([16, 8, T // 4]),
         )
-        size_col = sb.tile([P, PACK], F32, name="size_col")
-        nc.sync.dma_start(out=size_col[:], in_=size.rearrange("o (p t) -> p (o t)", t=PACK))
-        q_raw = sb.tile([P, PACK, Q], F32, name="q_raw")
-        nc.sync.dma_start(out=q_raw[:], in_=query.rearrange("(p j) q -> p j q", j=PACK))
+        q_rows = query.rearrange("(p j) q -> p j q", j=PACK)
+        q_raw = [sb.tile([P, PACK, QB], F32, name=f"q_raw{b}") for b in range(BLOCKS)]
+        nc.sync.dma_start(out=q_raw[0][:], in_=q_rows[:, :, 0:QB])
         book_w = sb.tile([P, C], I32, name="book_w")
         nc.sync.dma_start(out=book_w[:], in_=book_words[0].rearrange("p n t -> p (n t)").bitcast(I32))
         fine_w = sb.tile([P, T], U16, name="fine_w")
         nc.sync.dma_start(out=fine_w[:].bitcast(I32), in_=fine_words[0].bitcast(I32))
+        nc.sync.dma_start(out=q_raw[1][:], in_=q_rows[:, :, QB:Q])
         vals_rows = vals.rearrange("(p j) e -> p j e", j=PACK)
         v_first = sb.tile([P, PACK, V_CUTS[1]], F32, name="v_first")
         nc.sync.dma_start(out=v_first[:], in_=vals_rows[:, :, 0 : V_CUTS[1]])
@@ -80,12 +83,9 @@ def tile_attend_pqresid_pl_kernel(
         picked = sb.tile([P, 2 * SLOTS], U8, name="picked", align_bytes=64)
         nc.vector.tensor_copy(picked[:, 0:SLOTS], book_sc[:].indirect(book_list[:]))
         nc.vector.tensor_copy(picked[:, SLOTS : 2 * SLOTS], fine_sc[:].indirect(fine_list[:]))
-        for x in range(4):
-            nc.sync.dma_start(
-                out=key_planes[32 * x : 32 * x + 4, :].bitcast(I32),
-                in_=picked[32 * x : 32 * x + 32 : 8, :].bitcast(I32),
-            )
-        v_rest = sb.tile([P, PACK * (E - V_CUTS[1])], F32, name="v_rest", tag="late")
+        for j in range(4):
+            nc.sync.dma_start(out=key_planes[j:P:32, :].bitcast(I32), in_=picked[8 * j : P : 32, :].bitcast(I32))
+        v_rest = sb.tile([P, PACK * (E - V_CUTS[1])], F32, name="v_rest", tag="then_later_vals")
         v_raw = [v_first[:]]
         for lo, hi in zip(V_CUTS[1:-1], V_CUTS[2:]):
             at = PACK * (lo - V_CUTS[1])
@@ -95,7 +95,7 @@ def tile_attend_pqresid_pl_kernel(
         q_codes, q_plane = [], []
         for b in range(BLOCKS):
             grouped = sb.tile([P, QB, PACK], BF16, name=f"q_grouped{b}", tag=f"keys{b}", align_bytes=64)
-            interleave(nc.scalar.copy, grouped[:], q_raw[:, :, b * QB : (b + 1) * QB])
+            interleave(nc.scalar.copy, grouped[:], q_raw[b][:])
             codes = sb.tile([P, QB], U32, name=f"q_codes{b}", align_bytes=64)
             plane = sb.tile([P, QB], U8, name=f"q_plane{b}", align_bytes=64)
             nc.vector.quantize_mx(
@@ -107,7 +107,7 @@ def tile_attend_pqresid_pl_kernel(
         book_keys = sb.tile([P, SLOTS], U32, name="book_keys", tag="keys0", align_bytes=64)
         nc.vector.tensor_copy(book_keys[:], book_w[:].bitcast(U32).indirect(book_list[:]))
 
-        fine_keys = sb.tile([P, SLOTS], U16, name="fine_keys", tag="keys1", align_bytes=64)
+        fine_keys = sb.tile([P, SLOTS], U16, name="fine_keys", align_bytes=64)
         nc.vector.tensor_copy(fine_keys[:], fine_w[:].indirect(fine_list[:]))
 
         size_ps = ps.tile([P, PACK, P], F32, name="size_ps")
@@ -126,19 +126,21 @@ def tile_attend_pqresid_pl_kernel(
             )
 
         v_grouped = sb.tile([P, PACK, P, PACK], BF16, name="v_grouped", align_bytes=64)
-        for piece, lo, hi, copy in zip(v_raw, V_CUTS, V_CUTS[1:], [nc.vector.tensor_copy, nc.scalar.copy, nc.scalar.copy]):
+
+        def deal_vals(copy, piece):
+            lo, hi = V_CUTS[piece], V_CUTS[piece + 1]
             copy(
                 out=v_grouped[:, :, lo // PACK : hi // PACK, :].rearrange("p t m j -> p m j t"),
-                in_=piece.rearrange("p j (m t) -> p m j t", t=PACK),
+                in_=v_raw[piece].rearrange("p j (m t) -> p m j t", t=PACK),
             )
-        v_codes = sb.tile([P, E], U32, name="v_codes", align_bytes=64)
-        v_plane = sb.tile([P, E], U8, name="v_plane", align_bytes=64)
-        for g in range(2):
-            nc.vector.quantize_mx(
-                out=v_codes[:, 256 * g : 256 * g + 256].bitcast(FP8X4),
-                scales=v_plane[:, 256 * g : 256 * g + 256],
-                in_=v_grouped[:, 2 * g : 2 * g + 2, :, :].rearrange("p t m j -> p (t m j)"),
-            )
+
+        deal_vals(nc.vector.tensor_copy, 0)
+        deal_vals(nc.scalar.copy, 1)
+        nc.gpsimd.tensor_scalar(
+            out=v_grouped[:, :, V_CUTS[2] // PACK :, :].rearrange("p t m j -> p m t j"),
+            in0=v_raw[2].rearrange("p j (m t) -> p m t j", t=PACK),
+            scalar1=1.0, scalar2=0.0, op0=ALU.mult, op1=ALU.add,
+        )
 
         neg_max, probs, row_sum = [], [], []
         for b in range(BLOCKS):
@@ -146,7 +148,7 @@ def tile_attend_pqresid_pl_kernel(
             nc.vector.tensor_reduce(out=nm[:], in_=scores[b][:], axis=mybir.AxisListType.X, op=ALU.max, negate=True)
             neg_max.append(nm)
         for b in range(BLOCKS):
-            pr = sb.tile([P, 2, P, 2], F32, name=f"probs{b}")
+            pr = sb.tile([P, 2, P, 2], F32, name=f"probs{b}", tag=f"probs{b}", align_bytes=64)
             rs = sb.tile([P, 1], F32, name=f"row_sum{b}")
             nc.scalar.activation(
                 out=pr[:], in_=scores[b][:].rearrange("q (p u e) -> q u p e", u=2, e=2),
@@ -155,7 +157,7 @@ def tile_attend_pqresid_pl_kernel(
             probs.append(pr)
             row_sum.append(rs)
 
-        w_codes, w_plane = [], []
+        w_grouped = []
         for b in range(BLOCKS):
             inv = sb.tile([P, 1], F32, name=f"inv_sum{b}")
             nc.vector.reciprocal(out=inv[:], in_=row_sum[b][:])
@@ -168,49 +170,59 @@ def tile_attend_pqresid_pl_kernel(
                     op0=ALU.mult, op1=ALU.mult,
                 )
                 nc.tensor.transpose(turned[:, u, :], w[:].rearrange("q p e -> q (p e)").bitcast(F32), ident[:])
-            grouped = sb.tile([P, QB * PACK], BF16, name=f"w_grouped{b}", tag=f"grouped{b}", align_bytes=64)
+            grouped = sb.tile([P, QB * PACK], BF16, name=f"w_grouped{b}", align_bytes=64)
             nc.scalar.copy(
                 out=grouped[:].bitcast(F32).rearrange("p (q u) -> p q u", u=2),
                 in_=turned[:].rearrange("p u q -> p q u"),
             )
-            codes = sb.tile([P, QB], U32, name=f"w_codes{b}", align_bytes=64)
-            plane = sb.tile([P, QB], U8, name=f"w_plane{b}", align_bytes=64)
-            nc.vector.quantize_mx(out=codes[:].bitcast(FP8X4), scales=plane[:], in_=grouped[:])
+            w_grouped.append(grouped)
+
+        v_codes = sb.tile([P, E], U32, name="v_codes", tag=f"probs{BLOCKS - 1}", align_bytes=64)
+        v_plane = sb.tile([P, E], U8, name="v_plane", align_bytes=64)
+        w_codes, w_plane = [], []
+        for g in range(2):
+            nc.vector.quantize_mx(
+                out=v_codes[:, 256 * g : 256 * g + 256].bitcast(FP8X4),
+                scales=v_plane[:, 256 * g : 256 * g + 256],
+                in_=v_grouped[:, 2 * g : 2 * g + 2, :, :].rearrange("p t m j -> p (t m j)"),
+            )
+            codes = sb.tile([P, QB], U32, name=f"w_codes{g}", align_bytes=64)
+            plane = sb.tile([P, QB], U8, name=f"w_plane{g}", align_bytes=64)
+            nc.vector.quantize_mx(out=codes[:].bitcast(FP8X4), scales=plane[:], in_=w_grouped[g][:])
             w_codes.append(codes)
             w_plane.append(plane)
 
         o_codes = sb.tile([P, Q], I32, name="o_codes", align_bytes=64)
         o_plane = sb.tile([P, Q], U8, name="o_plane", align_bytes=64)
+        o_grouped = sb.tile([P, Q, PACK], BF16, name="o_grouped", align_bytes=64)
         out_rows = out_0.rearrange("(m t) q -> m t q", t=PACK)
-        acc_tags = [["acc_a", "acc_b"], ["acc_c", "scores0"]]
-        o_grouped = sb.tile([P, Q, PACK], BF16, name="o_grouped", tag=f"grouped{BLOCKS - 1}", align_bytes=64)
-        for b in range(BLOCKS):
-            y = sb.tile([P, PACK, QB], F32, name=f"y{b}")
-            for g in range(2):
-                acc = ps.tile([P, 2, QB], F32, name=f"acc{b}_{g}", tag=acc_tags[b][g])
-                for s in range(2):
-                    t = 2 * g + s
-                    nc.tensor.matmul_mx(
-                        out=acc[:, s, :], lhsT=v_codes[:, P * t : P * (t + 1)].bitcast(FP8X4),
-                        lhsT_scale=v_plane[:, P * t : P * (t + 1)],
-                        rhs=w_codes[b][:].bitcast(FP8X4), rhs_scale=w_plane[b][:], start=True, stop=True,
-                    )
-                nc.vector.tensor_copy(
-                    out=o_grouped[:, b * QB : (b + 1) * QB, 2 * g : 2 * g + 2], in_=acc[:].rearrange("p s q -> p q s")
-                )
-                nc.scalar.copy(out=y[:, 2 * g : 2 * g + 2, :], in_=acc[:])
-                if b == BLOCKS - 1:
-                    nc.sync.dma_start(
-                        out=out_rows[:, 2 * g : 2 * g + 2, b * QB : (b + 1) * QB], in_=y[:, 2 * g : 2 * g + 2, :]
-                    )
-            if b < BLOCKS - 1:
-                nc.sync.dma_start(out=out_rows[:, :, b * QB : (b + 1) * QB], in_=y[:])
+
+        def product(acc, b, t):
+            nc.tensor.matmul_mx(
+                out=acc, lhsT=v_codes[:, P * t : P * (t + 1)].bitcast(FP8X4),
+                lhsT_scale=v_plane[:, P * t : P * (t + 1)],
+                rhs=w_codes[b][:].bitcast(FP8X4), rhs_scale=w_plane[b][:], start=True, stop=True,
+            )
+
+        first = ps.tile([P, PACK, QB], F32, name="first")
+        for t in range(PACK):
+            product(first[:, t, :], 0, t)
+        y = sb.tile([P, PACK, QB], F32, name="y_first")
+        nc.scalar.copy(out=y[:], in_=first[:])
+        nc.sync.dma_start(out=out_rows[:, :, 0:QB], in_=y[:])
+        nc.scalar.copy(out=o_grouped[:, 0:QB, :], in_=first[:].rearrange("p t q -> p q t"))
+        for g in range(2):
+            acc = ps.tile([P, 2, QB], F32, name=f"last{g}")
+            for s in range(2):
+                product(acc[:, s, :], 1, 2 * g + s)
+            nc.vector.tensor_copy(out=o_grouped[:, QB:Q, 2 * g : 2 * g + 2], in_=acc[:].rearrange("p s q -> p q s"))
+            y = sb.tile([P, 2, QB], F32, name=f"y_last{g}")
+            nc.scalar.copy(out=y[:], in_=acc[:])
+            nc.sync.dma_start(out=out_rows[:, 2 * g : 2 * g + 2, QB:Q], in_=y[:])
         nc.vector.quantize_mx(
             out=o_codes[:].bitcast(FP8X4), scales=o_plane[:], in_=o_grouped[:].rearrange("p c t -> p (c t)")
         )
         nc.sync.dma_start(out=out_1[0].rearrange("p c t -> p (c t)").bitcast(I32), in_=o_codes[:])
-        for x in range(4):
-            queue = nc.scalar if x % 2 == 0 else nc.sync
-            queue.dma_start(
-                out=out_2[0, 4 * x : 4 * x + 4, :].bitcast(I32), in_=o_plane[32 * x : 32 * x + 4, :].bitcast(I32)
-            )
+        for j in range(4):
+            queue = nc.scalar if j % 2 == 0 else nc.sync
+            queue.dma_start(out=out_2[0, j:16:4, :].bitcast(I32), in_=o_plane[j:P:32, :].bitcast(I32))

@@ -21,7 +21,7 @@ P = 128
 PACK = 4
 QB = 128
 BLOCKS = Q // QB
-V_CUTS = (0, 192, 384, 512)
+V_CUT = 256
 
 
 def interleave(copy, grouped, planes):
@@ -39,41 +39,38 @@ def tile_attend_pqresid_pl_kernel(
         sb = ctx.enter_context(tc.tile_pool(name="sb", bufs=1))
         ps = ctx.enter_context(tc.psum_pool(name="ps", bufs=1))
 
+        reuse = ctx.enter_context(tc.tile_pool(name="reuse", bufs=1))
+
         size_col = sb.tile([P, PACK], F32, name="size_col")
         nc.gpsimd.dma_start(out=size_col[:], in_=size.rearrange("o (p t) -> p (o t)", t=PACK))
         ident = sb.tile([P, P], F32, name="ident")
         make_identity(nc, ident[:])
 
+        book_list = sb.tile([P, SLOTS // 16], U16, name="book_list")
+        nc.sync.dma_start(book_list[:], offs)
+        fine_list = sb.tile([P, SLOTS // 16], U16, name="fine_list")
+        nc.sync.dma_start(fine_list[:], offs2)
+        book_sc = sb.tile([P, C], U8, name="book_sc")
+        nc.vector.memset(book_sc[:].bitcast(I32), 0)
+        nc.sync.dma_start(out=book_sc[0:P:8, :].bitcast(I32), in_=book_scales[0].bitcast(I32))
+        fine_sc = reuse.tile([P, T], U8, name="fine_sc", offset=0, align_bytes=64)
+        nc.vector.memset(fine_sc[:].bitcast(I32), 0)
+        nc.sync.dma_start(out=fine_sc[0:P:8, :].bitcast(I32), in_=fine_scales[0].bitcast(I32))
+
+        q_raw = sb.tile([P, PACK, Q], F32, name="q_raw")
+        nc.scalar.dma_start(out=q_raw[:], in_=query.rearrange("(p j) q -> p j q", j=PACK))
+        book_w = sb.tile([P, C], I32, name="book_w", tag="book_w", align_bytes=64)
+        nc.scalar.dma_start(out=book_w[:], in_=book_words[0].rearrange("p n t -> p (n t)").bitcast(I32))
+        fine_w = sb.tile([P, T], U16, name="fine_w")
+        nc.scalar.dma_start(out=fine_w[:].bitcast(I32), in_=fine_words[0].bitcast(I32))
+        vals_rows = vals.rearrange("(p j) e -> p j e", j=PACK)
+        v_lo = sb.tile([P, PACK, V_CUT], F32, name="v_lo")
+        nc.scalar.dma_start(out=v_lo[:], in_=vals_rows[:, :, 0:V_CUT])
+
         warm_in = sb.tile([P, 1], F32, name="warm_in")
         nc.vector.memset(warm_in[:], 0.0)
         warm_out = sb.tile([P, 1], F32, name="warm_out")
         nc.scalar.activation(out=warm_out[:], in_=warm_in[:], func=ACT.Exp)
-
-        book_list = sb.tile([P, SLOTS // 16], U16, name="book_list")
-        nc.sync.dma_start(book_list[:], offs)
-        book_sc = sb.tile([P, C], U8, name="book_sc")
-        nc.sync.dma_start(
-            out=book_sc[:].bitcast(I32),
-            in_=book_scales[0].bitcast(I32).unsqueeze(1).to_broadcast([16, 8, C // 4]),
-        )
-        fine_list = sb.tile([P, SLOTS // 16], U16, name="fine_list")
-        nc.sync.dma_start(fine_list[:], offs2)
-        fine_sc = sb.tile([P, T], U8, name="fine_sc", tag="then_later_vals")
-        nc.sync.dma_start(
-            out=fine_sc[:].bitcast(I32),
-            in_=fine_scales[0].bitcast(I32).unsqueeze(1).to_broadcast([16, 8, T // 4]),
-        )
-        q_rows = query.rearrange("(p j) q -> p j q", j=PACK)
-        q_raw = [sb.tile([P, PACK, QB], F32, name=f"q_raw{b}") for b in range(BLOCKS)]
-        nc.sync.dma_start(out=q_raw[0][:], in_=q_rows[:, :, 0:QB])
-        book_w = sb.tile([P, C], I32, name="book_w")
-        nc.sync.dma_start(out=book_w[:], in_=book_words[0].rearrange("p n t -> p (n t)").bitcast(I32))
-        fine_w = sb.tile([P, T], U16, name="fine_w")
-        nc.sync.dma_start(out=fine_w[:].bitcast(I32), in_=fine_words[0].bitcast(I32))
-        nc.sync.dma_start(out=q_raw[1][:], in_=q_rows[:, :, QB:Q])
-        vals_rows = vals.rearrange("(p j) e -> p j e", j=PACK)
-        v_first = sb.tile([P, PACK, V_CUTS[1]], F32, name="v_first")
-        nc.sync.dma_start(out=v_first[:], in_=vals_rows[:, :, 0 : V_CUTS[1]])
 
         key_planes = sb.tile([P, 2 * SLOTS], U8, name="key_planes", align_bytes=64)
         nc.vector.memset(key_planes[:].bitcast(I32), 0)
@@ -85,29 +82,27 @@ def tile_attend_pqresid_pl_kernel(
         nc.vector.tensor_copy(picked[:, SLOTS : 2 * SLOTS], fine_sc[:].indirect(fine_list[:]))
         for j in range(4):
             nc.sync.dma_start(out=key_planes[j:P:32, :].bitcast(I32), in_=picked[8 * j : P : 32, :].bitcast(I32))
-        v_rest = sb.tile([P, PACK * (E - V_CUTS[1])], F32, name="v_rest", tag="then_later_vals")
-        v_raw = [v_first[:]]
-        for lo, hi in zip(V_CUTS[1:-1], V_CUTS[2:]):
-            at = PACK * (lo - V_CUTS[1])
-            piece = v_rest[:, at : at + PACK * (hi - lo)].rearrange("p (j e) -> p j e", j=PACK)
-            nc.sync.dma_start(out=piece, in_=vals_rows[:, :, lo:hi])
-            v_raw.append(piece)
-        q_codes, q_plane = [], []
-        for b in range(BLOCKS):
-            grouped = sb.tile([P, QB, PACK], BF16, name=f"q_grouped{b}", tag=f"keys{b}", align_bytes=64)
-            interleave(nc.scalar.copy, grouped[:], q_raw[b][:])
-            codes = sb.tile([P, QB], U32, name=f"q_codes{b}", align_bytes=64)
-            plane = sb.tile([P, QB], U8, name=f"q_plane{b}", align_bytes=64)
-            nc.vector.quantize_mx(
-                out=codes[:].bitcast(FP8X4), scales=plane[:], in_=grouped[:].rearrange("p c t -> p (c t)")
-            )
-            q_codes.append(codes)
-            q_plane.append(plane)
+        v_hi = reuse.tile([P, PACK, E - V_CUT], F32, name="v_hi", offset=T // 2, align_bytes=64)
+        nc.sync.dma_start(out=v_hi[:], in_=vals_rows[:, :, V_CUT:E])
 
+        q_codes = [
+            reuse.tile([P, QB], U32, name="q_codes0", offset=0, align_bytes=64),
+            sb.tile([P, QB], U32, name="q_codes1", tag="book_w", align_bytes=64),
+        ]
+        q_plane = [sb.tile([P, QB], U8, name=f"q_plane{b}", align_bytes=64) for b in range(BLOCKS)]
+
+        def quantise_queries(b):
+            grouped = sb.tile([P, QB, PACK], BF16, name=f"q_grouped{b}", tag=f"keys{b}", align_bytes=64)
+            interleave(nc.scalar.copy, grouped[:], q_raw[:, :, QB * b : QB * (b + 1)])
+            nc.vector.quantize_mx(
+                out=q_codes[b][:].bitcast(FP8X4), scales=q_plane[b][:], in_=grouped[:].rearrange("p c t -> p (c t)")
+            )
+
+        quantise_queries(0)
         book_keys = sb.tile([P, SLOTS], U32, name="book_keys", tag="keys0", align_bytes=64)
         nc.vector.tensor_copy(book_keys[:], book_w[:].bitcast(U32).indirect(book_list[:]))
-
-        fine_keys = sb.tile([P, SLOTS], U16, name="fine_keys", align_bytes=64)
+        quantise_queries(1)
+        fine_keys = sb.tile([P, SLOTS], U16, name="fine_keys", tag="keys1", align_bytes=64)
         nc.vector.tensor_copy(fine_keys[:], fine_w[:].indirect(fine_list[:]))
 
         size_ps = ps.tile([P, PACK, P], F32, name="size_ps")
@@ -115,30 +110,22 @@ def tile_attend_pqresid_pl_kernel(
             nc.tensor.transpose(size_ps[:, t, :], size_col[:, t : t + 1].to_broadcast([P, P]), ident[:])
 
         scores = [ps.tile([P, SLOTS], F32, name=f"scores{b}") for b in range(BLOCKS)]
-        for b in range(BLOCKS):
-            nc.tensor.matmul_mx(
-                out=scores[b][:], lhsT=q_codes[b][:].bitcast(FP8X4), lhsT_scale=q_plane[b][:],
-                rhs=book_keys[:].bitcast(FP8X4), rhs_scale=book_plane, start=True, stop=False,
-            )
-            nc.tensor.matmul_mx(
-                out=scores[b][:], lhsT=q_codes[b][:].bitcast(FP8X4), lhsT_scale=q_plane[b][:],
-                rhs=fine_keys[:].bitcast(FP4X4), rhs_scale=fine_plane, start=False, stop=True,
-            )
+        for keys, plane, first_pass in ((book_keys[:].bitcast(FP8X4), book_plane, True), (fine_keys[:].bitcast(FP4X4), fine_plane, False)):
+            for b in range(BLOCKS):
+                nc.tensor.matmul_mx(
+                    out=scores[b][:], lhsT=q_codes[b][:].bitcast(FP8X4), lhsT_scale=q_plane[b][:],
+                    rhs=keys, rhs_scale=plane, start=first_pass, stop=not first_pass,
+                )
 
         v_grouped = sb.tile([P, PACK, P, PACK], BF16, name="v_grouped", align_bytes=64)
 
-        def deal_vals(copy, piece):
-            lo, hi = V_CUTS[piece], V_CUTS[piece + 1]
-            copy(
-                out=v_grouped[:, :, lo // PACK : hi // PACK, :].rearrange("p t m j -> p m j t"),
-                in_=v_raw[piece].rearrange("p j (m t) -> p m j t", t=PACK),
-            )
-
-        deal_vals(nc.vector.tensor_copy, 0)
-        deal_vals(nc.scalar.copy, 1)
+        nc.scalar.copy(
+            out=v_grouped[:, :, 0 : V_CUT // PACK, :].rearrange("p t m j -> p m j t"),
+            in_=v_lo[:].rearrange("p j (m t) -> p m j t", t=PACK),
+        )
         nc.gpsimd.tensor_scalar(
-            out=v_grouped[:, :, V_CUTS[2] // PACK :, :].rearrange("p t m j -> p m t j"),
-            in0=v_raw[2].rearrange("p j (m t) -> p m t j", t=PACK),
+            out=v_grouped[:, :, V_CUT // PACK :, :],
+            in0=v_hi[:].rearrange("p j (m t) -> p t m j", t=PACK),
             scalar1=1.0, scalar2=0.0, op0=ALU.mult, op1=ALU.add,
         )
 

@@ -21,7 +21,7 @@ P = 128
 PACK = 4
 QB = 128
 BLOCKS = Q // QB
-V_CUT = 256
+V_CUT = 224
 
 
 def interleave(copy, grouped, planes):
@@ -41,31 +41,33 @@ def tile_attend_pqresid_pl_kernel(
 
         reuse = ctx.enter_context(tc.tile_pool(name="reuse", bufs=1))
 
-        size_col = sb.tile([P, PACK], F32, name="size_col")
-        nc.gpsimd.dma_start(out=size_col[:], in_=size.rearrange("o (p t) -> p (o t)", t=PACK))
         ident = sb.tile([P, P], F32, name="ident")
         make_identity(nc, ident[:])
 
+        fine_at = 4 * PACK * (E - V_CUT)
         book_list = sb.tile([P, SLOTS // 16], U16, name="book_list")
         nc.sync.dma_start(book_list[:], offs)
+        book_sc = sb.tile([P, C], U8, name="book_sc")
+        nc.sync.dma_start(
+            out=book_sc[:].bitcast(I32),
+            in_=book_scales[0].bitcast(I32).unsqueeze(1).to_broadcast([16, 8, C // 4]),
+        )
         fine_list = sb.tile([P, SLOTS // 16], U16, name="fine_list")
         nc.sync.dma_start(fine_list[:], offs2)
-        book_sc = sb.tile([P, C], U8, name="book_sc")
-        nc.vector.memset(book_sc[:].bitcast(I32), 0)
-        nc.sync.dma_start(out=book_sc[0:P:8, :].bitcast(I32), in_=book_scales[0].bitcast(I32))
-        fine_sc = reuse.tile([P, T], U8, name="fine_sc", offset=0, align_bytes=64)
-        nc.vector.memset(fine_sc[:].bitcast(I32), 0)
-        nc.sync.dma_start(out=fine_sc[0:P:8, :].bitcast(I32), in_=fine_scales[0].bitcast(I32))
-
+        fine_sc = reuse.tile([P, T], U8, name="fine_sc", offset=fine_at, align_bytes=64)
+        nc.sync.dma_start(
+            out=fine_sc[:].bitcast(I32),
+            in_=fine_scales[0].bitcast(I32).unsqueeze(1).to_broadcast([16, 8, T // 4]),
+        )
+        size_col = sb.tile([P, PACK], F32, name="size_col")
+        nc.sync.dma_start(out=size_col[:], in_=size.rearrange("o (p t) -> p (o t)", t=PACK))
         q_raw = sb.tile([P, PACK, Q], F32, name="q_raw")
-        nc.scalar.dma_start(out=q_raw[:], in_=query.rearrange("(p j) q -> p j q", j=PACK))
+        nc.sync.dma_start(out=q_raw[:], in_=query.rearrange("(p j) q -> p j q", j=PACK))
         book_w = sb.tile([P, C], I32, name="book_w", tag="book_w", align_bytes=64)
-        nc.scalar.dma_start(out=book_w[:], in_=book_words[0].rearrange("p n t -> p (n t)").bitcast(I32))
+        nc.sync.dma_start(out=book_w[:], in_=book_words[0].rearrange("p n t -> p (n t)").bitcast(I32))
         fine_w = sb.tile([P, T], U16, name="fine_w")
-        nc.scalar.dma_start(out=fine_w[:].bitcast(I32), in_=fine_words[0].bitcast(I32))
+        nc.sync.dma_start(out=fine_w[:].bitcast(I32), in_=fine_words[0].bitcast(I32))
         vals_rows = vals.rearrange("(p j) e -> p j e", j=PACK)
-        v_lo = sb.tile([P, PACK, V_CUT], F32, name="v_lo")
-        nc.scalar.dma_start(out=v_lo[:], in_=vals_rows[:, :, 0:V_CUT])
 
         warm_in = sb.tile([P, 1], F32, name="warm_in")
         nc.vector.memset(warm_in[:], 0.0)
@@ -82,11 +84,13 @@ def tile_attend_pqresid_pl_kernel(
         nc.vector.tensor_copy(picked[:, SLOTS : 2 * SLOTS], fine_sc[:].indirect(fine_list[:]))
         for j in range(4):
             nc.sync.dma_start(out=key_planes[j:P:32, :].bitcast(I32), in_=picked[8 * j : P : 32, :].bitcast(I32))
-        v_hi = reuse.tile([P, PACK, E - V_CUT], F32, name="v_hi", offset=T // 2, align_bytes=64)
+        v_lo = reuse.tile([P, PACK, V_CUT], F32, name="v_lo", offset=fine_at + T - 64, align_bytes=64)
+        nc.sync.dma_start(out=v_lo[:], in_=vals_rows[:, :, 0:V_CUT])
+        v_hi = reuse.tile([P, PACK, E - V_CUT], F32, name="v_hi", offset=64, align_bytes=64)
         nc.sync.dma_start(out=v_hi[:], in_=vals_rows[:, :, V_CUT:E])
 
         q_codes = [
-            reuse.tile([P, QB], U32, name="q_codes0", offset=0, align_bytes=64),
+            reuse.tile([P, QB], U32, name="q_codes0", offset=fine_at + 512, align_bytes=64),
             sb.tile([P, QB], U32, name="q_codes1", tag="book_w", align_bytes=64),
         ]
         q_plane = [sb.tile([P, QB], U8, name=f"q_plane{b}", align_bytes=64) for b in range(BLOCKS)]
@@ -129,13 +133,17 @@ def tile_attend_pqresid_pl_kernel(
             scalar1=1.0, scalar2=0.0, op0=ALU.mult, op1=ALU.add,
         )
 
+        probs_tiles = [
+            reuse.tile([P, 2, P, 2], F32, name="probs0", offset=fine_at + T - 64, align_bytes=64),
+            sb.tile([P, 2, P, 2], F32, name="probs1", tag="probs1", align_bytes=64),
+        ]
         neg_max, probs, row_sum = [], [], []
         for b in range(BLOCKS):
             nm = sb.tile([P, 1], F32, name=f"neg_max{b}")
             nc.vector.tensor_reduce(out=nm[:], in_=scores[b][:], axis=mybir.AxisListType.X, op=ALU.max, negate=True)
             neg_max.append(nm)
         for b in range(BLOCKS):
-            pr = sb.tile([P, 2, P, 2], F32, name=f"probs{b}", tag=f"probs{b}", align_bytes=64)
+            pr = probs_tiles[b]
             rs = sb.tile([P, 1], F32, name=f"row_sum{b}")
             nc.scalar.activation(
                 out=pr[:], in_=scores[b][:].rearrange("q (p u e) -> q u p e", u=2, e=2),

@@ -21,7 +21,7 @@ P = 128
 PACK = 4
 QB = 128
 BLOCKS = Q // QB
-V_CUT = 224
+V_CUTS = (0, 192, 352, 512)
 
 
 def interleave(copy, grouped, planes):
@@ -39,12 +39,13 @@ def tile_attend_pqresid_pl_kernel(
         sb = ctx.enter_context(tc.tile_pool(name="sb", bufs=1))
         ps = ctx.enter_context(tc.psum_pool(name="ps", bufs=1))
 
+        words = ctx.enter_context(tc.tile_pool(name="words", bufs=1))
         reuse = ctx.enter_context(tc.tile_pool(name="reuse", bufs=1))
 
         ident = sb.tile([P, P], F32, name="ident")
         make_identity(nc, ident[:])
 
-        fine_at = 4 * PACK * (E - V_CUT)
+        fine_at = 4 * PACK * (E - V_CUTS[1])
         book_list = sb.tile([P, SLOTS // 16], U16, name="book_list")
         nc.sync.dma_start(book_list[:], offs)
         book_sc = sb.tile([P, C], U8, name="book_sc")
@@ -54,29 +55,23 @@ def tile_attend_pqresid_pl_kernel(
         )
         fine_list = sb.tile([P, SLOTS // 16], U16, name="fine_list")
         nc.sync.dma_start(fine_list[:], offs2)
-        fine_sc = reuse.tile([P, T], U8, name="fine_sc", offset=fine_at, align_bytes=64)
-        nc.sync.dma_start(
-            out=fine_sc[:].bitcast(I32),
-            in_=fine_scales[0].bitcast(I32).unsqueeze(1).to_broadcast([16, 8, T // 4]),
-        )
-        size_col = sb.tile([P, PACK], F32, name="size_col")
-        nc.sync.dma_start(out=size_col[:], in_=size.rearrange("o (p t) -> p (o t)", t=PACK))
         q_raw = sb.tile([P, PACK, Q], F32, name="q_raw")
         nc.sync.dma_start(out=q_raw[:], in_=query.rearrange("(p j) q -> p j q", j=PACK))
-        book_w = sb.tile([P, C], I32, name="book_w", tag="book_w", align_bytes=64)
-        nc.sync.dma_start(out=book_w[:], in_=book_words[0].rearrange("p n t -> p (n t)").bitcast(I32))
-        fine_w = sb.tile([P, T], U16, name="fine_w")
-        nc.sync.dma_start(out=fine_w[:].bitcast(I32), in_=fine_words[0].bitcast(I32))
-        vals_rows = vals.rearrange("(p j) e -> p j e", j=PACK)
-
-        warm_in = sb.tile([P, 1], F32, name="warm_in")
+        fine_sc = reuse.tile([P, T], U8, name="fine_sc", offset=fine_at, align_bytes=64)
+        nc.vector.memset(fine_sc[:].bitcast(I32), 0)
+        nc.sync.dma_start(out=fine_sc[0:P:8, :].bitcast(I32), in_=fine_scales[0].bitcast(I32))
+        warm_in = words.tile([P, 16], F32, name="warm_in", offset=4 * C - 32)
         nc.vector.memset(warm_in[:], 0.0)
-        warm_out = sb.tile([P, 1], F32, name="warm_out")
-        nc.scalar.activation(out=warm_out[:], in_=warm_in[:], func=ACT.Exp)
+        one = sb.tile([P, 16], F32, name="one")
+        nc.scalar.activation(out=one[:], in_=warm_in[:], func=ACT.Exp)
+        fine_w = words.tile([P, T], U16, name="fine_w", offset=0)
+        nc.sync.dma_start(out=fine_w[:].bitcast(I32), in_=fine_words[0].bitcast(I32))
+        book_w = words.tile([P, C], I32, name="book_w", offset=2 * T)
+        nc.sync.dma_start(out=book_w[:], in_=book_words[0].rearrange("p n t -> p (n t)").bitcast(I32))
+        vals_rows = vals.rearrange("(p j) e -> p j e", j=PACK)
 
         key_planes = sb.tile([P, 2 * SLOTS], U8, name="key_planes", align_bytes=64)
         nc.vector.memset(key_planes[:].bitcast(I32), 0)
-        book_plane = key_planes[:, 0:SLOTS]
         fine_plane = key_planes[:, SLOTS : 2 * SLOTS]
 
         picked = sb.tile([P, 2 * SLOTS], U8, name="picked", align_bytes=64)
@@ -84,14 +79,21 @@ def tile_attend_pqresid_pl_kernel(
         nc.vector.tensor_copy(picked[:, SLOTS : 2 * SLOTS], fine_sc[:].indirect(fine_list[:]))
         for j in range(4):
             nc.sync.dma_start(out=key_planes[j:P:32, :].bitcast(I32), in_=picked[8 * j : P : 32, :].bitcast(I32))
-        v_lo = reuse.tile([P, PACK, V_CUT], F32, name="v_lo", offset=fine_at + T - 64, align_bytes=64)
-        nc.sync.dma_start(out=v_lo[:], in_=vals_rows[:, :, 0:V_CUT])
-        v_hi = reuse.tile([P, PACK, E - V_CUT], F32, name="v_hi", offset=64, align_bytes=64)
-        nc.sync.dma_start(out=v_hi[:], in_=vals_rows[:, :, V_CUT:E])
+        size_col = reuse.tile([P, PACK], F32, name="size_col", offset=fine_at + 1024)
+        nc.sync.dma_start(out=size_col[:], in_=size.rearrange("o (p t) -> p (o t)", t=PACK))
+        v_lo = reuse.tile([P, PACK, V_CUTS[1]], F32, name="v_lo", offset=fine_at + T - 64, align_bytes=64)
+        nc.sync.dma_start(out=v_lo[:], in_=vals_rows[:, :, 0 : V_CUTS[1]])
+        v_rest = reuse.tile([P, PACK * (E - V_CUTS[1])], F32, name="v_rest", offset=64, align_bytes=64)
+        v_pieces = []
+        for lo, hi in zip(V_CUTS[1:-1], V_CUTS[2:]):
+            at = PACK * (E - hi)
+            piece = v_rest[:, at : at + PACK * (hi - lo)].rearrange("p (j e) -> p j e", j=PACK)
+            nc.sync.dma_start(out=piece, in_=vals_rows[:, :, lo:hi])
+            v_pieces.append((piece, lo, hi))
 
         q_codes = [
             reuse.tile([P, QB], U32, name="q_codes0", offset=fine_at + 512, align_bytes=64),
-            sb.tile([P, QB], U32, name="q_codes1", tag="book_w", align_bytes=64),
+            words.tile([P, QB], U32, name="q_codes1", offset=0, align_bytes=64),
         ]
         q_plane = [sb.tile([P, QB], U8, name=f"q_plane{b}", align_bytes=64) for b in range(BLOCKS)]
 
@@ -103,38 +105,46 @@ def tile_attend_pqresid_pl_kernel(
             )
 
         quantise_queries(0)
-        book_keys = sb.tile([P, SLOTS], U32, name="book_keys", tag="keys0", align_bytes=64)
-        nc.vector.tensor_copy(book_keys[:], book_w[:].bitcast(U32).indirect(book_list[:]))
-        quantise_queries(1)
-        fine_keys = sb.tile([P, SLOTS], U16, name="fine_keys", tag="keys1", align_bytes=64)
+        fine_keys = sb.tile([P, SLOTS], U16, name="fine_keys", tag="keys0", align_bytes=64)
         nc.vector.tensor_copy(fine_keys[:], fine_w[:].indirect(fine_list[:]))
+        quantise_queries(1)
+        half = SLOTS // 2
+        book_keys = sb.tile([P, SLOTS], U32, name="book_keys", tag="keys1", align_bytes=64)
+        for h in range(2):
+            nc.vector.tensor_copy(
+                book_keys[:, h * half : (h + 1) * half],
+                book_w[:].bitcast(U32).indirect(book_list[:, h * half // 16 : (h + 1) * half // 16]),
+            )
+
+        scores = [ps.tile([P, SLOTS], F32, name=f"scores{b}") for b in range(BLOCKS)]
+        for b in range(BLOCKS):
+            nc.tensor.matmul_mx(
+                out=scores[b][:], lhsT=q_codes[b][:].bitcast(FP8X4), lhsT_scale=q_plane[b][:],
+                rhs=fine_keys[:].bitcast(FP4X4), rhs_scale=fine_plane, start=True, stop=False,
+            )
+        for b in range(BLOCKS):
+            for h in range(2):
+                cols = slice(h * half, (h + 1) * half)
+                nc.tensor.matmul_mx(
+                    out=scores[b][:, cols], lhsT=q_codes[b][:].bitcast(FP8X4), lhsT_scale=q_plane[b][:],
+                    rhs=book_keys[:, cols].bitcast(FP8X4), rhs_scale=key_planes[:, cols], start=False, stop=h == 1,
+                )
 
         size_ps = ps.tile([P, PACK, P], F32, name="size_ps")
         for t in range(PACK):
             nc.tensor.transpose(size_ps[:, t, :], size_col[:, t : t + 1].to_broadcast([P, P]), ident[:])
 
-        scores = [ps.tile([P, SLOTS], F32, name=f"scores{b}") for b in range(BLOCKS)]
-        for keys, plane, first_pass in ((book_keys[:].bitcast(FP8X4), book_plane, True), (fine_keys[:].bitcast(FP4X4), fine_plane, False)):
-            for b in range(BLOCKS):
-                nc.tensor.matmul_mx(
-                    out=scores[b][:], lhsT=q_codes[b][:].bitcast(FP8X4), lhsT_scale=q_plane[b][:],
-                    rhs=keys, rhs_scale=plane, start=first_pass, stop=not first_pass,
-                )
-
         v_grouped = sb.tile([P, PACK, P, PACK], BF16, name="v_grouped", align_bytes=64)
 
-        nc.scalar.copy(
-            out=v_grouped[:, :, 0 : V_CUT // PACK, :].rearrange("p t m j -> p m j t"),
-            in_=v_lo[:].rearrange("p j (m t) -> p m j t", t=PACK),
-        )
-        nc.gpsimd.tensor_scalar(
-            out=v_grouped[:, :, V_CUT // PACK :, :],
-            in0=v_hi[:].rearrange("p j (m t) -> p t m j", t=PACK),
-            scalar1=1.0, scalar2=0.0, op0=ALU.mult, op1=ALU.add,
-        )
+        for piece, lo, hi in [(v_lo[:], 0, V_CUTS[1]), v_pieces[0]]:
+            nc.gpsimd.tensor_scalar(
+                out=v_grouped[:, :, lo // PACK : hi // PACK, :],
+                in0=piece.rearrange("p j (m t) -> p t m j", t=PACK),
+                scalar1=one[:, 0:1], scalar2=0.0, op0=ALU.mult, op1=ALU.add,
+            )
 
         probs_tiles = [
-            reuse.tile([P, 2, P, 2], F32, name="probs0", offset=fine_at + T - 64, align_bytes=64),
+            sb.tile([P, 2, P, 2], F32, name="probs0", align_bytes=64),
             sb.tile([P, 2, P, 2], F32, name="probs1", tag="probs1", align_bytes=64),
         ]
         neg_max, probs, row_sum = [], [], []
@@ -152,25 +162,33 @@ def tile_attend_pqresid_pl_kernel(
             probs.append(pr)
             row_sum.append(rs)
 
-        w_grouped = []
-        for b in range(BLOCKS):
-            inv = sb.tile([P, 1], F32, name=f"inv_sum{b}")
-            nc.vector.reciprocal(out=inv[:], in_=row_sum[b][:])
-            turned = ps.tile([P, 2, QB], F32, name=f"turned{b}")
-            for u in range(2):
-                w = sb.tile([P, P, 2], BF16, name=f"w{b}_{u}")
-                nc.vector.scalar_tensor_tensor(
-                    out=w[:], in0=probs[b][:, u, :, :], scalar=inv[:],
-                    in1=size_ps[:, 2 * u : 2 * u + 2, :].rearrange("q e p -> q p e"),
-                    op0=ALU.mult, op1=ALU.mult,
-                )
-                nc.tensor.transpose(turned[:, u, :], w[:].rearrange("q p e -> q (p e)").bitcast(F32), ident[:])
-            grouped = sb.tile([P, QB * PACK], BF16, name=f"w_grouped{b}", align_bytes=64)
-            nc.scalar.copy(
-                out=grouped[:].bitcast(F32).rearrange("p (q u) -> p q u", u=2),
-                in_=turned[:].rearrange("p u q -> p q u"),
+        nc.scalar.copy(
+            out=v_grouped[:, :, V_CUTS[2] // PACK :, :].rearrange("p t m j -> p m j t"),
+            in_=v_pieces[1][0].rearrange("p j (m t) -> p m j t", t=PACK),
+        )
+
+        inv = [sb.tile([P, 1], F32, name=f"inv_sum{b}") for b in range(BLOCKS)]
+        turned = [ps.tile([P, 2, QB], F32, name=f"turned{b}") for b in range(BLOCKS)]
+        w_grouped = [sb.tile([P, QB * PACK], BF16, name=f"w_grouped{b}", align_bytes=64) for b in range(BLOCKS)]
+
+        def weigh(b, u):
+            w = sb.tile([P, P, 2], BF16, name=f"w{b}_{u}")
+            nc.vector.scalar_tensor_tensor(
+                out=w[:], in0=probs[b][:, u, :, :], scalar=inv[b][:],
+                in1=size_ps[:, 2 * u : 2 * u + 2, :].rearrange("q e p -> q p e"),
+                op0=ALU.mult, op1=ALU.mult,
             )
-            w_grouped.append(grouped)
+            nc.tensor.transpose(turned[b][:, u, :], w[:].rearrange("q p e -> q (p e)").bitcast(F32), ident[:])
+
+        for b in range(BLOCKS):
+            nc.vector.reciprocal(out=inv[b][:], in_=row_sum[b][:])
+        for b in range(BLOCKS):
+            for u in range(2):
+                weigh(b, u)
+            nc.scalar.copy(
+                out=w_grouped[b][:].bitcast(F32).rearrange("p (q u) -> p q u", u=2),
+                in_=turned[b][:].rearrange("p u q -> p q u"),
+            )
 
         v_codes = sb.tile([P, E], U32, name="v_codes", tag=f"probs{BLOCKS - 1}", align_bytes=64)
         v_plane = sb.tile([P, E], U8, name="v_plane", align_bytes=64)
@@ -214,9 +232,12 @@ def tile_attend_pqresid_pl_kernel(
             y = sb.tile([P, 2, QB], F32, name=f"y_last{g}")
             nc.scalar.copy(out=y[:], in_=acc[:])
             nc.sync.dma_start(out=out_rows[:, 2 * g : 2 * g + 2, QB:Q], in_=y[:])
-        nc.vector.quantize_mx(
-            out=o_codes[:].bitcast(FP8X4), scales=o_plane[:], in_=o_grouped[:].rearrange("p c t -> p (c t)")
-        )
+        for b in range(BLOCKS):
+            cols = slice(QB * b, QB * (b + 1))
+            nc.vector.quantize_mx(
+                out=o_codes[:, cols].bitcast(FP8X4), scales=o_plane[:, cols],
+                in_=o_grouped[:, cols, :].rearrange("p c t -> p (c t)"),
+            )
         nc.sync.dma_start(out=out_1[0].rearrange("p c t -> p (c t)").bitcast(I32), in_=o_codes[:])
         for j in range(4):
             queue = nc.scalar if j % 2 == 0 else nc.sync

@@ -21,14 +21,12 @@ P = 128
 PACK = 4
 QB = 128
 BLOCKS = Q // QB
-V_CUTS = (0, 192, 352, 512)
-
-
-def interleave(copy, grouped, planes):
-    copy(
-        out=grouped.rearrange("p (c i) t -> p c t i", i=4),
-        in_=planes.rearrange("p t (c i) -> p c t i", i=4),
-    )
+GROUP = 16
+SCALE_ROWS = D // 32
+ROW_STEP = P // SCALE_ROWS
+QUADRANT = 32
+HALF = SLOTS // 2
+V_CUTS = (0, 160, 352, 512)
 
 
 def tile_attend_pqresid_pl_kernel(
@@ -38,93 +36,100 @@ def tile_attend_pqresid_pl_kernel(
     with ExitStack() as ctx:
         sb = ctx.enter_context(tc.tile_pool(name="sb", bufs=1))
         ps = ctx.enter_context(tc.psum_pool(name="ps", bufs=1))
-
         words = ctx.enter_context(tc.tile_pool(name="words", bufs=1))
-        reuse = ctx.enter_context(tc.tile_pool(name="reuse", bufs=1))
+        late = ctx.enter_context(tc.tile_pool(name="late", bufs=1))
 
         ident = sb.tile([P, P], F32, name="ident")
         make_identity(nc, ident[:])
 
-        fine_at = 4 * PACK * (E - V_CUTS[1])
-        book_list = sb.tile([P, SLOTS // 16], U16, name="book_list")
+        book_list = sb.tile([P, SLOTS // GROUP], U16, name="book_list")
         nc.sync.dma_start(book_list[:], offs)
         book_sc = sb.tile([P, C], U8, name="book_sc")
         nc.sync.dma_start(
             out=book_sc[:].bitcast(I32),
-            in_=book_scales[0].bitcast(I32).unsqueeze(1).to_broadcast([16, 8, C // 4]),
+            in_=book_scales[0].bitcast(I32).unsqueeze(1).to_broadcast([SCALE_ROWS, ROW_STEP, C // 4]),
         )
-        fine_list = sb.tile([P, SLOTS // 16], U16, name="fine_list")
+        fine_list = sb.tile([P, SLOTS // GROUP], U16, name="fine_list")
         nc.sync.dma_start(fine_list[:], offs2)
         q_raw = sb.tile([P, PACK, Q], F32, name="q_raw")
         nc.sync.dma_start(out=q_raw[:], in_=query.rearrange("(p j) q -> p j q", j=PACK))
-        fine_sc = reuse.tile([P, T], U8, name="fine_sc", offset=fine_at, align_bytes=64)
+
+        fine_at = 4 * PACK * (E - V_CUTS[1])
+        fine_sc = late.tile([P, T], U8, name="fine_sc", offset=fine_at, align_bytes=64)
         nc.vector.memset(fine_sc[:].bitcast(I32), 0)
-        nc.sync.dma_start(out=fine_sc[0:P:8, :].bitcast(I32), in_=fine_scales[0].bitcast(I32))
-        warm_in = words.tile([P, 16], F32, name="warm_in", offset=4 * C - 32)
-        nc.vector.memset(warm_in[:], 0.0)
-        one = sb.tile([P, 16], F32, name="one")
-        nc.scalar.activation(out=one[:], in_=warm_in[:], func=ACT.Exp)
+        nc.sync.dma_start(out=fine_sc[0:P:ROW_STEP, :].bitcast(I32), in_=fine_scales[0].bitcast(I32))
+
+        words_meet = 2 * T
+        zeros = words.tile([P, 16], F32, name="zeros", offset=words_meet - 32)
+        nc.vector.memset(zeros[:, 7:9], 0.0)
+        ones = sb.tile([P, 2], F32, name="ones")
+        nc.scalar.activation(out=ones[:], in_=zeros[:, 7:9], func=ACT.Exp)
         fine_w = words.tile([P, T], U16, name="fine_w", offset=0)
         nc.sync.dma_start(out=fine_w[:].bitcast(I32), in_=fine_words[0].bitcast(I32))
-        book_w = words.tile([P, C], I32, name="book_w", offset=2 * T)
+        book_w = words.tile([P, C], I32, name="book_w", offset=words_meet)
         nc.sync.dma_start(out=book_w[:], in_=book_words[0].rearrange("p n t -> p (n t)").bitcast(I32))
-        vals_rows = vals.rearrange("(p j) e -> p j e", j=PACK)
 
         key_planes = sb.tile([P, 2 * SLOTS], U8, name="key_planes", align_bytes=64)
         nc.vector.memset(key_planes[:].bitcast(I32), 0)
-        fine_plane = key_planes[:, SLOTS : 2 * SLOTS]
 
         picked = sb.tile([P, 2 * SLOTS], U8, name="picked", align_bytes=64)
         nc.vector.tensor_copy(picked[:, 0:SLOTS], book_sc[:].indirect(book_list[:]))
         nc.vector.tensor_copy(picked[:, SLOTS : 2 * SLOTS], fine_sc[:].indirect(fine_list[:]))
         for j in range(4):
-            nc.sync.dma_start(out=key_planes[j:P:32, :].bitcast(I32), in_=picked[8 * j : P : 32, :].bitcast(I32))
-        size_col = reuse.tile([P, PACK], F32, name="size_col", offset=fine_at + 1024)
+            nc.sync.dma_start(
+                out=key_planes[j:P:QUADRANT, :].bitcast(I32),
+                in_=picked[ROW_STEP * j : P : QUADRANT, :].bitcast(I32),
+            )
+
+        vals_rows = vals.rearrange("(p j) e -> p j e", j=PACK)
+        v_first = late.tile([P, PACK, V_CUTS[1]], F32, name="v_first", offset=fine_at + T - 64, align_bytes=64)
+        nc.sync.dma_start(out=v_first[:], in_=vals_rows[:, :, 0 : V_CUTS[1]])
+        size_col = late.tile([P, PACK], F32, name="size_col", offset=fine_at + T // 2)
         nc.sync.dma_start(out=size_col[:], in_=size.rearrange("o (p t) -> p (o t)", t=PACK))
-        v_lo = reuse.tile([P, PACK, V_CUTS[1]], F32, name="v_lo", offset=fine_at + T - 64, align_bytes=64)
-        nc.sync.dma_start(out=v_lo[:], in_=vals_rows[:, :, 0 : V_CUTS[1]])
-        v_rest = reuse.tile([P, PACK * (E - V_CUTS[1])], F32, name="v_rest", offset=64, align_bytes=64)
-        v_pieces = []
+        v_rest = late.tile([P, PACK * (E - V_CUTS[1])], F32, name="v_rest", offset=64, align_bytes=64)
+        v_raw = [v_first[:]]
         for lo, hi in zip(V_CUTS[1:-1], V_CUTS[2:]):
             at = PACK * (E - hi)
             piece = v_rest[:, at : at + PACK * (hi - lo)].rearrange("p (j e) -> p j e", j=PACK)
             nc.sync.dma_start(out=piece, in_=vals_rows[:, :, lo:hi])
-            v_pieces.append((piece, lo, hi))
+            v_raw.append(piece)
 
         q_codes = [
-            reuse.tile([P, QB], U32, name="q_codes0", offset=fine_at + 512, align_bytes=64),
+            late.tile([P, QB], U32, name="q_codes0", offset=fine_at + T // 4, align_bytes=64),
             words.tile([P, QB], U32, name="q_codes1", offset=0, align_bytes=64),
         ]
         q_plane = [sb.tile([P, QB], U8, name=f"q_plane{b}", align_bytes=64) for b in range(BLOCKS)]
 
         def quantise_queries(b):
             grouped = sb.tile([P, QB, PACK], BF16, name=f"q_grouped{b}", tag=f"keys{b}", align_bytes=64)
-            interleave(nc.scalar.copy, grouped[:], q_raw[:, :, QB * b : QB * (b + 1)])
+            nc.scalar.copy(
+                out=grouped[:].rearrange("p (c i) j -> p c j i", i=4),
+                in_=q_raw[:, :, QB * b : QB * (b + 1)].rearrange("p j (c i) -> p c j i", i=4),
+            )
             nc.vector.quantize_mx(
-                out=q_codes[b][:].bitcast(FP8X4), scales=q_plane[b][:], in_=grouped[:].rearrange("p c t -> p (c t)")
+                out=q_codes[b][:].bitcast(FP8X4), scales=q_plane[b][:], in_=grouped[:].rearrange("p q j -> p (q j)")
             )
 
         quantise_queries(0)
         fine_keys = sb.tile([P, SLOTS], U16, name="fine_keys", tag="keys0", align_bytes=64)
         nc.vector.tensor_copy(fine_keys[:], fine_w[:].indirect(fine_list[:]))
         quantise_queries(1)
-        half = SLOTS // 2
         book_keys = sb.tile([P, SLOTS], U32, name="book_keys", tag="keys1", align_bytes=64)
         for h in range(2):
             nc.vector.tensor_copy(
-                book_keys[:, h * half : (h + 1) * half],
-                book_w[:].bitcast(U32).indirect(book_list[:, h * half // 16 : (h + 1) * half // 16]),
+                book_keys[:, h * HALF : (h + 1) * HALF],
+                book_w[:].bitcast(U32).indirect(book_list[:, h * HALF // GROUP : (h + 1) * HALF // GROUP]),
             )
 
         scores = [ps.tile([P, SLOTS], F32, name=f"scores{b}") for b in range(BLOCKS)]
         for b in range(BLOCKS):
             nc.tensor.matmul_mx(
                 out=scores[b][:], lhsT=q_codes[b][:].bitcast(FP8X4), lhsT_scale=q_plane[b][:],
-                rhs=fine_keys[:].bitcast(FP4X4), rhs_scale=fine_plane, start=True, stop=False,
+                rhs=fine_keys[:].bitcast(FP4X4), rhs_scale=key_planes[:, SLOTS : 2 * SLOTS], start=True, stop=False,
             )
         for b in range(BLOCKS):
             for h in range(2):
-                cols = slice(h * half, (h + 1) * half)
+                cols = slice(h * HALF, (h + 1) * HALF)
                 nc.tensor.matmul_mx(
                     out=scores[b][:, cols], lhsT=q_codes[b][:].bitcast(FP8X4), lhsT_scale=q_plane[b][:],
                     rhs=book_keys[:, cols].bitcast(FP8X4), rhs_scale=key_planes[:, cols], start=False, stop=h == 1,
@@ -135,75 +140,67 @@ def tile_attend_pqresid_pl_kernel(
             nc.tensor.transpose(size_ps[:, t, :], size_col[:, t : t + 1].to_broadcast([P, P]), ident[:])
 
         v_grouped = sb.tile([P, PACK, P, PACK], BF16, name="v_grouped", align_bytes=64)
-
-        for piece, lo, hi in [(v_lo[:], 0, V_CUTS[1]), v_pieces[0]]:
+        for piece in range(2):
+            lo, hi = V_CUTS[piece], V_CUTS[piece + 1]
             nc.gpsimd.tensor_scalar(
                 out=v_grouped[:, :, lo // PACK : hi // PACK, :],
-                in0=piece.rearrange("p j (m t) -> p t m j", t=PACK),
-                scalar1=one[:, 0:1], scalar2=0.0, op0=ALU.mult, op1=ALU.add,
+                in0=v_raw[piece].rearrange("p j (m t) -> p t m j", t=PACK),
+                scalar1=ones[:, piece : piece + 1], scalar2=0.0, op0=ALU.mult, op1=ALU.add,
             )
 
-        probs_tiles = [
+        probs = [
             sb.tile([P, 2, P, 2], F32, name="probs0", align_bytes=64),
             sb.tile([P, 2, P, 2], F32, name="probs1", tag="probs1", align_bytes=64),
         ]
-        neg_max, probs, row_sum = [], [], []
+        neg_max, row_sum = [], []
         for b in range(BLOCKS):
             nm = sb.tile([P, 1], F32, name=f"neg_max{b}")
             nc.vector.tensor_reduce(out=nm[:], in_=scores[b][:], axis=mybir.AxisListType.X, op=ALU.max, negate=True)
             neg_max.append(nm)
         for b in range(BLOCKS):
-            pr = probs_tiles[b]
             rs = sb.tile([P, 1], F32, name=f"row_sum{b}")
             nc.scalar.activation(
-                out=pr[:], in_=scores[b][:].rearrange("q (p u e) -> q u p e", u=2, e=2),
+                out=probs[b][:], in_=scores[b][:].rearrange("q (p u e) -> q u p e", u=2, e=2),
                 func=ACT.Exp, bias=neg_max[b][:], scale=1.0, accum_out=rs[:],
             )
-            probs.append(pr)
             row_sum.append(rs)
 
         nc.scalar.copy(
             out=v_grouped[:, :, V_CUTS[2] // PACK :, :].rearrange("p t m j -> p m j t"),
-            in_=v_pieces[1][0].rearrange("p j (m t) -> p m j t", t=PACK),
+            in_=v_raw[2].rearrange("p j (m t) -> p m j t", t=PACK),
         )
 
         inv = [sb.tile([P, 1], F32, name=f"inv_sum{b}") for b in range(BLOCKS)]
         turned = [ps.tile([P, 2, QB], F32, name=f"turned{b}") for b in range(BLOCKS)]
         w_grouped = [sb.tile([P, QB * PACK], BF16, name=f"w_grouped{b}", align_bytes=64) for b in range(BLOCKS)]
-
-        def weigh(b, u):
-            w = sb.tile([P, P, 2], BF16, name=f"w{b}_{u}")
-            nc.vector.scalar_tensor_tensor(
-                out=w[:], in0=probs[b][:, u, :, :], scalar=inv[b][:],
-                in1=size_ps[:, 2 * u : 2 * u + 2, :].rearrange("q e p -> q p e"),
-                op0=ALU.mult, op1=ALU.mult,
-            )
-            nc.tensor.transpose(turned[b][:, u, :], w[:].rearrange("q p e -> q (p e)").bitcast(F32), ident[:])
-
         for b in range(BLOCKS):
             nc.vector.reciprocal(out=inv[b][:], in_=row_sum[b][:])
         for b in range(BLOCKS):
             for u in range(2):
-                weigh(b, u)
+                w = sb.tile([P, P, 2], BF16, name=f"w{b}_{u}")
+                nc.vector.scalar_tensor_tensor(
+                    out=w[:], in0=probs[b][:, u, :, :], scalar=inv[b][:],
+                    in1=size_ps[:, 2 * u : 2 * u + 2, :].rearrange("q e p -> q p e"),
+                    op0=ALU.mult, op1=ALU.mult,
+                )
+                nc.tensor.transpose(turned[b][:, u, :], w[:].rearrange("q p e -> q (p e)").bitcast(F32), ident[:])
             nc.scalar.copy(
                 out=w_grouped[b][:].bitcast(F32).rearrange("p (q u) -> p q u", u=2),
                 in_=turned[b][:].rearrange("p u q -> p q u"),
             )
 
-        v_codes = sb.tile([P, E], U32, name="v_codes", tag=f"probs{BLOCKS - 1}", align_bytes=64)
+        v_codes = sb.tile([P, E], U32, name="v_codes", tag="probs1", align_bytes=64)
         v_plane = sb.tile([P, E], U8, name="v_plane", align_bytes=64)
-        w_codes, w_plane = [], []
+        w_codes = [sb.tile([P, QB], U32, name=f"w_codes{b}", align_bytes=64) for b in range(BLOCKS)]
+        w_plane = [sb.tile([P, QB], U8, name=f"w_plane{b}", align_bytes=64) for b in range(BLOCKS)]
+        nc.vector.quantize_mx(out=w_codes[0][:].bitcast(FP8X4), scales=w_plane[0][:], in_=w_grouped[0][:])
         for g in range(2):
+            cols = slice(2 * P * g, 2 * P * (g + 1))
             nc.vector.quantize_mx(
-                out=v_codes[:, 256 * g : 256 * g + 256].bitcast(FP8X4),
-                scales=v_plane[:, 256 * g : 256 * g + 256],
+                out=v_codes[:, cols].bitcast(FP8X4), scales=v_plane[:, cols],
                 in_=v_grouped[:, 2 * g : 2 * g + 2, :, :].rearrange("p t m j -> p (t m j)"),
             )
-            codes = sb.tile([P, QB], U32, name=f"w_codes{g}", align_bytes=64)
-            plane = sb.tile([P, QB], U8, name=f"w_plane{g}", align_bytes=64)
-            nc.vector.quantize_mx(out=codes[:].bitcast(FP8X4), scales=plane[:], in_=w_grouped[g][:])
-            w_codes.append(codes)
-            w_plane.append(plane)
+        nc.vector.quantize_mx(out=w_codes[1][:].bitcast(FP8X4), scales=w_plane[1][:], in_=w_grouped[1][:])
 
         o_codes = sb.tile([P, Q], I32, name="o_codes", align_bytes=64)
         o_plane = sb.tile([P, Q], U8, name="o_plane", align_bytes=64)
@@ -220,25 +217,28 @@ def tile_attend_pqresid_pl_kernel(
         first = ps.tile([P, PACK, QB], F32, name="first")
         for t in range(PACK):
             product(first[:, t, :], 0, t)
-        y = sb.tile([P, PACK, QB], F32, name="y_first")
-        nc.scalar.copy(out=y[:], in_=first[:])
-        nc.sync.dma_start(out=out_rows[:, :, 0:QB], in_=y[:])
+        y_first = sb.tile([P, PACK, QB], F32, name="y_first")
+        nc.scalar.copy(out=y_first[:], in_=first[:])
+        nc.sync.dma_start(out=out_rows[:, :, 0:QB], in_=y_first[:])
         nc.scalar.copy(out=o_grouped[:, 0:QB, :], in_=first[:].rearrange("p t q -> p q t"))
         for g in range(2):
             acc = ps.tile([P, 2, QB], F32, name=f"last{g}")
             for s in range(2):
                 product(acc[:, s, :], 1, 2 * g + s)
             nc.vector.tensor_copy(out=o_grouped[:, QB:Q, 2 * g : 2 * g + 2], in_=acc[:].rearrange("p s q -> p q s"))
-            y = sb.tile([P, 2, QB], F32, name=f"y_last{g}")
-            nc.scalar.copy(out=y[:], in_=acc[:])
-            nc.sync.dma_start(out=out_rows[:, 2 * g : 2 * g + 2, QB:Q], in_=y[:])
+            y_last = sb.tile([P, 2, QB], F32, name=f"y_last{g}")
+            nc.scalar.copy(out=y_last[:], in_=acc[:])
+            nc.sync.dma_start(out=out_rows[:, 2 * g : 2 * g + 2, QB:Q], in_=y_last[:])
+
         for b in range(BLOCKS):
             cols = slice(QB * b, QB * (b + 1))
             nc.vector.quantize_mx(
                 out=o_codes[:, cols].bitcast(FP8X4), scales=o_plane[:, cols],
-                in_=o_grouped[:, cols, :].rearrange("p c t -> p (c t)"),
+                in_=o_grouped[:, cols, :].rearrange("p q t -> p (q t)"),
             )
-        nc.sync.dma_start(out=out_1[0].rearrange("p c t -> p (c t)").bitcast(I32), in_=o_codes[:])
+        nc.sync.dma_start(out=out_1[0].rearrange("p q t -> p (q t)").bitcast(I32), in_=o_codes[:])
         for j in range(4):
             queue = nc.scalar if j % 2 == 0 else nc.sync
-            queue.dma_start(out=out_2[0, j:16:4, :].bitcast(I32), in_=o_plane[j:P:32, :].bitcast(I32))
+            queue.dma_start(
+                out=out_2[0, j:SCALE_ROWS:4, :].bitcast(I32), in_=o_plane[j:P:QUADRANT, :].bitcast(I32)
+            )

@@ -26,6 +26,7 @@ SCALE_ROWS = D // 32
 ROW_STEP = P // SCALE_ROWS
 QUADRANT = 32
 HALF = SLOTS // 2
+WORD_BYTES = 4096
 V_CUTS = (0, 160, 352, 512)
 
 
@@ -53,55 +54,47 @@ def tile_attend_pqresid_pl_kernel(
         nc.sync.dma_start(fine_list[:], offs2)
         q_raw = sb.tile([P, PACK, Q], F32, name="q_raw")
         nc.sync.dma_start(out=q_raw[:], in_=query.rearrange("(p j) q -> p j q", j=PACK))
-
-        fine_at = 4 * PACK * (E - V_CUTS[1])
-        fine_sc = late.tile([P, T], U8, name="fine_sc", offset=fine_at, align_bytes=64)
+        fine_sc = sb.tile([P, T], U8, name="fine_sc", tag="fine_sc", align_bytes=64)
         nc.vector.memset(fine_sc[:].bitcast(I32), 0)
         nc.sync.dma_start(out=fine_sc[0:P:ROW_STEP, :].bitcast(I32), in_=fine_scales[0].bitcast(I32))
 
-        words_meet = 2 * T
-        zeros = words.tile([P, 16], F32, name="zeros", offset=words_meet - 32)
+        zeros = words.tile([P, 16], F32, name="zeros", offset=WORD_BYTES - 32)
         nc.vector.memset(zeros[:, 7:9], 0.0)
         ones = sb.tile([P, 2], F32, name="ones")
         nc.scalar.activation(out=ones[:], in_=zeros[:, 7:9], func=ACT.Exp)
-        fine_w = words.tile([P, T], U16, name="fine_w", offset=0)
-        nc.sync.dma_start(out=fine_w[:].bitcast(I32), in_=fine_words[0].bitcast(I32))
-        book_w = words.tile([P, C], I32, name="book_w", offset=words_meet)
+        book_w = words.tile([P, C], I32, name="book_w", offset=0)
         nc.sync.dma_start(out=book_w[:], in_=book_words[0].rearrange("p n t -> p (n t)").bitcast(I32))
+        fine_w = words.tile([P, T], U16, name="fine_w", offset=WORD_BYTES)
+        nc.sync.dma_start(out=fine_w[:].bitcast(I32), in_=fine_words[0].bitcast(I32))
 
-        key_planes = sb.tile([P, 2 * SLOTS], U8, name="key_planes", align_bytes=64)
-        nc.vector.memset(key_planes[:].bitcast(I32), 0)
+        book_plane = sb.tile([P, SLOTS], U8, name="book_plane", align_bytes=64)
+        nc.vector.memset(book_plane[:].bitcast(I32), 0)
 
-        picked = sb.tile([P, 2 * SLOTS], U8, name="picked", align_bytes=64)
-        nc.vector.tensor_copy(picked[:, 0:SLOTS], book_sc[:].indirect(book_list[:]))
-        nc.vector.tensor_copy(picked[:, SLOTS : 2 * SLOTS], fine_sc[:].indirect(fine_list[:]))
-        for j in range(4):
-            nc.sync.dma_start(
-                out=key_planes[j:P:QUADRANT, :].bitcast(I32),
-                in_=picked[ROW_STEP * j : P : QUADRANT, :].bitcast(I32),
-            )
+        def move_rows(plane, picked, first):
+            for j in range(first, 4):
+                nc.sync.dma_start(
+                    out=plane[j:P:QUADRANT, :].bitcast(I32), in_=picked[ROW_STEP * j : P : QUADRANT, :].bitcast(I32)
+                )
 
-        vals_rows = vals.rearrange("(p j) e -> p j e", j=PACK)
-        v_first = late.tile([P, PACK, V_CUTS[1]], F32, name="v_first", offset=fine_at + T - 64, align_bytes=64)
-        nc.sync.dma_start(out=v_first[:], in_=vals_rows[:, :, 0 : V_CUTS[1]])
-        size_col = late.tile([P, PACK], F32, name="size_col", offset=fine_at + T // 2)
-        nc.sync.dma_start(out=size_col[:], in_=size.rearrange("o (p t) -> p (o t)", t=PACK))
-        v_rest = late.tile([P, PACK * (E - V_CUTS[1])], F32, name="v_rest", offset=64, align_bytes=64)
-        v_raw = [v_first[:]]
-        for lo, hi in zip(V_CUTS[1:-1], V_CUTS[2:]):
-            at = PACK * (E - hi)
-            piece = v_rest[:, at : at + PACK * (hi - lo)].rearrange("p (j e) -> p j e", j=PACK)
-            nc.sync.dma_start(out=piece, in_=vals_rows[:, :, lo:hi])
-            v_raw.append(piece)
+        book_picked = sb.tile([P, SLOTS], U8, name="book_picked", align_bytes=64)
+        nc.vector.tensor_copy(book_picked[:], book_sc[:].indirect(book_list[:]))
+        move_rows(book_plane, book_picked, 0)
+        fine_picked = sb.tile([P, SLOTS], U8, name="fine_picked", align_bytes=64)
+        nc.vector.tensor_copy(fine_picked[:], fine_sc[:].indirect(fine_list[:]))
 
         q_codes = [
-            late.tile([P, QB], U32, name="q_codes0", offset=fine_at + T // 4, align_bytes=64),
-            words.tile([P, QB], U32, name="q_codes1", offset=0, align_bytes=64),
+            sb.tile([P, QB], U32, name="q_codes0", tag="fine_sc", align_bytes=64),
+            sb.tile([P, QB], U32, name="q_codes1", align_bytes=64),
+        ]
+        first_at = 4 * SLOTS - 64
+        q_grouped = [
+            sb.tile([P, QB, PACK], BF16, name="q_grouped0", tag="grouped0", align_bytes=64),
+            late.tile([P, QB, PACK], BF16, name="q_grouped1", offset=first_at, align_bytes=64),
         ]
         q_plane = [sb.tile([P, QB], U8, name=f"q_plane{b}", align_bytes=64) for b in range(BLOCKS)]
 
         def quantise_queries(b):
-            grouped = sb.tile([P, QB, PACK], BF16, name=f"q_grouped{b}", tag=f"keys{b}", align_bytes=64)
+            grouped = q_grouped[b]
             nc.scalar.copy(
                 out=grouped[:].rearrange("p (c i) j -> p c j i", i=4),
                 in_=q_raw[:, :, QB * b : QB * (b + 1)].rearrange("p j (c i) -> p c j i", i=4),
@@ -110,30 +103,64 @@ def tile_attend_pqresid_pl_kernel(
                 out=q_codes[b][:].bitcast(FP8X4), scales=q_plane[b][:], in_=grouped[:].rearrange("p q j -> p (q j)")
             )
 
+        def gather_words(keys, window, offsets):
+            for h in range(2):
+                nc.vector.tensor_copy(
+                    keys[:, h * HALF : (h + 1) * HALF],
+                    window.indirect(offsets[:, h * HALF // GROUP : (h + 1) * HALF // GROUP]),
+                )
+
         quantise_queries(0)
-        fine_keys = sb.tile([P, SLOTS], U16, name="fine_keys", tag="keys0", align_bytes=64)
-        nc.vector.tensor_copy(fine_keys[:], fine_w[:].indirect(fine_list[:]))
+        fine_plane = sb.tile([P, SLOTS], U8, name="fine_plane", tag="grouped0", align_bytes=64)
+        nc.vector.tensor_copy(fine_plane[:].bitcast(I32), fine_picked[:].bitcast(I32))
+        move_rows(fine_plane, fine_picked, 1)
         quantise_queries(1)
-        book_keys = sb.tile([P, SLOTS], U32, name="book_keys", tag="keys1", align_bytes=64)
-        for h in range(2):
-            nc.vector.tensor_copy(
-                book_keys[:, h * HALF : (h + 1) * HALF],
-                book_w[:].bitcast(U32).indirect(book_list[:, h * HALF // GROUP : (h + 1) * HALF // GROUP]),
+
+        vals_rows = vals.rearrange("(p j) e -> p j e", j=PACK)
+        v_all = late.tile([P, PACK * E], F32, name="v_all", offset=first_at + 2 * PACK * QB - 64, align_bytes=64)
+        size_col = late.tile([P, PACK], F32, name="size_col", offset=first_at + PACK * QB)
+        nc.sync.dma_start(out=size_col[:], in_=size.rearrange("o (p t) -> p (o t)", t=PACK))
+        v_raw = []
+        for lo, hi in zip(V_CUTS[:-1], V_CUTS[1:]):
+            piece = v_all[:, PACK * lo : PACK * hi].rearrange("p (j e) -> p j e", j=PACK)
+            nc.sync.dma_start(out=piece, in_=vals_rows[:, :, lo:hi])
+            v_raw.append(piece)
+
+        book_keys = late.tile([P, SLOTS], U32, name="book_keys", offset=0, align_bytes=64)
+        gather_words(book_keys, book_w[:].bitcast(U32), book_list)
+        fine_keys = words.tile([P, SLOTS], U16, name="fine_keys", offset=0, align_bytes=64)
+        gather_words(fine_keys, fine_w[:], fine_list)
+
+        halves0 = [ps.tile([P, HALF], F32, name=f"scores0{h}", tag=f"bank{h}") for h in range(2)]
+        scores1 = ps.tile([P, SLOTS], F32, name="scores1")
+        banks = [[halves0[0][:], halves0[1][:]], [scores1[:, 0:HALF], scores1[:, HALF:SLOTS]]]
+
+        def book_pass(b, h):
+            cols = slice(h * HALF, (h + 1) * HALF)
+            nc.tensor.matmul_mx(
+                out=banks[b][h], lhsT=q_codes[b][:].bitcast(FP8X4), lhsT_scale=q_plane[b][:],
+                rhs=book_keys[:, cols].bitcast(FP8X4), rhs_scale=book_plane[:, cols],
+                start=b == 0 or h == 0, stop=False,
             )
 
-        scores = [ps.tile([P, SLOTS], F32, name=f"scores{b}") for b in range(BLOCKS)]
-        for b in range(BLOCKS):
-            nc.tensor.matmul_mx(
-                out=scores[b][:], lhsT=q_codes[b][:].bitcast(FP8X4), lhsT_scale=q_plane[b][:],
-                rhs=fine_keys[:].bitcast(FP4X4), rhs_scale=key_planes[:, SLOTS : 2 * SLOTS], start=True, stop=False,
-            )
-        for b in range(BLOCKS):
-            for h in range(2):
-                cols = slice(h * HALF, (h + 1) * HALF)
+        def fine_passes(h):
+            for c in range(2):
+                cols = slice(h * HALF + c * QB, h * HALF + (c + 1) * QB)
                 nc.tensor.matmul_mx(
-                    out=scores[b][:, cols], lhsT=q_codes[b][:].bitcast(FP8X4), lhsT_scale=q_plane[b][:],
-                    rhs=book_keys[:, cols].bitcast(FP8X4), rhs_scale=key_planes[:, cols], start=False, stop=h == 1,
+                    out=banks[0][h][:, c * QB : (c + 1) * QB], lhsT=q_codes[0][:].bitcast(FP8X4),
+                    lhsT_scale=q_plane[0][:], rhs=fine_keys[:, cols].bitcast(FP4X4), rhs_scale=fine_plane[:, cols],
+                    start=False, stop=c == 1,
                 )
+
+        for h in range(2):
+            for b in range(BLOCKS):
+                book_pass(b, h)
+        for h in range(2):
+            fine_passes(h)
+        nc.tensor.matmul_mx(
+            out=scores1[:], lhsT=q_codes[1][:].bitcast(FP8X4), lhsT_scale=q_plane[1][:],
+            rhs=fine_keys[:].bitcast(FP4X4), rhs_scale=fine_plane[:], start=False, stop=True,
+        )
 
         size_ps = ps.tile([P, PACK, P], F32, name="size_ps")
         for t in range(PACK):
@@ -152,18 +179,26 @@ def tile_attend_pqresid_pl_kernel(
             sb.tile([P, 2, P, 2], F32, name="probs0", align_bytes=64),
             sb.tile([P, 2, P, 2], F32, name="probs1", tag="probs1", align_bytes=64),
         ]
-        neg_max, row_sum = [], []
-        for b in range(BLOCKS):
-            nm = sb.tile([P, 1], F32, name=f"neg_max{b}")
-            nc.vector.tensor_reduce(out=nm[:], in_=scores[b][:], axis=mybir.AxisListType.X, op=ALU.max, negate=True)
-            neg_max.append(nm)
-        for b in range(BLOCKS):
-            rs = sb.tile([P, 1], F32, name=f"row_sum{b}")
-            nc.scalar.activation(
-                out=probs[b][:], in_=scores[b][:].rearrange("q (p u e) -> q u p e", u=2, e=2),
-                func=ACT.Exp, bias=neg_max[b][:], scale=1.0, accum_out=rs[:],
+        neg_scores = sb.tile([P, 2, P, 2], F32, name="neg_scores", align_bytes=64)
+        so_far = None
+        for h in range(2):
+            running = sb.tile([P, 1], F32, name=f"neg_max0{h}", tag=f"running{h}")
+            nc.vector.tensor_scalar(
+                out=neg_scores[:, :, h * P // 2 : (h + 1) * P // 2, :],
+                in0=banks[0][h].rearrange("q (p u e) -> q u p e", u=2, e=2),
+                scalar1=-1.0, scalar2=so_far, op0=ALU.mult, op1=ALU.min, accum_out=running[:],
             )
-            row_sum.append(rs)
+            so_far = running[:]
+        neg_max1 = sb.tile([P, 1], F32, name="neg_max1", tag="running0")
+        nc.vector.tensor_reduce(out=neg_max1[:], in_=scores1[:], axis=mybir.AxisListType.X, op=ALU.max, negate=True)
+        row_sum = [sb.tile([P, 1], F32, name=f"row_sum{b}") for b in range(BLOCKS)]
+        nc.scalar.activation(
+            out=probs[0][:], in_=neg_scores[:], func=ACT.Exp, bias=so_far, scale=-1.0, accum_out=row_sum[0][:]
+        )
+        nc.scalar.activation(
+            out=probs[1][:], in_=scores1[:].rearrange("q (p u e) -> q u p e", u=2, e=2),
+            func=ACT.Exp, bias=neg_max1[:], scale=1.0, accum_out=row_sum[1][:],
+        )
 
         nc.scalar.copy(
             out=v_grouped[:, :, V_CUTS[2] // PACK :, :].rearrange("p t m j -> p m j t"),
@@ -173,8 +208,7 @@ def tile_attend_pqresid_pl_kernel(
         inv = [sb.tile([P, 1], F32, name=f"inv_sum{b}") for b in range(BLOCKS)]
         turned = [ps.tile([P, 2, QB], F32, name=f"turned{b}") for b in range(BLOCKS)]
         w_grouped = [sb.tile([P, QB * PACK], BF16, name=f"w_grouped{b}", align_bytes=64) for b in range(BLOCKS)]
-        for b in range(BLOCKS):
-            nc.vector.reciprocal(out=inv[b][:], in_=row_sum[b][:])
+        nc.vector.reciprocal(out=inv[0][:], in_=row_sum[0][:])
         for b in range(BLOCKS):
             for u in range(2):
                 w = sb.tile([P, P, 2], BF16, name=f"w{b}_{u}")
@@ -183,6 +217,8 @@ def tile_attend_pqresid_pl_kernel(
                     in1=size_ps[:, 2 * u : 2 * u + 2, :].rearrange("q e p -> q p e"),
                     op0=ALU.mult, op1=ALU.mult,
                 )
+                if (b, u) == (0, 0):
+                    nc.vector.reciprocal(out=inv[1][:], in_=row_sum[1][:])
                 nc.tensor.transpose(turned[b][:, u, :], w[:].rearrange("q p e -> q (p e)").bitcast(F32), ident[:])
             nc.scalar.copy(
                 out=w_grouped[b][:].bitcast(F32).rearrange("p (q u) -> p q u", u=2),
@@ -214,20 +250,26 @@ def tile_attend_pqresid_pl_kernel(
                 rhs=w_codes[b][:].bitcast(FP8X4), rhs_scale=w_plane[b][:], start=True, stop=True,
             )
 
-        first = ps.tile([P, PACK, QB], F32, name="first")
-        for t in range(PACK):
-            product(first[:, t, :], 0, t)
         y_first = sb.tile([P, PACK, QB], F32, name="y_first")
-        nc.scalar.copy(out=y_first[:], in_=first[:])
-        nc.sync.dma_start(out=out_rows[:, :, 0:QB], in_=y_first[:])
-        nc.scalar.copy(out=o_grouped[:, 0:QB, :], in_=first[:].rearrange("p t q -> p q t"))
         for g in range(2):
-            acc = ps.tile([P, 2, QB], F32, name=f"last{g}")
+            acc = ps.tile([P, 2, QB], F32, name=f"first{g}", tag=f"bank{g}")
             for s in range(2):
-                product(acc[:, s, :], 1, 2 * g + s)
-            nc.vector.tensor_copy(out=o_grouped[:, QB:Q, 2 * g : 2 * g + 2], in_=acc[:].rearrange("p s q -> p q s"))
+                product(acc[:, s, :], 0, 2 * g + s)
+            nc.scalar.copy(out=y_first[:, 2 * g : 2 * g + 2, :], in_=acc[:])
+        nc.sync.dma_start(out=out_rows[:, :, 0:QB], in_=y_first[:])
+        nc.vector.tensor_copy(
+            out=o_grouped[:, 0:QB, :].rearrange("p (c i) t -> p c t i", i=4),
+            in_=y_first[:].rearrange("p t (c i) -> p c t i", i=4),
+        )
+        last = [ps.tile([P, 2, QB], F32, name=f"last{g}") for g in range(2)]
+        for g in range(2):
+            for s in range(2):
+                product(last[g][:, s, :], 1, 2 * g + s)
+        nc.scalar.copy(out=o_grouped[:, QB:Q, 0:2], in_=last[0][:].rearrange("p s q -> p q s"))
+        nc.vector.tensor_copy(out=o_grouped[:, QB:Q, 2:4], in_=last[1][:].rearrange("p s q -> p q s"))
+        for g in range(2):
             y_last = sb.tile([P, 2, QB], F32, name=f"y_last{g}")
-            nc.scalar.copy(out=y_last[:], in_=acc[:])
+            nc.scalar.copy(out=y_last[:], in_=last[g][:])
             nc.sync.dma_start(out=out_rows[:, 2 * g : 2 * g + 2, QB:Q], in_=y_last[:])
 
         for b in range(BLOCKS):

@@ -25,7 +25,9 @@ GROUP = 16
 SCALE_ROWS = D // 32
 ROW_STEP = P // SCALE_ROWS
 QUADRANT = 32
+FINE_AT = P - SCALE_ROWS
 HALF = SLOTS // 2
+LAST = SLOTS - QB
 WORD_BYTES = 4096
 V_CUTS = (0, 160, 352, 512)
 
@@ -40,56 +42,49 @@ def tile_attend_pqresid_pl_kernel(
         words = ctx.enter_context(tc.tile_pool(name="words", bufs=1))
         late = ctx.enter_context(tc.tile_pool(name="late", bufs=1))
 
-        ident = sb.tile([P, P], F32, name="ident")
-        make_identity(nc, ident[:])
-
+        fine_list = sb.tile([P, SLOTS // GROUP], U16, name="fine_list")
+        nc.sync.dma_start(fine_list[:], offs2)
+        fine_sc = sb.tile([P, T], U8, name="fine_sc", align_bytes=64)
+        nc.sync.dma_start(out=fine_sc[FINE_AT:P, :].bitcast(I32), in_=fine_scales[0].bitcast(I32))
         book_list = sb.tile([P, SLOTS // GROUP], U16, name="book_list")
         nc.sync.dma_start(book_list[:], offs)
-        book_sc = sb.tile([P, C], U8, name="book_sc")
+        book_sc = sb.tile([P, C], U8, name="book_sc", align_bytes=64)
         nc.sync.dma_start(
             out=book_sc[:].bitcast(I32),
             in_=book_scales[0].bitcast(I32).unsqueeze(1).to_broadcast([SCALE_ROWS, ROW_STEP, C // 4]),
         )
-        fine_list = sb.tile([P, SLOTS // GROUP], U16, name="fine_list")
-        nc.sync.dma_start(fine_list[:], offs2)
         q_raw = sb.tile([P, PACK, Q], F32, name="q_raw")
         nc.sync.dma_start(out=q_raw[:], in_=query.rearrange("(p j) q -> p j q", j=PACK))
-        fine_sc = sb.tile([P, T], U8, name="fine_sc", tag="fine_sc", align_bytes=64)
-        nc.vector.memset(fine_sc[:].bitcast(I32), 0)
-        nc.sync.dma_start(out=fine_sc[0:P:ROW_STEP, :].bitcast(I32), in_=fine_scales[0].bitcast(I32))
+        nc.vector.memset(fine_sc[0:FINE_AT, :].bitcast(I32), 0)
 
-        zeros = words.tile([P, 16], F32, name="zeros", offset=WORD_BYTES - 32)
-        nc.vector.memset(zeros[:, 7:9], 0.0)
+        zeros = sb.tile([P, 2], F32, name="zeros")
+        nc.vector.memset(zeros[:], 0.0)
         ones = sb.tile([P, 2], F32, name="ones")
-        nc.scalar.activation(out=ones[:], in_=zeros[:, 7:9], func=ACT.Exp)
-        book_w = words.tile([P, C], I32, name="book_w", offset=0)
-        nc.sync.dma_start(out=book_w[:], in_=book_words[0].rearrange("p n t -> p (n t)").bitcast(I32))
-        fine_w = words.tile([P, T], U16, name="fine_w", offset=WORD_BYTES)
+        nc.scalar.activation(out=ones[:], in_=zeros[:], func=ACT.Exp)
+        fine_w = words.tile([P, T], U16, name="fine_w", offset=0)
         nc.sync.dma_start(out=fine_w[:].bitcast(I32), in_=fine_words[0].bitcast(I32))
+        book_w = words.tile([P, C], I32, name="book_w", offset=WORD_BYTES)
+        nc.sync.dma_start(out=book_w[:], in_=book_words[0].rearrange("p n t -> p (n t)").bitcast(I32))
 
-        book_plane = sb.tile([P, SLOTS], U8, name="book_plane", align_bytes=64)
-        nc.vector.memset(book_plane[:].bitcast(I32), 0)
+        ident = sb.tile([P, P], F32, name="ident")
+        make_identity(nc, ident[:])
 
-        def move_rows(plane, picked, first):
-            for j in range(first, 4):
-                nc.sync.dma_start(
-                    out=plane[j:P:QUADRANT, :].bitcast(I32), in_=picked[ROW_STEP * j : P : QUADRANT, :].bitcast(I32)
-                )
+        fine_plane = sb.tile([P, SLOTS], U8, name="fine_plane", align_bytes=64)
+        nc.vector.memset(fine_plane[:].bitcast(I32), 0)
 
-        book_picked = sb.tile([P, SLOTS], U8, name="book_picked", align_bytes=64)
-        nc.vector.tensor_copy(book_picked[:], book_sc[:].indirect(book_list[:]))
-        move_rows(book_plane, book_picked, 0)
         fine_picked = sb.tile([P, SLOTS], U8, name="fine_picked", align_bytes=64)
         nc.vector.tensor_copy(fine_picked[:], fine_sc[:].indirect(fine_list[:]))
+        for j in range(4):
+            nc.sync.dma_start(
+                out=fine_plane[j:P:QUADRANT, :].bitcast(I32), in_=fine_picked[FINE_AT + j : P : 4, :].bitcast(I32)
+            )
+        book_picked = sb.tile([P, SLOTS], U8, name="book_picked", align_bytes=64)
+        nc.vector.tensor_copy(book_picked[:], book_sc[:].indirect(book_list[:]))
 
-        q_codes = [
-            sb.tile([P, QB], U32, name="q_codes0", tag="fine_sc", align_bytes=64),
-            sb.tile([P, QB], U32, name="q_codes1", align_bytes=64),
-        ]
-        first_at = 4 * SLOTS - 64
+        q_codes = [sb.tile([P, QB], U32, name=f"q_codes{b}", align_bytes=64) for b in range(BLOCKS)]
         q_grouped = [
-            sb.tile([P, QB, PACK], BF16, name="q_grouped0", tag="grouped0", align_bytes=64),
-            late.tile([P, QB, PACK], BF16, name="q_grouped1", offset=first_at, align_bytes=64),
+            late.tile([P, QB, PACK], BF16, name="q_grouped0", offset=0, align_bytes=64),
+            sb.tile([P, QB, PACK], BF16, name="q_grouped1", align_bytes=64),
         ]
         q_plane = [sb.tile([P, QB], U8, name=f"q_plane{b}", align_bytes=64) for b in range(BLOCKS)]
 
@@ -103,22 +98,23 @@ def tile_attend_pqresid_pl_kernel(
                 out=q_codes[b][:].bitcast(FP8X4), scales=q_plane[b][:], in_=grouped[:].rearrange("p q j -> p (q j)")
             )
 
-        def gather_words(keys, window, offsets):
-            for h in range(2):
-                nc.vector.tensor_copy(
-                    keys[:, h * HALF : (h + 1) * HALF],
-                    window.indirect(offsets[:, h * HALF // GROUP : (h + 1) * HALF // GROUP]),
-                )
+        def gather_words(keys, window, offsets, cuts):
+            for lo, hi in zip(cuts[:-1], cuts[1:]):
+                nc.vector.tensor_copy(keys[:, lo:hi], window.indirect(offsets[:, lo // GROUP : hi // GROUP]))
 
-        quantise_queries(0)
-        fine_plane = sb.tile([P, SLOTS], U8, name="fine_plane", tag="grouped0", align_bytes=64)
-        nc.vector.tensor_copy(fine_plane[:].bitcast(I32), fine_picked[:].bitcast(I32))
-        move_rows(fine_plane, fine_picked, 1)
-        quantise_queries(1)
+        book_plane = sb.tile([P, SLOTS], U8, name="book_plane", align_bytes=64)
+        nc.vector.tensor_copy(book_plane[:].bitcast(I32), book_picked[:].bitcast(I32))
+        for j in range(1, 4):
+            nc.sync.dma_start(
+                out=book_plane[j:P:QUADRANT, :].bitcast(I32),
+                in_=book_picked[ROW_STEP * j : P : QUADRANT, :].bitcast(I32),
+            )
+        for b in range(BLOCKS):
+            quantise_queries(b)
 
         vals_rows = vals.rearrange("(p j) e -> p j e", j=PACK)
-        v_all = late.tile([P, PACK * E], F32, name="v_all", offset=first_at + 2 * PACK * QB - 64, align_bytes=64)
-        size_col = late.tile([P, PACK], F32, name="size_col", offset=first_at + PACK * QB)
+        v_all = late.tile([P, PACK * E], F32, name="v_all", offset=2 * PACK * QB - 64, align_bytes=64)
+        size_col = late.tile([P, PACK], F32, name="size_col", offset=0)
         nc.sync.dma_start(out=size_col[:], in_=size.rearrange("o (p t) -> p (o t)", t=PACK))
         v_raw = []
         for lo, hi in zip(V_CUTS[:-1], V_CUTS[1:]):
@@ -126,41 +122,31 @@ def tile_attend_pqresid_pl_kernel(
             nc.sync.dma_start(out=piece, in_=vals_rows[:, :, lo:hi])
             v_raw.append(piece)
 
-        book_keys = late.tile([P, SLOTS], U32, name="book_keys", offset=0, align_bytes=64)
-        gather_words(book_keys, book_w[:].bitcast(U32), book_list)
-        fine_keys = words.tile([P, SLOTS], U16, name="fine_keys", offset=0, align_bytes=64)
-        gather_words(fine_keys, fine_w[:], fine_list)
+        fine_keys = sb.tile([P, SLOTS], U16, name="fine_keys", align_bytes=64)
+        gather_words(fine_keys, fine_w[:], fine_list, (0, HALF, SLOTS))
+        book_keys = sb.tile([P, SLOTS], U32, name="book_keys", align_bytes=64)
+        gather_words(book_keys, book_w[:].bitcast(U32), book_list, (0, HALF, LAST, SLOTS))
 
-        halves0 = [ps.tile([P, HALF], F32, name=f"scores0{h}", tag=f"bank{h}") for h in range(2)]
+        head0 = ps.tile([P, LAST], F32, name="head0", tag="bank0")
+        tail0 = ps.tile([P, SLOTS - LAST], F32, name="tail0", tag="bank1")
         scores1 = ps.tile([P, SLOTS], F32, name="scores1")
-        banks = [[halves0[0][:], halves0[1][:]], [scores1[:, 0:HALF], scores1[:, HALF:SLOTS]]]
 
-        def book_pass(b, h):
-            cols = slice(h * HALF, (h + 1) * HALF)
+        def score_pass(out, b, keys, plane, dtype, lo, hi, start, stop):
             nc.tensor.matmul_mx(
-                out=banks[b][h], lhsT=q_codes[b][:].bitcast(FP8X4), lhsT_scale=q_plane[b][:],
-                rhs=book_keys[:, cols].bitcast(FP8X4), rhs_scale=book_plane[:, cols],
-                start=b == 0 or h == 0, stop=False,
+                out=out, lhsT=q_codes[b][:].bitcast(FP8X4), lhsT_scale=q_plane[b][:],
+                rhs=keys[:, lo:hi].bitcast(dtype), rhs_scale=plane[:, lo:hi], start=start, stop=stop,
             )
 
-        def fine_passes(h):
-            for c in range(2):
-                cols = slice(h * HALF + c * QB, h * HALF + (c + 1) * QB)
-                nc.tensor.matmul_mx(
-                    out=banks[0][h][:, c * QB : (c + 1) * QB], lhsT=q_codes[0][:].bitcast(FP8X4),
-                    lhsT_scale=q_plane[0][:], rhs=fine_keys[:, cols].bitcast(FP4X4), rhs_scale=fine_plane[:, cols],
-                    start=False, stop=c == 1,
-                )
-
-        for h in range(2):
-            for b in range(BLOCKS):
-                book_pass(b, h)
-        for h in range(2):
-            fine_passes(h)
-        nc.tensor.matmul_mx(
-            out=scores1[:], lhsT=q_codes[1][:].bitcast(FP8X4), lhsT_scale=q_plane[1][:],
-            rhs=fine_keys[:].bitcast(FP4X4), rhs_scale=fine_plane[:], start=False, stop=True,
-        )
+        score_pass(head0[:, 0:HALF], 0, fine_keys, fine_plane, FP4X4, 0, HALF, True, False)
+        score_pass(scores1[:, 0:HALF], 1, fine_keys, fine_plane, FP4X4, 0, HALF, True, False)
+        score_pass(head0[:, HALF:LAST], 0, fine_keys, fine_plane, FP4X4, HALF, LAST, False, False)
+        score_pass(tail0[:], 0, fine_keys, fine_plane, FP4X4, LAST, SLOTS, True, False)
+        score_pass(scores1[:, HALF:SLOTS], 1, fine_keys, fine_plane, FP4X4, HALF, SLOTS, False, False)
+        score_pass(head0[:, 0:HALF], 0, book_keys, book_plane, FP8X4, 0, HALF, False, False)
+        score_pass(scores1[:, 0:HALF], 1, book_keys, book_plane, FP8X4, 0, HALF, False, False)
+        score_pass(head0[:, HALF:LAST], 0, book_keys, book_plane, FP8X4, HALF, LAST, False, True)
+        score_pass(tail0[:], 0, book_keys, book_plane, FP8X4, LAST, SLOTS, False, True)
+        score_pass(scores1[:, HALF:SLOTS], 1, book_keys, book_plane, FP8X4, HALF, SLOTS, False, True)
 
         size_ps = ps.tile([P, PACK, P], F32, name="size_ps")
         for t in range(PACK):
@@ -181,11 +167,11 @@ def tile_attend_pqresid_pl_kernel(
         ]
         neg_scores = sb.tile([P, 2, P, 2], F32, name="neg_scores", align_bytes=64)
         so_far = None
-        for h in range(2):
+        for h, (bank, lo, hi) in enumerate(((head0, 0, LAST), (tail0, LAST, SLOTS))):
             running = sb.tile([P, 1], F32, name=f"neg_max0{h}", tag=f"running{h}")
             nc.vector.tensor_scalar(
-                out=neg_scores[:, :, h * P // 2 : (h + 1) * P // 2, :],
-                in0=banks[0][h].rearrange("q (p u e) -> q u p e", u=2, e=2),
+                out=neg_scores[:, :, lo // PACK : hi // PACK, :],
+                in0=bank[:].rearrange("q (p u e) -> q u p e", u=2, e=2),
                 scalar1=-1.0, scalar2=so_far, op0=ALU.mult, op1=ALU.min, accum_out=running[:],
             )
             so_far = running[:]
@@ -265,11 +251,11 @@ def tile_attend_pqresid_pl_kernel(
         for g in range(2):
             for s in range(2):
                 product(last[g][:, s, :], 1, 2 * g + s)
-        nc.scalar.copy(out=o_grouped[:, QB:Q, 0:2], in_=last[0][:].rearrange("p s q -> p q s"))
-        nc.vector.tensor_copy(out=o_grouped[:, QB:Q, 2:4], in_=last[1][:].rearrange("p s q -> p q s"))
-        for g in range(2):
+        nc.vector.tensor_copy(out=o_grouped[:, QB:Q, 0:2], in_=last[0][:].rearrange("p s q -> p q s"))
+        nc.scalar.copy(out=o_grouped[:, QB:Q, 2:4], in_=last[1][:].rearrange("p s q -> p q s"))
+        for g, copy in enumerate((nc.vector.tensor_copy, nc.scalar.copy)):
             y_last = sb.tile([P, 2, QB], F32, name=f"y_last{g}")
-            nc.scalar.copy(out=y_last[:], in_=last[g][:])
+            copy(out=y_last[:], in_=last[g][:])
             nc.sync.dma_start(out=out_rows[:, 2 * g : 2 * g + 2, QB:Q], in_=y_last[:])
 
         for b in range(BLOCKS):

@@ -57,10 +57,10 @@ def tile_attend_pqresid_pl_kernel(
         nc.sync.dma_start(out=q_raw[:], in_=query.rearrange("(p j) q -> p j q", j=PACK))
         nc.vector.memset(fine_sc[0:FINE_AT, :].bitcast(I32), 0)
 
-        zeros = sb.tile([P, 2], F32, name="zeros")
-        nc.vector.memset(zeros[:], 0.0)
-        ones = sb.tile([P, 2], F32, name="ones")
-        nc.scalar.activation(out=ones[:], in_=zeros[:], func=ACT.Exp)
+        zero = sb.tile([P, 1], F32, name="zero")
+        nc.vector.memset(zero[:], 0.0)
+        one = sb.tile([P, 1], F32, name="one", tag="book_plane", align_bytes=64)
+        nc.scalar.activation(out=one[:], in_=zero[:], func=ACT.Exp)
         fine_w = words.tile([P, T], U16, name="fine_w", offset=0)
         nc.sync.dma_start(out=fine_w[:].bitcast(I32), in_=fine_words[0].bitcast(I32))
         book_w = words.tile([P, C], I32, name="book_w", offset=WORD_BYTES)
@@ -83,16 +83,17 @@ def tile_attend_pqresid_pl_kernel(
 
         q_codes = [sb.tile([P, QB], U32, name=f"q_codes{b}", align_bytes=64) for b in range(BLOCKS)]
         q_grouped = [
-            late.tile([P, QB, PACK], BF16, name="q_grouped0", offset=0, align_bytes=64),
-            sb.tile([P, QB, PACK], BF16, name="q_grouped1", align_bytes=64),
+            sb.tile([P, QB, PACK], BF16, name="q_grouped0", align_bytes=64),
+            late.tile([P, QB, PACK], BF16, name="q_grouped1", offset=0, align_bytes=64),
         ]
         q_plane = [sb.tile([P, QB], U8, name=f"q_plane{b}", align_bytes=64) for b in range(BLOCKS)]
 
-        def quantise_queries(b):
+        def quantise_queries(b, scale):
             grouped = q_grouped[b]
-            nc.scalar.copy(
+            nc.scalar.activation(
                 out=grouped[:].rearrange("p (c i) j -> p c j i", i=4),
                 in_=q_raw[:, :, QB * b : QB * (b + 1)].rearrange("p j (c i) -> p c j i", i=4),
+                func=ACT.Copy, scale=scale,
             )
             nc.vector.quantize_mx(
                 out=q_codes[b][:].bitcast(FP8X4), scales=q_plane[b][:], in_=grouped[:].rearrange("p q j -> p (q j)")
@@ -102,15 +103,15 @@ def tile_attend_pqresid_pl_kernel(
             for lo, hi in zip(cuts[:-1], cuts[1:]):
                 nc.vector.tensor_copy(keys[:, lo:hi], window.indirect(offsets[:, lo // GROUP : hi // GROUP]))
 
-        book_plane = sb.tile([P, SLOTS], U8, name="book_plane", align_bytes=64)
+        quantise_queries(0, one[:])
+        book_plane = sb.tile([P, SLOTS], U8, name="book_plane", tag="book_plane", align_bytes=64)
         nc.vector.tensor_copy(book_plane[:].bitcast(I32), book_picked[:].bitcast(I32))
         for j in range(1, 4):
             nc.sync.dma_start(
                 out=book_plane[j:P:QUADRANT, :].bitcast(I32),
                 in_=book_picked[ROW_STEP * j : P : QUADRANT, :].bitcast(I32),
             )
-        for b in range(BLOCKS):
-            quantise_queries(b)
+        quantise_queries(1, 1.0)
 
         vals_rows = vals.rearrange("(p j) e -> p j e", j=PACK)
         v_all = late.tile([P, PACK * E], F32, name="v_all", offset=2 * PACK * QB - 64, align_bytes=64)
@@ -127,8 +128,8 @@ def tile_attend_pqresid_pl_kernel(
         book_keys = sb.tile([P, SLOTS], U32, name="book_keys", align_bytes=64)
         gather_words(book_keys, book_w[:].bitcast(U32), book_list, (0, HALF, LAST, SLOTS))
 
-        head0 = ps.tile([P, LAST], F32, name="head0", tag="bank0")
-        tail0 = ps.tile([P, SLOTS - LAST], F32, name="tail0", tag="bank1")
+        head0 = ps.tile([P, HALF], F32, name="head0", tag="bank0")
+        tail0 = ps.tile([P, HALF], F32, name="tail0", tag="bank1")
         scores1 = ps.tile([P, SLOTS], F32, name="scores1")
 
         def score_pass(out, b, keys, plane, dtype, lo, hi, start, stop):
@@ -137,16 +138,13 @@ def tile_attend_pqresid_pl_kernel(
                 rhs=keys[:, lo:hi].bitcast(dtype), rhs_scale=plane[:, lo:hi], start=start, stop=stop,
             )
 
-        score_pass(head0[:, 0:HALF], 0, fine_keys, fine_plane, FP4X4, 0, HALF, True, False)
-        score_pass(scores1[:, 0:HALF], 1, fine_keys, fine_plane, FP4X4, 0, HALF, True, False)
-        score_pass(head0[:, HALF:LAST], 0, fine_keys, fine_plane, FP4X4, HALF, LAST, False, False)
-        score_pass(tail0[:], 0, fine_keys, fine_plane, FP4X4, LAST, SLOTS, True, False)
-        score_pass(scores1[:, HALF:SLOTS], 1, fine_keys, fine_plane, FP4X4, HALF, SLOTS, False, False)
-        score_pass(head0[:, 0:HALF], 0, book_keys, book_plane, FP8X4, 0, HALF, False, False)
-        score_pass(scores1[:, 0:HALF], 1, book_keys, book_plane, FP8X4, 0, HALF, False, False)
-        score_pass(head0[:, HALF:LAST], 0, book_keys, book_plane, FP8X4, HALF, LAST, False, True)
-        score_pass(tail0[:], 0, book_keys, book_plane, FP8X4, LAST, SLOTS, False, True)
-        score_pass(scores1[:, HALF:SLOTS], 1, book_keys, book_plane, FP8X4, HALF, SLOTS, False, True)
+        score_pass(head0[:], 0, fine_keys, fine_plane, FP4X4, 0, HALF, True, False)
+        score_pass(tail0[:], 0, fine_keys, fine_plane, FP4X4, HALF, SLOTS, True, False)
+        score_pass(scores1[:], 1, fine_keys, fine_plane, FP4X4, 0, SLOTS, True, False)
+        score_pass(head0[:], 0, book_keys, book_plane, FP8X4, 0, HALF, False, True)
+        score_pass(tail0[:, 0:QB], 0, book_keys, book_plane, FP8X4, HALF, LAST, False, False)
+        score_pass(tail0[:, QB:HALF], 0, book_keys, book_plane, FP8X4, LAST, SLOTS, False, True)
+        score_pass(scores1[:], 1, book_keys, book_plane, FP8X4, 0, SLOTS, False, True)
 
         size_ps = ps.tile([P, PACK, P], F32, name="size_ps")
         for t in range(PACK):
@@ -158,7 +156,7 @@ def tile_attend_pqresid_pl_kernel(
             nc.gpsimd.tensor_scalar(
                 out=v_grouped[:, :, lo // PACK : hi // PACK, :],
                 in0=v_raw[piece].rearrange("p j (m t) -> p t m j", t=PACK),
-                scalar1=ones[:, piece : piece + 1], scalar2=0.0, op0=ALU.mult, op1=ALU.add,
+                scalar1=1.0, scalar2=0.0, op0=ALU.mult, op1=ALU.add,
             )
 
         probs = [
@@ -167,7 +165,7 @@ def tile_attend_pqresid_pl_kernel(
         ]
         neg_scores = sb.tile([P, 2, P, 2], F32, name="neg_scores", align_bytes=64)
         so_far = None
-        for h, (bank, lo, hi) in enumerate(((head0, 0, LAST), (tail0, LAST, SLOTS))):
+        for h, (bank, lo, hi) in enumerate(((head0, 0, HALF), (tail0, HALF, SLOTS))):
             running = sb.tile([P, 1], F32, name=f"neg_max0{h}", tag=f"running{h}")
             nc.vector.tensor_scalar(
                 out=neg_scores[:, :, lo // PACK : hi // PACK, :],

@@ -45,7 +45,7 @@ def tile_attend_pqresid_pl_kernel(
         fine_list = sb.tile([P, SLOTS // GROUP], U16, name="fine_list")
         nc.sync.dma_start(fine_list[:], offs2)
         fine_sc = sb.tile([P, T], U8, name="fine_sc", align_bytes=64)
-        nc.sync.dma_start(out=fine_sc[FINE_AT:P, :].bitcast(I32), in_=fine_scales[0].bitcast(I32))
+        nc.scalar.dma_start(out=fine_sc[FINE_AT:P, :].bitcast(I32), in_=fine_scales[0].bitcast(I32))
         book_list = sb.tile([P, SLOTS // GROUP], U16, name="book_list")
         nc.sync.dma_start(book_list[:], offs)
         book_sc = sb.tile([P, C], U8, name="book_sc", align_bytes=64)
@@ -128,23 +128,21 @@ def tile_attend_pqresid_pl_kernel(
         book_keys = sb.tile([P, SLOTS], U32, name="book_keys", align_bytes=64)
         gather_words(book_keys, book_w[:].bitcast(U32), book_list, (0, HALF, LAST, SLOTS))
 
-        head0 = ps.tile([P, HALF], F32, name="head0", tag="bank0")
-        tail0 = ps.tile([P, HALF], F32, name="tail0", tag="bank1")
-        scores1 = ps.tile([P, SLOTS], F32, name="scores1")
+        scores = [ps.tile([P, SLOTS], F32, name=f"scores{b}", tag=f"bank{b}") for b in range(BLOCKS)]
 
-        def score_pass(out, b, keys, plane, dtype, lo, hi, start, stop):
+        def score_pass(b, keys, plane, dtype, lo, hi, start, stop):
             nc.tensor.matmul_mx(
-                out=out, lhsT=q_codes[b][:].bitcast(FP8X4), lhsT_scale=q_plane[b][:],
+                out=scores[b][:, lo:hi], lhsT=q_codes[b][:].bitcast(FP8X4), lhsT_scale=q_plane[b][:],
                 rhs=keys[:, lo:hi].bitcast(dtype), rhs_scale=plane[:, lo:hi], start=start, stop=stop,
             )
 
-        score_pass(head0[:], 0, fine_keys, fine_plane, FP4X4, 0, HALF, True, False)
-        score_pass(tail0[:], 0, fine_keys, fine_plane, FP4X4, HALF, SLOTS, True, False)
-        score_pass(scores1[:], 1, fine_keys, fine_plane, FP4X4, 0, SLOTS, True, False)
-        score_pass(head0[:], 0, book_keys, book_plane, FP8X4, 0, HALF, False, True)
-        score_pass(tail0[:, 0:QB], 0, book_keys, book_plane, FP8X4, HALF, LAST, False, False)
-        score_pass(tail0[:, QB:HALF], 0, book_keys, book_plane, FP8X4, LAST, SLOTS, False, True)
-        score_pass(scores1[:], 1, book_keys, book_plane, FP8X4, 0, SLOTS, False, True)
+        score_pass(0, fine_keys, fine_plane, FP4X4, 0, HALF, True, False)
+        score_pass(0, fine_keys, fine_plane, FP4X4, HALF, SLOTS, False, False)
+        score_pass(1, fine_keys, fine_plane, FP4X4, 0, SLOTS, True, False)
+        score_pass(0, book_keys, book_plane, FP8X4, 0, HALF, False, False)
+        score_pass(0, book_keys, book_plane, FP8X4, HALF, LAST, False, False)
+        score_pass(0, book_keys, book_plane, FP8X4, LAST, SLOTS, False, True)
+        score_pass(1, book_keys, book_plane, FP8X4, 0, SLOTS, False, True)
 
         size_ps = ps.tile([P, PACK, P], F32, name="size_ps")
         for t in range(PACK):
@@ -161,28 +159,18 @@ def tile_attend_pqresid_pl_kernel(
 
         probs = [
             sb.tile([P, 2, P, 2], F32, name="probs0", align_bytes=64),
-            sb.tile([P, 2, P, 2], F32, name="probs1", tag="probs1", align_bytes=64),
+            sb.tile([P, 2, P, 2], F32, name="probs1", align_bytes=64),
         ]
-        neg_scores = sb.tile([P, 2, P, 2], F32, name="neg_scores", align_bytes=64)
-        so_far = None
-        for h, (bank, lo, hi) in enumerate(((head0, 0, HALF), (tail0, HALF, SLOTS))):
-            running = sb.tile([P, 1], F32, name=f"neg_max0{h}", tag=f"running{h}")
-            nc.vector.tensor_scalar(
-                out=neg_scores[:, :, lo // PACK : hi // PACK, :],
-                in0=bank[:].rearrange("q (p u e) -> q u p e", u=2, e=2),
-                scalar1=-1.0, scalar2=so_far, op0=ALU.mult, op1=ALU.min, accum_out=running[:],
-            )
-            so_far = running[:]
-        neg_max1 = sb.tile([P, 1], F32, name="neg_max1", tag="running0")
-        nc.vector.tensor_reduce(out=neg_max1[:], in_=scores1[:], axis=mybir.AxisListType.X, op=ALU.max, negate=True)
         row_sum = [sb.tile([P, 1], F32, name=f"row_sum{b}") for b in range(BLOCKS)]
-        nc.scalar.activation(
-            out=probs[0][:], in_=neg_scores[:], func=ACT.Exp, bias=so_far, scale=-1.0, accum_out=row_sum[0][:]
-        )
-        nc.scalar.activation(
-            out=probs[1][:], in_=scores1[:].rearrange("q (p u e) -> q u p e", u=2, e=2),
-            func=ACT.Exp, bias=neg_max1[:], scale=1.0, accum_out=row_sum[1][:],
-        )
+        for b in range(BLOCKS):
+            neg_max = sb.tile([P, 1], F32, name=f"neg_max{b}")
+            nc.vector.tensor_reduce(
+                out=neg_max[:], in_=scores[b][:], axis=mybir.AxisListType.X, op=ALU.max, negate=True
+            )
+            nc.scalar.activation(
+                out=probs[b][:], in_=scores[b][:].rearrange("q (p u e) -> q u p e", u=2, e=2),
+                func=ACT.Exp, bias=neg_max[:], scale=1.0, accum_out=row_sum[b][:],
+            )
 
         nc.scalar.copy(
             out=v_grouped[:, :, V_CUTS[2] // PACK :, :].rearrange("p t m j -> p m j t"),
@@ -195,7 +183,7 @@ def tile_attend_pqresid_pl_kernel(
         nc.vector.reciprocal(out=inv[0][:], in_=row_sum[0][:])
         for b in range(BLOCKS):
             for u in range(2):
-                w = sb.tile([P, P, 2], BF16, name=f"w{b}_{u}")
+                w = sb.tile([P, P, 2], BF16, name=f"w{b}_{u}", tag=f"w{b}_{u}", align_bytes=64)
                 nc.vector.scalar_tensor_tensor(
                     out=w[:], in0=probs[b][:, u, :, :], scalar=inv[b][:],
                     in1=size_ps[:, 2 * u : 2 * u + 2, :].rearrange("q e p -> q p e"),
@@ -209,18 +197,17 @@ def tile_attend_pqresid_pl_kernel(
                 in_=turned[b][:].rearrange("p u q -> p q u"),
             )
 
-        v_codes = sb.tile([P, E], U32, name="v_codes", tag="probs1", align_bytes=64)
+        v_codes = sb.tile([P, E], U32, name="v_codes", tag="w0_1", align_bytes=64)
         v_plane = sb.tile([P, E], U8, name="v_plane", align_bytes=64)
         w_codes = [sb.tile([P, QB], U32, name=f"w_codes{b}", align_bytes=64) for b in range(BLOCKS)]
         w_plane = [sb.tile([P, QB], U8, name=f"w_plane{b}", align_bytes=64) for b in range(BLOCKS)]
-        nc.vector.quantize_mx(out=w_codes[0][:].bitcast(FP8X4), scales=w_plane[0][:], in_=w_grouped[0][:])
         for g in range(2):
             cols = slice(2 * P * g, 2 * P * (g + 1))
             nc.vector.quantize_mx(
                 out=v_codes[:, cols].bitcast(FP8X4), scales=v_plane[:, cols],
                 in_=v_grouped[:, 2 * g : 2 * g + 2, :, :].rearrange("p t m j -> p (t m j)"),
             )
-        nc.vector.quantize_mx(out=w_codes[1][:].bitcast(FP8X4), scales=w_plane[1][:], in_=w_grouped[1][:])
+            nc.vector.quantize_mx(out=w_codes[g][:].bitcast(FP8X4), scales=w_plane[g][:], in_=w_grouped[g][:])
 
         o_codes = sb.tile([P, Q], I32, name="o_codes", align_bytes=64)
         o_plane = sb.tile([P, Q], U8, name="o_plane", align_bytes=64)
@@ -249,12 +236,13 @@ def tile_attend_pqresid_pl_kernel(
         for g in range(2):
             for s in range(2):
                 product(last[g][:, s, :], 1, 2 * g + s)
+        y_last = [sb.tile([P, 2, QB], F32, name=f"y_last{g}") for g in range(2)]
+        nc.scalar.copy(out=y_last[0][:], in_=last[0][:])
+        nc.sync.dma_start(out=out_rows[:, 0:2, QB:Q], in_=y_last[0][:])
         nc.vector.tensor_copy(out=o_grouped[:, QB:Q, 0:2], in_=last[0][:].rearrange("p s q -> p q s"))
         nc.scalar.copy(out=o_grouped[:, QB:Q, 2:4], in_=last[1][:].rearrange("p s q -> p q s"))
-        for g, copy in enumerate((nc.vector.tensor_copy, nc.scalar.copy)):
-            y_last = sb.tile([P, 2, QB], F32, name=f"y_last{g}")
-            copy(out=y_last[:], in_=last[g][:])
-            nc.sync.dma_start(out=out_rows[:, 2 * g : 2 * g + 2, QB:Q], in_=y_last[:])
+        nc.scalar.copy(out=y_last[1][:], in_=last[1][:])
+        nc.sync.dma_start(out=out_rows[:, 2:4, QB:Q], in_=y_last[1][:])
 
         for b in range(BLOCKS):
             cols = slice(QB * b, QB * (b + 1))

@@ -53,7 +53,7 @@ def tile_attend_pqresid_pl_kernel(
             out=book_sc[:].bitcast(I32),
             in_=book_scales[0].bitcast(I32).unsqueeze(1).to_broadcast([SCALE_ROWS, ROW_STEP, C // 4]),
         )
-        q_raw = sb.tile([P, PACK, Q], F32, name="q_raw")
+        q_raw = late.tile([P, PACK, Q], F32, name="q_raw", offset=0)
         nc.sync.dma_start(out=q_raw[:], in_=query.rearrange("(p j) q -> p j q", j=PACK))
         nc.vector.memset(fine_sc[0:FINE_AT, :].bitcast(I32), 0)
 
@@ -82,10 +82,7 @@ def tile_attend_pqresid_pl_kernel(
         nc.vector.tensor_copy(book_picked[:], book_sc[:].indirect(book_list[:]))
 
         q_codes = [sb.tile([P, QB], U32, name=f"q_codes{b}", align_bytes=64) for b in range(BLOCKS)]
-        q_grouped = [
-            sb.tile([P, QB, PACK], BF16, name="q_grouped0", align_bytes=64),
-            late.tile([P, QB, PACK], BF16, name="q_grouped1", offset=0, align_bytes=64),
-        ]
+        q_grouped = [sb.tile([P, QB, PACK], BF16, name=f"q_grouped{b}", align_bytes=64) for b in range(BLOCKS)]
         q_plane = [sb.tile([P, QB], U8, name=f"q_plane{b}", align_bytes=64) for b in range(BLOCKS)]
 
         def quantise_queries(b, scale):
@@ -114,14 +111,15 @@ def tile_attend_pqresid_pl_kernel(
         quantise_queries(1, 1.0)
 
         vals_rows = vals.rearrange("(p j) e -> p j e", j=PACK)
-        v_all = late.tile([P, PACK * E], F32, name="v_all", offset=2 * PACK * QB - 64, align_bytes=64)
+        v_all = late.tile([P, PACK * E], F32, name="v_all", offset=64)
         size_col = late.tile([P, PACK], F32, name="size_col", offset=0)
-        nc.sync.dma_start(out=size_col[:], in_=size.rearrange("o (p t) -> p (o t)", t=PACK))
         v_raw = []
         for lo, hi in zip(V_CUTS[:-1], V_CUTS[1:]):
             piece = v_all[:, PACK * lo : PACK * hi].rearrange("p (j e) -> p j e", j=PACK)
             nc.sync.dma_start(out=piece, in_=vals_rows[:, :, lo:hi])
             v_raw.append(piece)
+            if lo == 0:
+                nc.sync.dma_start(out=size_col[:], in_=size.rearrange("o (p t) -> p (o t)", t=PACK))
 
         fine_keys = sb.tile([P, SLOTS], U16, name="fine_keys", align_bytes=64)
         gather_words(fine_keys, fine_w[:], fine_list, (0, HALF, SLOTS))
@@ -152,8 +150,8 @@ def tile_attend_pqresid_pl_kernel(
         for piece in range(2):
             lo, hi = V_CUTS[piece], V_CUTS[piece + 1]
             nc.gpsimd.tensor_scalar(
-                out=v_grouped[:, :, lo // PACK : hi // PACK, :],
-                in0=v_raw[piece].rearrange("p j (m t) -> p t m j", t=PACK),
+                out=v_grouped[:, :, lo // PACK : hi // PACK, :].rearrange("p t m j -> p m t j"),
+                in0=v_raw[piece].rearrange("p j (m t) -> p m t j", t=PACK),
                 scalar1=1.0, scalar2=0.0, op0=ALU.mult, op1=ALU.add,
             )
 

@@ -219,28 +219,27 @@ def tile_attend_pqresid_pl_kernel(
                 rhs=w_codes[b][:].bitcast(FP8X4), rhs_scale=w_plane[b][:], start=True, stop=True,
             )
 
-        y_first = sb.tile([P, PACK, QB], F32, name="y_first")
+        y = sb.tile([P, PACK, Q], F32, name="y")
         for g in range(2):
             acc = ps.tile([P, 2, QB], F32, name=f"first{g}", tag=f"bank{g}")
             for s in range(2):
                 product(acc[:, s, :], 0, 2 * g + s)
-            nc.scalar.copy(out=y_first[:, 2 * g : 2 * g + 2, :], in_=acc[:])
-        nc.sync.dma_start(out=out_rows[:, :, 0:QB], in_=y_first[:])
+            nc.scalar.copy(out=y[:, 2 * g : 2 * g + 2, 0:QB], in_=acc[:])
+        nc.sync.dma_start(out=out_rows[:, 2:4, 0:QB], in_=y[:, 2:4, 0:QB])
         nc.vector.tensor_copy(
             out=o_grouped[:, 0:QB, :].rearrange("p (c i) t -> p c t i", i=4),
-            in_=y_first[:].rearrange("p t (c i) -> p c t i", i=4),
+            in_=y[:, :, 0:QB].rearrange("p t (c i) -> p c t i", i=4),
         )
         last = [ps.tile([P, 2, QB], F32, name=f"last{g}") for g in range(2)]
         for g in range(2):
             for s in range(2):
                 product(last[g][:, s, :], 1, 2 * g + s)
-        y_last = [sb.tile([P, 2, QB], F32, name=f"y_last{g}") for g in range(2)]
-        nc.scalar.copy(out=y_last[0][:], in_=last[0][:])
-        nc.sync.dma_start(out=out_rows[:, 0:2, QB:Q], in_=y_last[0][:])
-        nc.vector.tensor_copy(out=o_grouped[:, QB:Q, 0:2], in_=last[0][:].rearrange("p s q -> p q s"))
+        nc.scalar.copy(out=y[:, 0:2, QB:Q], in_=last[0][:])
+        nc.sync.dma_start(out=out_rows[:, 0:2, :], in_=y[:, 0:2, :])
+        nc.vector.tensor_copy(out=o_grouped[:, QB:Q, 0:2], in_=y[:, 0:2, QB:Q].rearrange("p s q -> p q s"))
         nc.scalar.copy(out=o_grouped[:, QB:Q, 2:4], in_=last[1][:].rearrange("p s q -> p q s"))
-        nc.scalar.copy(out=y_last[1][:], in_=last[1][:])
-        nc.sync.dma_start(out=out_rows[:, 2:4, QB:Q], in_=y_last[1][:])
+        nc.scalar.copy(out=y[:, 2:4, QB:Q], in_=last[1][:])
+        nc.sync.dma_start(out=out_rows[:, 2:4, QB:Q], in_=y[:, 2:4, QB:Q])
 
         for b in range(BLOCKS):
             cols = slice(QB * b, QB * (b + 1))

@@ -22,9 +22,9 @@ PACK = 4
 QB = 128
 BLOCKS = Q // QB
 GROUP = 16
+QUADRANT = 32
 SCALE_ROWS = D // 32
 ROW_STEP = P // SCALE_ROWS
-QUADRANT = 32
 FINE_AT = P - SCALE_ROWS
 HALF = SLOTS // 2
 LAST = SLOTS - QB
@@ -147,18 +147,15 @@ def tile_attend_pqresid_pl_kernel(
             nc.tensor.transpose(size_ps[:, t, :], size_col[:, t : t + 1].to_broadcast([P, P]), ident[:])
 
         v_grouped = sb.tile([P, PACK, P, PACK], BF16, name="v_grouped", align_bytes=64)
-        for piece in range(2):
-            lo, hi = V_CUTS[piece], V_CUTS[piece + 1]
+        for n in range(2):
+            lo, hi = V_CUTS[n], V_CUTS[n + 1]
             nc.gpsimd.tensor_scalar(
                 out=v_grouped[:, :, lo // PACK : hi // PACK, :].rearrange("p t m j -> p m t j"),
-                in0=v_raw[piece].rearrange("p j (m t) -> p m t j", t=PACK),
+                in0=v_raw[n].rearrange("p j (m t) -> p m t j", t=PACK),
                 scalar1=1.0, scalar2=0.0, op0=ALU.mult, op1=ALU.add,
             )
 
-        probs = [
-            sb.tile([P, 2, P, 2], F32, name="probs0", align_bytes=64),
-            sb.tile([P, 2, P, 2], F32, name="probs1", align_bytes=64),
-        ]
+        probs = [sb.tile([P, 2, P, 2], F32, name=f"probs{b}", align_bytes=64) for b in range(BLOCKS)]
         row_sum = [sb.tile([P, 1], F32, name=f"row_sum{b}") for b in range(BLOCKS)]
         for b in range(BLOCKS):
             neg_max = sb.tile([P, 1], F32, name=f"neg_max{b}")
@@ -175,6 +172,7 @@ def tile_attend_pqresid_pl_kernel(
             in_=v_raw[2].rearrange("p j (m t) -> p m j t", t=PACK),
         )
 
+        q_cuts = ((0, QB), (0, QB // 2, QB))
         inv = [sb.tile([P, 1], F32, name=f"inv_sum{b}") for b in range(BLOCKS)]
         turned = [ps.tile([P, 2, QB], F32, name=f"turned{b}") for b in range(BLOCKS)]
         w_grouped = [sb.tile([P, QB * PACK], BF16, name=f"w_grouped{b}", align_bytes=64) for b in range(BLOCKS)]
@@ -190,22 +188,27 @@ def tile_attend_pqresid_pl_kernel(
                 if (b, u) == (0, 0):
                     nc.vector.reciprocal(out=inv[1][:], in_=row_sum[1][:])
                 nc.tensor.transpose(turned[b][:, u, :], w[:].rearrange("q p e -> q (p e)").bitcast(F32), ident[:])
-            nc.scalar.copy(
-                out=w_grouped[b][:].bitcast(F32).rearrange("p (q u) -> p q u", u=2),
-                in_=turned[b][:].rearrange("p u q -> p q u"),
-            )
+            for lo, hi in zip(q_cuts[b][:-1], q_cuts[b][1:]):
+                nc.scalar.copy(
+                    out=w_grouped[b][:].bitcast(F32).rearrange("p (q u) -> p q u", u=2)[:, lo:hi, :],
+                    in_=turned[b][:, :, lo:hi].rearrange("p u q -> p q u"),
+                )
 
         v_codes = sb.tile([P, E], U32, name="v_codes", tag="w0_1", align_bytes=64)
         v_plane = sb.tile([P, E], U8, name="v_plane", align_bytes=64)
         w_codes = [sb.tile([P, QB], U32, name=f"w_codes{b}", align_bytes=64) for b in range(BLOCKS)]
         w_plane = [sb.tile([P, QB], U8, name=f"w_plane{b}", align_bytes=64) for b in range(BLOCKS)]
-        for g in range(2):
-            cols = slice(2 * P * g, 2 * P * (g + 1))
+        for b in range(BLOCKS):
+            cols = slice(2 * P * b, 2 * P * (b + 1))
             nc.vector.quantize_mx(
                 out=v_codes[:, cols].bitcast(FP8X4), scales=v_plane[:, cols],
-                in_=v_grouped[:, 2 * g : 2 * g + 2, :, :].rearrange("p t m j -> p (t m j)"),
+                in_=v_grouped[:, 2 * b : 2 * b + 2, :, :].rearrange("p t m j -> p (t m j)"),
             )
-            nc.vector.quantize_mx(out=w_codes[g][:].bitcast(FP8X4), scales=w_plane[g][:], in_=w_grouped[g][:])
+            for lo, hi in zip(q_cuts[b][:-1], q_cuts[b][1:]):
+                nc.vector.quantize_mx(
+                    out=w_codes[b][:, lo:hi].bitcast(FP8X4), scales=w_plane[b][:, lo:hi],
+                    in_=w_grouped[b][:, PACK * lo : PACK * hi],
+                )
 
         o_codes = sb.tile([P, Q], I32, name="o_codes", align_bytes=64)
         o_plane = sb.tile([P, Q], U8, name="o_plane", align_bytes=64)

@@ -55,10 +55,10 @@ def tile_attend_pqresid_pl_kernel(
         )
         q_raw = late.tile([P, PACK, Q], F32, name="q_raw", offset=0)
         nc.sync.dma_start(out=q_raw[:], in_=query.rearrange("(p j) q -> p j q", j=PACK))
-        nc.vector.memset(fine_sc[0:FINE_AT, :].bitcast(I32), 0)
 
         zero = sb.tile([P, 1], F32, name="zero")
         nc.vector.memset(zero[:], 0.0)
+        nc.vector.memset(fine_sc[0:FINE_AT, :].bitcast(I32), 0)
         one = sb.tile([P, 1], F32, name="one", tag="book_plane", align_bytes=64)
         nc.scalar.activation(out=one[:], in_=zero[:], func=ACT.Exp)
         fine_w = words.tile([P, T], U16, name="fine_w", offset=0)

@@ -28,6 +28,7 @@ ROW_STEP = P // SCALE_ROWS
 FINE_AT = P - SCALE_ROWS
 HALF = SLOTS // 2
 LAST = SLOTS - QB
+PARTS = ((0, HALF), (HALF, SLOTS))
 WORD_BYTES = 4096
 V_CUTS = (0, 160, 352, 512)
 
@@ -55,10 +56,10 @@ def tile_attend_pqresid_pl_kernel(
         )
         q_raw = late.tile([P, PACK, Q], F32, name="q_raw", offset=0)
         nc.sync.dma_start(out=q_raw[:], in_=query.rearrange("(p j) q -> p j q", j=PACK))
+        nc.vector.memset(fine_sc[0:FINE_AT, :].bitcast(I32), 0)
 
         zero = sb.tile([P, 1], F32, name="zero")
         nc.vector.memset(zero[:], 0.0)
-        nc.vector.memset(fine_sc[0:FINE_AT, :].bitcast(I32), 0)
         one = sb.tile([P, 1], F32, name="one", tag="book_plane", align_bytes=64)
         nc.scalar.activation(out=one[:], in_=zero[:], func=ACT.Exp)
         fine_w = words.tile([P, T], U16, name="fine_w", offset=0)
@@ -126,18 +127,19 @@ def tile_attend_pqresid_pl_kernel(
         book_keys = sb.tile([P, SLOTS], U32, name="book_keys", align_bytes=64)
         gather_words(book_keys, book_w[:].bitcast(U32), book_list, (0, HALF, LAST, SLOTS))
 
-        scores = [ps.tile([P, SLOTS], F32, name=f"scores{b}", tag=f"bank{b}") for b in range(BLOCKS)]
+        parts = [ps.tile([P, hi - lo], F32, name=f"part{h}", tag=f"bank{h}") for h, (lo, hi) in enumerate(PARTS)]
+        whole = ps.tile([P, SLOTS], F32, name="whole")
 
         def score_pass(b, keys, plane, dtype, lo, hi, start, stop):
             nc.tensor.matmul_mx(
-                out=scores[b][:, lo:hi], lhsT=q_codes[b][:].bitcast(FP8X4), lhsT_scale=q_plane[b][:],
+                out=whole[:, lo:hi] if b else parts[lo // HALF][:, lo % HALF : lo % HALF + hi - lo], lhsT=q_codes[b][:].bitcast(FP8X4), lhsT_scale=q_plane[b][:],
                 rhs=keys[:, lo:hi].bitcast(dtype), rhs_scale=plane[:, lo:hi], start=start, stop=stop,
             )
 
         score_pass(0, fine_keys, fine_plane, FP4X4, 0, HALF, True, False)
-        score_pass(0, fine_keys, fine_plane, FP4X4, HALF, SLOTS, False, False)
+        score_pass(0, fine_keys, fine_plane, FP4X4, HALF, SLOTS, True, False)
         score_pass(1, fine_keys, fine_plane, FP4X4, 0, SLOTS, True, False)
-        score_pass(0, book_keys, book_plane, FP8X4, 0, HALF, False, False)
+        score_pass(0, book_keys, book_plane, FP8X4, 0, HALF, False, True)
         score_pass(0, book_keys, book_plane, FP8X4, HALF, LAST, False, False)
         score_pass(0, book_keys, book_plane, FP8X4, LAST, SLOTS, False, True)
         score_pass(1, book_keys, book_plane, FP8X4, 0, SLOTS, False, True)
@@ -156,54 +158,98 @@ def tile_attend_pqresid_pl_kernel(
             )
 
         probs = [sb.tile([P, 2, P, 2], F32, name=f"probs{b}", align_bytes=64) for b in range(BLOCKS)]
-        row_sum = [sb.tile([P, 1], F32, name=f"row_sum{b}") for b in range(BLOCKS)]
-        for b in range(BLOCKS):
-            neg_max = sb.tile([P, 1], F32, name=f"neg_max{b}")
+        part_max = [sb.tile([P, 1], F32, name=f"part_max{h}") for h in range(2)]
+        part_sum = [sb.tile([P, 1], F32, name=f"part_sum{h}") for h in range(2)]
+        ratio = [sb.tile([P, 1], F32, name=f"ratio{h}") for h in range(2)]
+        spans = [slice(lo // PACK, hi // PACK) for lo, hi in PARTS]
+        for h in range(2):
             nc.vector.tensor_reduce(
-                out=neg_max[:], in_=scores[b][:], axis=mybir.AxisListType.X, op=ALU.max, negate=True
+                out=part_max[h][:], in_=parts[h][:], axis=mybir.AxisListType.X, op=ALU.max, negate=True
             )
             nc.scalar.activation(
-                out=probs[b][:], in_=scores[b][:].rearrange("q (p u e) -> q u p e", u=2, e=2),
-                func=ACT.Exp, bias=neg_max[:], scale=1.0, accum_out=row_sum[b][:],
+                out=probs[0][:, :, spans[h], :], in_=parts[h][:].rearrange("q (p u e) -> q u p e", u=2, e=2),
+                func=ACT.Exp, bias=part_max[h][:], scale=1.0, accum_out=part_sum[h][:],
             )
+        for h in range(2):
+            nc.scalar.activation(
+                out=ratio[h][:], in_=part_max[1 - h][:], func=ACT.Exp, bias=part_max[h][:], scale=-1.0
+            )
+        neg_max = sb.tile([P, 1], F32, name="neg_max")
+        row_sum = sb.tile([P, 1], F32, name="row_sum", tag="row_sum", align_bytes=64)
+        nc.vector.tensor_reduce(out=neg_max[:], in_=whole[:], axis=mybir.AxisListType.X, op=ALU.max, negate=True)
+        nc.scalar.activation(
+            out=probs[1][:], in_=whole[:].rearrange("q (p u e) -> q u p e", u=2, e=2),
+            func=ACT.Exp, bias=neg_max[:], scale=1.0, accum_out=row_sum[:],
+        )
 
-        nc.scalar.copy(
+        unit = sb.tile([P, 1], F32, name="unit")
+        nc.vector.tensor_scalar(out=unit[:], in0=neg_max[:], scalar1=neg_max[:], scalar2=None, op0=ALU.is_equal)
+        nc.scalar.activation(
             out=v_grouped[:, :, V_CUTS[2] // PACK :, :].rearrange("p t m j -> p m j t"),
-            in_=v_raw[2].rearrange("p j (m t) -> p m j t", t=PACK),
+            in_=v_raw[2].rearrange("p j (m t) -> p m j t", t=PACK), func=ACT.Copy, scale=unit[:],
         )
 
         q_cuts = ((0, QB), (0, QB // 2, QB))
-        inv = [sb.tile([P, 1], F32, name=f"inv_sum{b}") for b in range(BLOCKS)]
         turned = [ps.tile([P, 2, QB], F32, name=f"turned{b}") for b in range(BLOCKS)]
         w_grouped = [sb.tile([P, QB * PACK], BF16, name=f"w_grouped{b}", align_bytes=64) for b in range(BLOCKS)]
-        nc.vector.reciprocal(out=inv[0][:], in_=row_sum[0][:])
-        for b in range(BLOCKS):
-            for u in range(2):
-                w = sb.tile([P, P, 2], BF16, name=f"w{b}_{u}", tag=f"w{b}_{u}", align_bytes=64)
-                nc.vector.scalar_tensor_tensor(
-                    out=w[:], in0=probs[b][:, u, :, :], scalar=inv[b][:],
-                    in1=size_ps[:, 2 * u : 2 * u + 2, :].rearrange("q e p -> q p e"),
-                    op0=ALU.mult, op1=ALU.mult,
-                )
-                if (b, u) == (0, 0):
-                    nc.vector.reciprocal(out=inv[1][:], in_=row_sum[1][:])
-                nc.tensor.transpose(turned[b][:, u, :], w[:].rearrange("q p e -> q (p e)").bitcast(F32), ident[:])
+        size_view = size_ps[:].rearrange("q (u e) p -> q u p e", u=2)
+        sized = sb.tile([P, 2, P, 2], F32, name="sized", align_bytes=64)
+        total = sb.tile([P, 2], F32, name="total")
+        inv0 = sb.tile([P, 2], F32, name="inv0")
+        inv1 = sb.tile([P, 1], F32, name="inv1")
+        w0 = sb.tile([P, 2, P, 2], BF16, name="w0", align_bytes=64)
+        w1 = [sb.tile([P, P, 2], BF16, name=f"w1_{u}", align_bytes=64) for u in range(2)]
+
+        def weigh(h, us):
+            nc.vector.tensor_tensor(
+                out=sized[:, us, spans[h], :], in0=probs[0][:, us, spans[h], :], in1=size_view[:, us, spans[h], :],
+                op=ALU.mult,
+            )
+
+        def turn(b, u, pairs):
+            nc.tensor.transpose(turned[b][:, u, :], pairs.rearrange("q p e -> q (p e)").bitcast(F32), ident[:])
+
+        def copy_out(b):
             for lo, hi in zip(q_cuts[b][:-1], q_cuts[b][1:]):
                 nc.scalar.copy(
                     out=w_grouped[b][:].bitcast(F32).rearrange("p (q u) -> p q u", u=2)[:, lo:hi, :],
                     in_=turned[b][:, :, lo:hi].rearrange("p u q -> p q u"),
                 )
 
-        v_codes = sb.tile([P, E], U32, name="v_codes", tag="w0_1", align_bytes=64)
+        weigh(0, slice(0, 2))
+        for h in range(2):
+            nc.vector.tensor_scalar(
+                out=total[:, h : h + 1], in0=ratio[h][:], scalar1=part_sum[1 - h][:], scalar2=part_sum[h][:],
+                op0=ALU.mult, op1=ALU.add,
+            )
+        weigh(1, slice(0, 1))
+        nc.vector.reciprocal(out=inv0[:], in_=total[:])
+        weigh(1, slice(1, 2))
+        for h in range(2):
+            nc.vector.tensor_scalar(
+                out=w0[:, :, spans[h], :], in0=sized[:, :, spans[h], :], scalar1=inv0[:, h : h + 1], scalar2=None,
+                op0=ALU.mult,
+            )
+        for u in range(2):
+            turn(0, u, w0[:, u, :, :])
+        copy_out(0)
+        nc.vector.reciprocal(out=inv1[:], in_=row_sum[:])
+        for u in range(2):
+            nc.vector.scalar_tensor_tensor(
+                out=w1[u][:], in0=probs[1][:, u, :, :], scalar=inv1[:],
+                in1=size_ps[:, 2 * u : 2 * u + 2, :].rearrange("q e p -> q p e"), op0=ALU.mult, op1=ALU.mult,
+            )
+            turn(1, u, w1[u][:])
+        copy_out(1)
+
+        v_codes = sb.tile([P, E], U32, name="v_codes", tag="row_sum", align_bytes=64)
         v_plane = sb.tile([P, E], U8, name="v_plane", align_bytes=64)
         w_codes = [sb.tile([P, QB], U32, name=f"w_codes{b}", align_bytes=64) for b in range(BLOCKS)]
         w_plane = [sb.tile([P, QB], U8, name=f"w_plane{b}", align_bytes=64) for b in range(BLOCKS)]
+        nc.vector.quantize_mx(
+            out=v_codes[:].bitcast(FP8X4), scales=v_plane[:], in_=v_grouped[:].rearrange("p t m j -> p (t m j)")
+        )
         for b in range(BLOCKS):
-            cols = slice(2 * P * b, 2 * P * (b + 1))
-            nc.vector.quantize_mx(
-                out=v_codes[:, cols].bitcast(FP8X4), scales=v_plane[:, cols],
-                in_=v_grouped[:, 2 * b : 2 * b + 2, :, :].rearrange("p t m j -> p (t m j)"),
-            )
             for lo, hi in zip(q_cuts[b][:-1], q_cuts[b][1:]):
                 nc.vector.quantize_mx(
                     out=w_codes[b][:, lo:hi].bitcast(FP8X4), scales=w_plane[b][:, lo:hi],

@@ -30,7 +30,7 @@ HALF = SLOTS // 2
 LAST = SLOTS - QB
 PARTS = ((0, HALF), (HALF, SLOTS))
 WORD_BYTES = 4096
-V_CUTS = (0, 160, 352, 512)
+V_CUTS = (0, 192, 384, 512)
 
 
 def tile_attend_pqresid_pl_kernel(
@@ -182,27 +182,20 @@ def tile_attend_pqresid_pl_kernel(
             func=ACT.Exp, bias=neg_max[:], scale=1.0, accum_out=row_sum[:],
         )
 
-        unit = sb.tile([P, 1], F32, name="unit")
-        nc.vector.tensor_scalar(out=unit[:], in0=neg_max[:], scalar1=neg_max[:], scalar2=None, op0=ALU.is_equal)
-        nc.scalar.activation(
-            out=v_grouped[:, :, V_CUTS[2] // PACK :, :].rearrange("p t m j -> p m j t"),
-            in_=v_raw[2].rearrange("p j (m t) -> p m j t", t=PACK), func=ACT.Copy, scale=unit[:],
-        )
-
         q_cuts = ((0, QB), (0, QB // 2, QB))
         turned = [ps.tile([P, 2, QB], F32, name=f"turned{b}") for b in range(BLOCKS)]
         w_grouped = [sb.tile([P, QB * PACK], BF16, name=f"w_grouped{b}", align_bytes=64) for b in range(BLOCKS)]
         size_view = size_ps[:].rearrange("q (u e) p -> q u p e", u=2)
-        sized = sb.tile([P, 2, P, 2], F32, name="sized", align_bytes=64)
+        sized = sb.tile([P, P, 2], F32, name="sized", align_bytes=64)
         total = sb.tile([P, 2], F32, name="total")
         inv0 = sb.tile([P, 2], F32, name="inv0")
         inv1 = sb.tile([P, 1], F32, name="inv1")
-        w0 = sb.tile([P, 2, P, 2], BF16, name="w0", align_bytes=64)
+        w0 = [sb.tile([P, P, 2], BF16, name=f"w0_{u}", align_bytes=64) for u in range(2)]
         w1 = [sb.tile([P, P, 2], BF16, name=f"w1_{u}", align_bytes=64) for u in range(2)]
 
-        def weigh(h, us):
+        def weigh(h):
             nc.vector.tensor_tensor(
-                out=sized[:, us, spans[h], :], in0=probs[0][:, us, spans[h], :], in1=size_view[:, us, spans[h], :],
+                out=sized[:, spans[h], :], in0=probs[0][:, 1, spans[h], :], in1=size_view[:, 1, spans[h], :],
                 op=ALU.mult,
             )
 
@@ -216,22 +209,30 @@ def tile_attend_pqresid_pl_kernel(
                     in_=turned[b][:, :, lo:hi].rearrange("p u q -> p q u"),
                 )
 
-        weigh(0, slice(0, 2))
+        weigh(0)
         for h in range(2):
             nc.vector.tensor_scalar(
                 out=total[:, h : h + 1], in0=ratio[h][:], scalar1=part_sum[1 - h][:], scalar2=part_sum[h][:],
                 op0=ALU.mult, op1=ALU.add,
             )
-        weigh(1, slice(0, 1))
+        weigh(1)
         nc.vector.reciprocal(out=inv0[:], in_=total[:])
-        weigh(1, slice(1, 2))
+        unit = sb.tile([P, 1], F32, name="unit")
+        nc.vector.tensor_scalar(out=unit[:], in0=total[:, 0:1], scalar1=total[:, 0:1], scalar2=None, op0=ALU.is_equal)
         for h in range(2):
-            nc.vector.tensor_scalar(
-                out=w0[:, :, spans[h], :], in0=sized[:, :, spans[h], :], scalar1=inv0[:, h : h + 1], scalar2=None,
-                op0=ALU.mult,
+            nc.vector.scalar_tensor_tensor(
+                out=w0[0][:, spans[h], :], in0=probs[0][:, 0, spans[h], :], scalar=inv0[:, h : h + 1],
+                in1=size_view[:, 0, spans[h], :], op0=ALU.mult, op1=ALU.mult,
             )
+            nc.scalar.activation(
+                out=w0[1][:, spans[h], :], in_=sized[:, spans[h], :], func=ACT.Copy, scale=inv0[:, h : h + 1]
+            )
+        nc.scalar.activation(
+            out=v_grouped[:, :, V_CUTS[2] // PACK :, :].rearrange("p t m j -> p m j t"),
+            in_=v_raw[2].rearrange("p j (m t) -> p m j t", t=PACK), func=ACT.Copy, scale=unit[:],
+        )
         for u in range(2):
-            turn(0, u, w0[:, u, :, :])
+            turn(0, u, w0[u][:])
         copy_out(0)
         nc.vector.reciprocal(out=inv1[:], in_=row_sum[:])
         for u in range(2):
@@ -246,10 +247,12 @@ def tile_attend_pqresid_pl_kernel(
         v_plane = sb.tile([P, E], U8, name="v_plane", align_bytes=64)
         w_codes = [sb.tile([P, QB], U32, name=f"w_codes{b}", align_bytes=64) for b in range(BLOCKS)]
         w_plane = [sb.tile([P, QB], U8, name=f"w_plane{b}", align_bytes=64) for b in range(BLOCKS)]
-        nc.vector.quantize_mx(
-            out=v_codes[:].bitcast(FP8X4), scales=v_plane[:], in_=v_grouped[:].rearrange("p t m j -> p (t m j)")
-        )
         for b in range(BLOCKS):
+            cols = slice(2 * P * b, 2 * P * (b + 1))
+            nc.vector.quantize_mx(
+                out=v_codes[:, cols].bitcast(FP8X4), scales=v_plane[:, cols],
+                in_=v_grouped[:, 2 * b : 2 * b + 2, :, :].rearrange("p t m j -> p (t m j)"),
+            )
             for lo, hi in zip(q_cuts[b][:-1], q_cuts[b][1:]):
                 nc.vector.quantize_mx(
                     out=w_codes[b][:, lo:hi].bitcast(FP8X4), scales=w_plane[b][:, lo:hi],

@@ -224,6 +224,8 @@ def tile_attend_pqresid_pl_kernel(
                 out=w0[0][:, spans[h], :], in0=probs[0][:, 0, spans[h], :], scalar=inv0[:, h : h + 1],
                 in1=size_view[:, 0, spans[h], :], op0=ALU.mult, op1=ALU.mult,
             )
+            if h == 0:
+                nc.vector.reciprocal(out=inv1[:], in_=row_sum[:])
             nc.scalar.activation(
                 out=w0[1][:, spans[h], :], in_=sized[:, spans[h], :], func=ACT.Copy, scale=inv0[:, h : h + 1]
             )
@@ -234,7 +236,6 @@ def tile_attend_pqresid_pl_kernel(
         for u in range(2):
             turn(0, u, w0[u][:])
         copy_out(0)
-        nc.vector.reciprocal(out=inv1[:], in_=row_sum[:])
         for u in range(2):
             nc.vector.scalar_tensor_tensor(
                 out=w1[u][:], in0=probs[1][:, u, :, :], scalar=inv1[:],
@@ -245,14 +246,15 @@ def tile_attend_pqresid_pl_kernel(
 
         v_codes = sb.tile([P, E], U32, name="v_codes", tag="row_sum", align_bytes=64)
         v_plane = sb.tile([P, E], U8, name="v_plane", align_bytes=64)
+        t_cuts = ((0, 2), (2, 3, 4))
         w_codes = [sb.tile([P, QB], U32, name=f"w_codes{b}", align_bytes=64) for b in range(BLOCKS)]
         w_plane = [sb.tile([P, QB], U8, name=f"w_plane{b}", align_bytes=64) for b in range(BLOCKS)]
         for b in range(BLOCKS):
-            cols = slice(2 * P * b, 2 * P * (b + 1))
-            nc.vector.quantize_mx(
-                out=v_codes[:, cols].bitcast(FP8X4), scales=v_plane[:, cols],
-                in_=v_grouped[:, 2 * b : 2 * b + 2, :, :].rearrange("p t m j -> p (t m j)"),
-            )
+            for lo, hi in zip(t_cuts[b][:-1], t_cuts[b][1:]):
+                nc.vector.quantize_mx(
+                    out=v_codes[:, P * lo : P * hi].bitcast(FP8X4), scales=v_plane[:, P * lo : P * hi],
+                    in_=v_grouped[:, lo:hi, :, :].rearrange("p t m j -> p (t m j)"),
+                )
             for lo, hi in zip(q_cuts[b][:-1], q_cuts[b][1:]):
                 nc.vector.quantize_mx(
                     out=w_codes[b][:, lo:hi].bitcast(FP8X4), scales=w_plane[b][:, lo:hi],

@@ -159,7 +159,7 @@ def tile_attend_pqresid_pl_kernel(
 
         probs = [sb.tile([P, 2, P, 2], F32, name=f"probs{b}", align_bytes=64) for b in range(BLOCKS)]
         part_max = [sb.tile([P, 1], F32, name=f"part_max{h}") for h in range(2)]
-        part_sum = [sb.tile([P, 1], F32, name=f"part_sum{h}") for h in range(2)]
+        part_sum = [sb.tile([P, 1], F32, name=f"part_sum{h}", tag=f"part_sum{h}", align_bytes=64) for h in range(2)]
         ratio = [sb.tile([P, 1], F32, name=f"ratio{h}") for h in range(2)]
         spans = [slice(lo // PACK, hi // PACK) for lo, hi in PARTS]
         for h in range(2):
@@ -186,7 +186,7 @@ def tile_attend_pqresid_pl_kernel(
         turned = [ps.tile([P, 2, QB], F32, name=f"turned{b}") for b in range(BLOCKS)]
         w_grouped = [sb.tile([P, QB * PACK], BF16, name=f"w_grouped{b}", align_bytes=64) for b in range(BLOCKS)]
         size_view = size_ps[:].rearrange("q (u e) p -> q u p e", u=2)
-        sized = sb.tile([P, P, 2], F32, name="sized", align_bytes=64)
+        sized = sb.tile([P, P, 2], F32, name="sized", tag="part_sum0", align_bytes=64)
         total = sb.tile([P, 2], F32, name="total")
         inv0 = sb.tile([P, 2], F32, name="inv0")
         inv1 = sb.tile([P, 1], F32, name="inv1")
@@ -209,14 +209,14 @@ def tile_attend_pqresid_pl_kernel(
                     in_=turned[b][:, :, lo:hi].rearrange("p u q -> p q u"),
                 )
 
-        weigh(0)
         for h in range(2):
             nc.vector.tensor_scalar(
                 out=total[:, h : h + 1], in0=ratio[h][:], scalar1=part_sum[1 - h][:], scalar2=part_sum[h][:],
                 op0=ALU.mult, op1=ALU.add,
             )
-        weigh(1)
         nc.vector.reciprocal(out=inv0[:], in_=total[:])
+        for h in range(2):
+            weigh(h)
         unit = sb.tile([P, 1], F32, name="unit")
         nc.vector.tensor_scalar(out=unit[:], in0=total[:, 0:1], scalar1=total[:, 0:1], scalar2=None, op0=ALU.is_equal)
         for h in range(2):

from contextlib import ExitStack

import concourse.mybir as mybir
from concourse.masks import make_identity

D, C, T, SLOTS, Q, E = 512, 1024, 2048, 512, 256, 512
FLOPS = 2 * D * Q * SLOTS * 2 + 2 * SLOTS * E * Q

F32 = mybir.dt.float32
BF16 = mybir.dt.bfloat16
I32 = mybir.dt.int32
U32 = mybir.dt.uint32
U16 = mybir.dt.uint16
U8 = mybir.dt.uint8
FP8X4 = mybir.dt.float8_e4m3fn_x4
FP4X4 = mybir.dt.float4_e2m1fn_x4
ACT = mybir.ActivationFunctionType
ALU = mybir.AluOpType

P = 128
PACK = 4
QB = 128
BLOCKS = Q // QB
GROUP = 16
QUADRANT = 32
SCALE_ROWS = D // 32
ROW_STEP = P // SCALE_ROWS
FINE_AT = P - SCALE_ROWS
HALF = SLOTS // 2
LAST = SLOTS - QB
PARTS = ((0, HALF), (HALF, SLOTS))
WORD_BYTES = 4096
V_CUTS = (0, 192, 384, 512)


def tile_attend_pqresid_pl_kernel(
    tc, query, book_words, book_scales, fine_words, fine_scales, size, vals, offs, offs2, out_0, out_1, out_2
):
    nc = tc.nc
    with ExitStack() as ctx:
        sb = ctx.enter_context(tc.tile_pool(name="sb", bufs=1))
        ps = ctx.enter_context(tc.psum_pool(name="ps", bufs=1))
        words = ctx.enter_context(tc.tile_pool(name="words", bufs=1))
        late = ctx.enter_context(tc.tile_pool(name="late", bufs=1))

        fine_list = sb.tile([P, SLOTS // GROUP], U16, name="fine_list")
        nc.sync.dma_start(fine_list[:], offs2)
        fine_sc = sb.tile([P, T], U8, name="fine_sc", align_bytes=64)
        nc.scalar.dma_start(out=fine_sc[FINE_AT:P, :].bitcast(I32), in_=fine_scales[0].bitcast(I32))
        book_list = sb.tile([P, SLOTS // GROUP], U16, name="book_list")
        nc.sync.dma_start(book_list[:], offs)
        book_sc = sb.tile([P, C], U8, name="book_sc", align_bytes=64)
        nc.sync.dma_start(
            out=book_sc[:].bitcast(I32),
            in_=book_scales[0].bitcast(I32).unsqueeze(1).to_broadcast([SCALE_ROWS, ROW_STEP, C // 4]),
        )
        q_raw = late.tile([P, PACK, Q], F32, name="q_raw", offset=0)
        nc.sync.dma_start(out=q_raw[:], in_=query.rearrange("(p j) q -> p j q", j=PACK))
        nc.vector.memset(fine_sc[0:FINE_AT, :].bitcast(I32), 0)

        zero = sb.tile([P, 1], F32, name="zero")
        nc.vector.memset(zero[:], 0.0)
        one = sb.tile([P, 1], F32, name="one", tag="book_plane", align_bytes=64)
        nc.scalar.activation(out=one[:], in_=zero[:], func=ACT.Exp)
        fine_w = words.tile([P, T], U16, name="fine_w", offset=0)
        nc.sync.dma_start(out=fine_w[:].bitcast(I32), in_=fine_words[0].bitcast(I32))
        book_w = words.tile([P, C], I32, name="book_w", offset=WORD_BYTES)
        nc.sync.dma_start(out=book_w[:], in_=book_words[0].rearrange("p n t -> p (n t)").bitcast(I32))

        ident = sb.tile([P, P], F32, name="ident")
        make_identity(nc, ident[:])

        fine_plane = sb.tile([P, SLOTS], U8, name="fine_plane", align_bytes=64)
        nc.vector.memset(fine_plane[:].bitcast(I32), 0)

        fine_picked = sb.tile([P, SLOTS], U8, name="fine_picked", align_bytes=64)
        nc.vector.tensor_copy(fine_picked[:], fine_sc[:].indirect(fine_list[:]))
        for j in range(4):
            nc.sync.dma_start(
                out=fine_plane[j:P:QUADRANT, :].bitcast(I32), in_=fine_picked[FINE_AT + j : P : 4, :].bitcast(I32)
            )
        book_picked = sb.tile([P, SLOTS], U8, name="book_picked", align_bytes=64)
        nc.vector.tensor_copy(book_picked[:], book_sc[:].indirect(book_list[:]))

        q_codes = [sb.tile([P, QB], U32, name=f"q_codes{b}", align_bytes=64) for b in range(BLOCKS)]
        q_grouped = [sb.tile([P, QB, PACK], BF16, name=f"q_grouped{b}", align_bytes=64) for b in range(BLOCKS)]
        q_plane = [sb.tile([P, QB], U8, name=f"q_plane{b}", align_bytes=64) for b in range(BLOCKS)]

        def quantise_queries(b, scale):
            grouped = q_grouped[b]
            nc.scalar.activation(
                out=grouped[:].rearrange("p (c i) j -> p c j i", i=4),
                in_=q_raw[:, :, QB * b : QB * (b + 1)].rearrange("p j (c i) -> p c j i", i=4),
                func=ACT.Copy, scale=scale,
            )
            nc.vector.quantize_mx(
                out=q_codes[b][:].bitcast(FP8X4), scales=q_plane[b][:], in_=grouped[:].rearrange("p q j -> p (q j)")
            )

        def gather_words(keys, window, offsets, cuts):
            for lo, hi in zip(cuts[:-1], cuts[1:]):
                nc.vector.tensor_copy(keys[:, lo:hi], window.indirect(offsets[:, lo // GROUP : hi // GROUP]))

        quantise_queries(0, one[:])
        book_plane = sb.tile([P, SLOTS], U8, name="book_plane", tag="book_plane", align_bytes=64)
        nc.vector.tensor_copy(book_plane[:].bitcast(I32), book_picked[:].bitcast(I32))
        for j in range(1, 4):
            nc.sync.dma_start(
                out=book_plane[j:P:QUADRANT, :].bitcast(I32),
                in_=book_picked[ROW_STEP * j : P : QUADRANT, :].bitcast(I32),
            )
        quantise_queries(1, 1.0)

        vals_rows = vals.rearrange("(p j) e -> p j e", j=PACK)
        v_all = late.tile([P, PACK * E], F32, name="v_all", offset=64)
        size_col = late.tile([P, PACK], F32, name="size_col", offset=0)
        v_raw = []
        for lo, hi in zip(V_CUTS[:-1], V_CUTS[1:]):
            piece = v_all[:, PACK * lo : PACK * hi].rearrange("p (j e) -> p j e", j=PACK)
            nc.sync.dma_start(out=piece, in_=vals_rows[:, :, lo:hi])
            v_raw.append(piece)
            if lo == 0:
                nc.sync.dma_start(out=size_col[:], in_=size.rearrange("o (p t) -> p (o t)", t=PACK))

        fine_keys = sb.tile([P, SLOTS], U16, name="fine_keys", align_bytes=64)
        gather_words(fine_keys, fine_w[:], fine_list, (0, HALF, SLOTS))
        book_keys = sb.tile([P, SLOTS], U32, name="book_keys", align_bytes=64)
        gather_words(book_keys, book_w[:].bitcast(U32), book_list, (0, HALF, LAST, SLOTS))

        parts = [ps.tile([P, hi - lo], F32, name=f"part{h}", tag=f"bank{h}") for h, (lo, hi) in enumerate(PARTS)]
        whole = ps.tile([P, SLOTS], F32, name="whole")

        def score_pass(b, keys, plane, dtype, lo, hi, start, stop):
            nc.tensor.matmul_mx(
                out=whole[:, lo:hi] if b else parts[lo // HALF][:, lo % HALF : lo % HALF + hi - lo], lhsT=q_codes[b][:].bitcast(FP8X4), lhsT_scale=q_plane[b][:],
                rhs=keys[:, lo:hi].bitcast(dtype), rhs_scale=plane[:, lo:hi], start=start, stop=stop,
            )

        score_pass(0, fine_keys, fine_plane, FP4X4, 0, HALF, True, False)
        score_pass(0, fine_keys, fine_plane, FP4X4, HALF, SLOTS, True, False)
        score_pass(1, fine_keys, fine_plane, FP4X4, 0, SLOTS, True, False)
        score_pass(0, book_keys, book_plane, FP8X4, 0, HALF, False, True)
        score_pass(0, book_keys, book_plane, FP8X4, HALF, LAST, False, False)
        score_pass(0, book_keys, book_plane, FP8X4, LAST, SLOTS, False, True)
        score_pass(1, book_keys, book_plane, FP8X4, 0, SLOTS, False, True)

        size_ps = ps.tile([P, PACK, P], F32, name="size_ps")
        for t in range(PACK):
            nc.tensor.transpose(size_ps[:, t, :], size_col[:, t : t + 1].to_broadcast([P, P]), ident[:])

        v_grouped = sb.tile([P, PACK, P, PACK], BF16, name="v_grouped", align_bytes=64)
        for n in range(2):
            lo, hi = V_CUTS[n], V_CUTS[n + 1]
            nc.gpsimd.tensor_scalar(
                out=v_grouped[:, :, lo // PACK : hi // PACK, :].rearrange("p t m j -> p m t j"),
                in0=v_raw[n].rearrange("p j (m t) -> p m t j", t=PACK),
                scalar1=1.0, scalar2=0.0, op0=ALU.mult, op1=ALU.add,
            )

        probs = [sb.tile([P, 2, P, 2], F32, name=f"probs{b}", align_bytes=64) for b in range(BLOCKS)]
        part_max = [sb.tile([P, 1], F32, name=f"part_max{h}") for h in range(2)]
        part_sum = [sb.tile([P, 1], F32, name=f"part_sum{h}", tag=f"part_sum{h}", align_bytes=64) for h in range(2)]
        ratio = [sb.tile([P, 1], F32, name=f"ratio{h}") for h in range(2)]
        spans = [slice(lo // PACK, hi // PACK) for lo, hi in PARTS]
        for h in range(2):
            nc.vector.tensor_reduce(
                out=part_max[h][:], in_=parts[h][:], axis=mybir.AxisListType.X, op=ALU.max, negate=True
            )
            nc.scalar.activation(
                out=probs[0][:, :, spans[h], :], in_=parts[h][:].rearrange("q (p u e) -> q u p e", u=2, e=2),
                func=ACT.Exp, bias=part_max[h][:], scale=1.0, accum_out=part_sum[h][:],
            )
        for h in range(2):
            nc.scalar.activation(
                out=ratio[h][:], in_=part_max[1 - h][:], func=ACT.Exp, bias=part_max[h][:], scale=-1.0
            )
        neg_max = sb.tile([P, 1], F32, name="neg_max")
        row_sum = sb.tile([P, 1], F32, name="row_sum", tag="row_sum", align_bytes=64)
        nc.vector.tensor_reduce(out=neg_max[:], in_=whole[:], axis=mybir.AxisListType.X, op=ALU.max, negate=True)
        nc.scalar.activation(
            out=probs[1][:], in_=whole[:].rearrange("q (p u e) -> q u p e", u=2, e=2),
            func=ACT.Exp, bias=neg_max[:], scale=1.0, accum_out=row_sum[:],
        )

        q_cuts = ((0, QB), (0, QB // 2, QB))
        turned = [ps.tile([P, 2, QB], F32, name=f"turned{b}") for b in range(BLOCKS)]
        w_grouped = [sb.tile([P, QB * PACK], BF16, name=f"w_grouped{b}", align_bytes=64) for b in range(BLOCKS)]
        size_view = size_ps[:].rearrange("q (u e) p -> q u p e", u=2)
        sized = sb.tile([P, P, 2], F32, name="sized", tag="part_sum0", align_bytes=64)
        total = sb.tile([P, 2], F32, name="total")
        inv0 = sb.tile([P, 2], F32, name="inv0")
        inv1 = sb.tile([P, 1], F32, name="inv1")
        w0 = [sb.tile([P, P, 2], BF16, name=f"w0_{u}", align_bytes=64) for u in range(2)]
        w1 = [sb.tile([P, P, 2], BF16, name=f"w1_{u}", align_bytes=64) for u in range(2)]

        def weigh(h):
            nc.vector.tensor_tensor(
                out=sized[:, spans[h], :], in0=probs[0][:, 1, spans[h], :], in1=size_view[:, 1, spans[h], :],
                op=ALU.mult,
            )

        def turn(b, u, pairs):
            nc.tensor.transpose(turned[b][:, u, :], pairs.rearrange("q p e -> q (p e)").bitcast(F32), ident[:])

        def copy_out(b):
            for lo, hi in zip(q_cuts[b][:-1], q_cuts[b][1:]):
                nc.scalar.copy(
                    out=w_grouped[b][:].bitcast(F32).rearrange("p (q u) -> p q u", u=2)[:, lo:hi, :],
                    in_=turned[b][:, :, lo:hi].rearrange("p u q -> p q u"),
                )

        for h in range(2):
            nc.vector.tensor_scalar(
                out=total[:, h : h + 1], in0=ratio[h][:], scalar1=part_sum[1 - h][:], scalar2=part_sum[h][:],
                op0=ALU.mult, op1=ALU.add,
            )
        nc.vector.reciprocal(out=inv0[:], in_=total[:])
        for h in range(2):
            weigh(h)
        unit = sb.tile([P, 1], F32, name="unit")
        nc.vector.tensor_scalar(out=unit[:], in0=total[:, 0:1], scalar1=total[:, 0:1], scalar2=None, op0=ALU.is_equal)
        for h in range(2):
            nc.vector.scalar_tensor_tensor(
                out=w0[0][:, spans[h], :], in0=probs[0][:, 0, spans[h], :], scalar=inv0[:, h : h + 1],
                in1=size_view[:, 0, spans[h], :], op0=ALU.mult, op1=ALU.mult,
            )
            if h == 0:
                nc.vector.reciprocal(out=inv1[:], in_=row_sum[:])
            nc.scalar.activation(
                out=w0[1][:, spans[h], :], in_=sized[:, spans[h], :], func=ACT.Copy, scale=inv0[:, h : h + 1]
            )
        nc.scalar.activation(
            out=v_grouped[:, :, V_CUTS[2] // PACK :, :].rearrange("p t m j -> p m j t"),
            in_=v_raw[2].rearrange("p j (m t) -> p m j t", t=PACK), func=ACT.Copy, scale=unit[:],
        )
        for u in range(2):
            turn(0, u, w0[u][:])
        copy_out(0)
        for u in range(2):
            nc.vector.scalar_tensor_tensor(
                out=w1[u][:], in0=probs[1][:, u, :, :], scalar=inv1[:],
                in1=size_ps[:, 2 * u : 2 * u + 2, :].rearrange("q e p -> q p e"), op0=ALU.mult, op1=ALU.mult,
            )
            turn(1, u, w1[u][:])
        copy_out(1)

        v_codes = sb.tile([P, E], U32, name="v_codes", tag="row_sum", align_bytes=64)
        v_plane = sb.tile([P, E], U8, name="v_plane", align_bytes=64)
        t_cuts = ((0, 2), (2, 3, 4))
        w_codes = [sb.tile([P, QB], U32, name=f"w_codes{b}", align_bytes=64) for b in range(BLOCKS)]
        w_plane = [sb.tile([P, QB], U8, name=f"w_plane{b}", align_bytes=64) for b in range(BLOCKS)]
        for b in range(BLOCKS):
            for lo, hi in zip(t_cuts[b][:-1], t_cuts[b][1:]):
                nc.vector.quantize_mx(
                    out=v_codes[:, P * lo : P * hi].bitcast(FP8X4), scales=v_plane[:, P * lo : P * hi],
                    in_=v_grouped[:, lo:hi, :, :].rearrange("p t m j -> p (t m j)"),
                )
            for lo, hi in zip(q_cuts[b][:-1], q_cuts[b][1:]):
                nc.vector.quantize_mx(
                    out=w_codes[b][:, lo:hi].bitcast(FP8X4), scales=w_plane[b][:, lo:hi],
                    in_=w_grouped[b][:, PACK * lo : PACK * hi],
                )

        o_codes = sb.tile([P, Q], I32, name="o_codes", align_bytes=64)
        o_plane = sb.tile([P, Q], U8, name="o_plane", align_bytes=64)
        o_grouped = sb.tile([P, Q, PACK], BF16, name="o_grouped", align_bytes=64)
        out_rows = out_0.rearrange("(m t) q -> m t q", t=PACK)

        def product(acc, b, t):
            nc.tensor.matmul_mx(
                out=acc, lhsT=v_codes[:, P * t : P * (t + 1)].bitcast(FP8X4),
                lhsT_scale=v_plane[:, P * t : P * (t + 1)],
                rhs=w_codes[b][:].bitcast(FP8X4), rhs_scale=w_plane[b][:], start=True, stop=True,
            )

        y = sb.tile([P, PACK, Q], F32, name="y")
        for g in range(2):
            acc = ps.tile([P, 2, QB], F32, name=f"first{g}", tag=f"bank{g}")
            for s in range(2):
                product(acc[:, s, :], 0, 2 * g + s)
            nc.scalar.copy(out=y[:, 2 * g : 2 * g + 2, 0:QB], in_=acc[:])
        nc.sync.dma_start(out=out_rows[:, 2:4, 0:QB], in_=y[:, 2:4, 0:QB])
        nc.vector.tensor_copy(
            out=o_grouped[:, 0:QB, :].rearrange("p (c i) t -> p c t i", i=4),
            in_=y[:, :, 0:QB].rearrange("p t (c i) -> p c t i", i=4),
        )
        last = [ps.tile([P, 2, QB], F32, name=f"last{g}") for g in range(2)]
        for g in range(2):
            for s in range(2):
                product(last[g][:, s, :], 1, 2 * g + s)
        nc.scalar.copy(out=y[:, 0:2, QB:Q], in_=last[0][:])
        nc.sync.dma_start(out=out_rows[:, 0:2, :], in_=y[:, 0:2, :])
        nc.vector.tensor_copy(out=o_grouped[:, QB:Q, 0:2], in_=y[:, 0:2, QB:Q].rearrange("p s q -> p q s"))
        nc.scalar.copy(out=o_grouped[:, QB:Q, 2:4], in_=last[1][:].rearrange("p s q -> p q s"))
        nc.scalar.copy(out=y[:, 2:4, QB:Q], in_=last[1][:])
        nc.sync.dma_start(out=out_rows[:, 2:4, QB:Q], in_=y[:, 2:4, QB:Q])

        for b in range(BLOCKS):
            cols = slice(QB * b, QB * (b + 1))
            nc.vector.quantize_mx(
                out=o_codes[:, cols].bitcast(FP8X4), scales=o_plane[:, cols],
                in_=o_grouped[:, cols, :].rearrange("p q t -> p (q t)"),
            )
        nc.sync.dma_start(out=out_1[0].rearrange("p q t -> p (q t)").bitcast(I32), in_=o_codes[:])
        for j in range(4):
            queue = nc.scalar if j % 2 == 0 else nc.sync
            queue.dma_start(
                out=out_2[0, j:SCALE_ROWS:4, :].bitcast(I32), in_=o_plane[j:P:QUADRANT, :].bitcast(I32)
            )
